import numpy as np, ml_dtypes
CORES = [3,7,11,15,131,135,139,143]
N = 8
import mx_ref
BF = ml_dtypes.bfloat16
def entries(a):
    return np.ascontiguousarray(a.T).reshape(-1)
def table(e):
    return np.ascontiguousarray(np.reshape(e, (-1, 16)).T).astype(np.int32)
def pick(q, e):
    c = np.concatenate([q[0].reshape(128, -1, 4), np.zeros((128, 1, 4), np.uint8)], axis=1); s = np.concatenate([q[1], np.ones((16, 1), np.uint8)], axis=1)
    return (np.ascontiguousarray(c[:, e].reshape(128, -1)), np.ascontiguousarray(s[:, e]))
def join(*qs):
    return (np.concatenate([q[0] for q in qs], axis=1), np.concatenate([q[1] for q in qs], axis=1))
def put(q, e, v):
    c, s = q[0].reshape(128, -1, 4).copy(), q[1].copy(); c[:, e] = v[0].reshape(128, -1, 4); s[:, e] = v[1]
    return (c.reshape(128, -1), s)
def pk(c, s):
    return (np.ascontiguousarray(c), mx_ref.live(s))
def emit(q):
    return q[0], q[1]
def decode(q):
    o = []
    for b in range(4):
        e = np.zeros((128, 128, 4), np.float32); e[np.arange(128), np.arange(128), b] = 1
        o.append(mx_ref.matmul(mx_ref.quantize(e.reshape(128, 512).astype(BF)), q))
    return np.stack(o, axis=2).reshape(128, -1)
def cut(t, i, w=512):
    return t[:, w * i:w * i + w]
def f(rng, *shape):
    return mx_ref.flush((rng.standard_normal(shape, dtype=np.float32) * np.exp2(rng.integers(-2, 3, shape[:-1] + (1,)))).astype(BF))
def wide(rng, *shape, cols=0):
    v = rng.standard_normal(shape, dtype=np.float32) * np.exp2(rng.integers(-12, 13, shape)).astype(np.float32)
    if cols: v *= np.repeat(np.exp2(rng.integers(-cols, cols + 1, shape[:-2] + (1, shape[-1] // 4))) * (rng.random(shape[:-2] + (1, shape[-1] // 4)) > 0.0625), 4, axis=-1).astype(np.float32)
    return mx_ref.flush(v.astype(BF))
P, M, A, CAPP, R = 256, 64, 32, 16, 2
def big(v):
    v = v.astype(np.float32)
    v[np.abs(v) < np.float32(2.0 ** -16)] = 0
    return v.astype(BF)
def listed(e):
    return np.stack([table(v) for v in e])
def setup_inputs(rng):
    return {"ky": big(f(rng, N, 128, 4 * P)), "nx": listed(rng.integers(0, N * M, (N, P))), "x": big(f(rng, N, 128, 4 * A)), "st": listed(rng.integers(0, N * M, (N, A))), "w": f(rng, N, 128, 512)}
def setup_inputs_spread(rng):
    d = setup_inputs(rng)
    d["ky"] = big(wide(rng, N, 128, 4 * P, cols=6))
    d["x"] = big(wide(rng, N, 128, 4 * A, cols=4))
    return d
def setup_inputs_ties(rng):
    d = setup_inputs(rng)
    o = np.argsort(rng.random((N, M, 4)), axis=2) % 2
    v = d["ky"].reshape(N, 128, M, 4, 4)
    v = np.ascontiguousarray(np.stack([np.take_along_axis(v[r], np.broadcast_to(o[r][None, :, :, None], (128, M, 4, 4)), axis=2) for r in range(N)]))
    for r in range(N): v[r][:, rng.permutation(M)[:M // 8]] = 0
    d["ky"] = v.reshape(N, 128, 4 * P)
    to = np.argsort(rng.random((N, M, N)), axis=2)[:, :, :4]
    d["nx"] = listed((to * M + rng.integers(0, M, (N, M, 4))).reshape(N, P))
    return d
def setup_inputs_crowd(rng):
    d = setup_inputs(rng)
    o, st = rng.permutation(N), np.zeros((N, A), int)
    for i in range(N):
        s, to = o[i], o[(i + 1) % N]
        here = rng.permutation(A) < (CAPP if i % 2 == 0 else A - CAPP // 4)
        near = to * M + (rng.integers(0, M, A) if i % 2 == 0 else np.full(A, int(rng.integers(0, M))))
        far = (to + rng.integers(1, N, A)) % N * M + rng.integers(0, M, A)
        st[s] = np.where(here, near, far)
    d["st"] = listed(st)
    return d
def kept(rng, *shape):
    return 4 * rng.integers(0, M // 4, shape) + rng.integers(0, 3, shape)
def setup_inputs_stay(rng):
    d = setup_inputs(rng)
    o = rng.permutation(N)
    z, z2 = int(o[0]), int(o[1])
    v = np.arange(M)[None, :, None]
    to = np.arange(N)[:, None, None] * M + np.where(v % 2 == 0, v, kept(rng, N, M, 4))
    to[z, 3::4] = o[rng.integers(2, N, (M // 4, 4))] * M + rng.integers(0, M, (M // 4, 4))
    to[z2] = z * M + kept(rng, M, 4)
    d["nx"] = listed(to.reshape(N, P))
    leave = np.zeros((N, A), bool)
    leave[:, :CAPP] = np.argsort(rng.random((N, CAPP)), axis=1) < CAPP // 4
    st = z * M + np.where(leave, 4 * rng.integers(0, M // 4, (N, A)) + 3, kept(rng, N, A))
    n = CAPP + CAPP // 2
    st[:, n:] = z2 * M + rng.integers(0, M, (N, A - n))
    low = rng.permutation(N) < N // 2
    st[low] = np.roll(st[low], A - n, axis=1)
    d["st"] = listed(st)
    return d
def setup_inputs_turn(rng):
    d = setup_inputs(rng)
    sign = rng.choice([-1.0, 1.0], (128, 4))
    top = np.arange(128) < 64
    o = np.argsort(rng.random((N, M, 4)), axis=2).reshape(N, P)
    g = np.where(top[None, :, None], np.exp2(-2.0 * o)[:, None, :], np.exp2(2.0 * o + 2)[:, None, :])
    d["ky"] = big(((1 + rng.random((N, 128, P, 4))) * g[..., None] * sign[None, :, None, :]).reshape(N, 128, 4 * P))
    d["x"] = big(((1 + rng.random((N, 128, A, 4))) * top[None, :, None, None] * sign[None, :, None, :]).reshape(N, 128, 4 * A))
    return d
def check_inputs(d):
    b = []
    for k, lo, hi in (("ky", -16, 24), ("x", -16, 24), ("w", -30, 30)):
        v = np.abs(d[k].astype(np.float32))
        if not (np.isfinite(v).all() and ((v == 0) | (v >= 2.0 ** lo) & (v <= 2.0 ** hi)).all()): b.append("a value of " + k)
    for k in ("nx", "st"):
        if d[k].min() < 0 or d[k].max() >= N * M: b.append("an entry of " + k)
    return b
def served(node):
    ok = np.zeros(N * A, bool)
    for s in range(N):
        at = node[A * s:A * s + A] // M
        for d in range(N): ok[A * s + np.flatnonzero(at == d)[:CAPP]] = True
    return np.flatnonzero(ok)
def reference(ky, nx, x, st, w):
    pieces = [mx_ref.quantize(np.ascontiguousarray(cut(ky[d], i))) for d in range(N) for i in range(P // 128)]
    dk = decode(join(*pieces)).reshape(128, N * P, 4)
    leads = np.concatenate([entries(nx[d]) for d in range(N)])
    q = join(*[mx_ref.quantize(np.ascontiguousarray(x[s])) for s in range(N)])
    node = np.concatenate([entries(st[s]) for s in range(N)])
    e = np.arange(N * A)
    way = [node]
    for t in range(R):
        go = served(node)
        z = np.concatenate([mx_ref.matmul(p, q) for p in pieces])
        four = 4 * node[:, None] + np.arange(4)
        k = 4 * node + np.argmax(z[four, e[:, None]] + np.float32(0), axis=1)
        v = decode(q).reshape(128, N * A, 4) * np.float32(0.5) + dk[:, k] * np.float32(0.5)
        new = mx_ref.quantize(np.ascontiguousarray(v.reshape(128, -1).astype(BF)))
        q = put(q, go, pick(new, go))
        node = node.copy()
        node[go] = leads[k[go]]
        way.append(node)
    oc, osc = np.zeros((N, 128, 4 * A), np.uint8), np.zeros((N, 16, A), np.uint8)
    nd, y = np.zeros((N, R + 1, A), np.float32), np.zeros((N, 128, A), np.float32)
    for s in range(N):
        own = pick(q, np.arange(A * s, A * s + A))
        oc[s], osc[s] = emit(own)
        nd[s] = np.stack(way)[:, A * s:A * s + A]
        y[s] = mx_ref.matmul(mx_ref.quantize(np.ascontiguousarray(w[s])), own)
    return {"oc": oc, "osc": osc, "nd": nd, "y": y}

@@ -1,0 +1,479 @@
+from concourse.bass import DstId, RemoteDMATransfer
+from concourse.mybir import dt, AluOpType, AxisListType, ActivationFunctionType
+
+N, P, A, CAPP = 8, 256, 32, 16
+F8, U8, F32, BF, I32, U16 = "float8_e4m3fn_x4", "uint8", "float32", "bfloat16", "int32", "uint16"
+BIG = 32 * 16384
+SCRATCH = {}
+
+
+def _add(name, cols, dtype, where="sbuf"):
+    SCRATCH[name] = (where, [128, cols], dtype)
+
+
+for _n, _c in (("qx", 128), ("lx0", 256), ("send0", 32), ("land0", 128), ("new0", 128), ("wina", 160), ("send1", 128),
+               ("land1", 128), ("new1", 128), ("winb", 160), ("fin", 128), ("kq", 256), ("wq", 128), ("h", 512), ("ws", 128),
+               ("kp0", 128), ("kp1", 128), ("xq0", 128), ("xq1", 128)):
+    _add(_n + "c", _c, F8)
+    _add(_n + "s", _c, U8)
+for _n, _c, _d in (("xt", 512, BF), ("kt", 1024, BF), ("wt", 512, BF), ("hb", 516, BF), ("wb", 512, BF), ("xb", 512, BF),
+                   ("iop", 8, I32), ("ioj", 32, I32), ("jmp", 128, I32), ("xa0", 32, F32), ("xa1", 32, F32),
+                   ("el", 8, I32), ("elst", 8, U16), ("locrow", 128, F32), ("rowc", 128, F32), ("io16", 8, I32), ("slott", 8, F32),
+                   ("pd", 8, I32), ("mm", 128, F32), ("dm", 64, F32), ("blk", 8, F32), ("bki", 8, F32),
+                   ("r1", 1, F32), ("ibq", 4, F32), ("dcol", 4, F32), ("rst", 128, BF), ("rs2", 128, F32),
+                   ("fs", 8, F32), ("cc", 8, F32), ("str1", 32, I32), ("strb", 32, I32), ("nd0f", 32, F32),
+                   ("nxt", 32, I32), ("nxh", 32, I32), ("nxp", 32, F32), ("nxq", 32, F32), ("nx1", 256, F32), ("nxf", 256, F32),
+                   ("lsu", 8, U16), ("pl", 2, U16), ("sl", 8, U16), ("ol", 2, U16), ("ys", 32, F32),
+                   ("dr", 32, I32), ("xm", 32, I32), ("xx", 32, F32), ("shx", 8, I32), ("zl", 4, U16), ("ct", 8, U16),
+                   ("win", 160, F32), ("lu", 8, U16), ("so", 160, F32), ("dn", 32, F32), ("dl", 32, I32),
+                   ("vi", 8, I32), ("vm", 8, F32), ("v", 1, F32), ("v4", 8, F32), ("zlf", 4, F32), ("zs", 256, F32), ("zg", 64, F32), ("rm", 64, F32),
+                   ("eqb", 128, BF), ("cum", 128, BF), ("yy", 128, F32), ("mn", 128, F32),
+                   ("ia", 8, I32), ("fl", 8, F32), ("n2", 2, F32)):
+    _add(_n, _c, _d)
+for _t in ("0", "1"):
+    for _n, _c, _d in (("ti", 8, I32), ("xr", 32, I32), ("nodt", 128, F32), ("nt", 512, BF), ("rn", 32, F32),
+                       ("vv", 32, I32), ("nu", 2, U16), ("ndf", 32, F32)):
+        _add(_n + _t, _c, _d)
+_add("bank", 512 * 8, F32, "psum")
+ARRIVE = ["lx0", "xr0", "rn0", "ret0", "xr1", "land1", "rn1", "ret1"]
+DMAS = ["st", "x", "ky", "nx", "w", "nxr", "own0", "ownw", "nd0", "nd1", "nd2", "oc", "osc", "y"]
+SEMAPHORES = ["sg", "sv", "sa", "sp", "left"] + ["a_" + k for k in ARRIVE] + ["d_" + k for k in DMAS]
+
+
+def _bits(m):
+    return bin(m).count("1")
+
+
+def _plan(topo, cores, me):
+    others = [c for c in cores if c != me]
+    near = [c for c in others if c in topo.cores_of(me)]
+    far = [c for c in others if c not in near]
+    mate = [c for c in far if topo.mates(me, c) and topo.die(me) == topo.die(c)]
+    port = topo.engines(me, far[0])
+    rest = [e for e in topo.engines(me, near[0]) if e not in port]
+    load = {e: 0 for e in port}
+    turn = [0]
+
+    def masks(dsts):
+        o = {}
+        for c in dsts:
+            if c in near:
+                o[c] = sum(1 << e for e in rest)
+        f = [c for c in dsts if c in far]
+        if len(f) == 1:
+            o[f[0]] = sum(1 << e for e in port)
+            return o
+        k = turn[0] % len(f)
+        turn[0] += 2
+        f = f[k:] + f[:k]
+        free = sorted(port, key=lambda e: load[e])
+        doubles = len(free) - len(f)
+        for i, c in enumerate(f):
+            take = 1 if i < len(f) - doubles else 2
+            o[c] = sum(1 << e for e in free[:take])
+            for e in free[:take]:
+                load[e] += 2 // take
+            free = free[take:]
+        return o
+
+    picked = near + mate
+    wide = [c for c in far if c not in picked]
+    out = {"wide_c": masks(wide), "wide_s": masks(wide), "xr0": masks(others), "pick_c": masks(picked), "pick_s": masks(picked)}
+    for k in ("rn0", "ret0_c", "ret0_s", "xr1", "land1_c", "land1_s", "rn1", "ret1_c", "ret1_s"):
+        out[k] = masks(others)
+    return out, picked, wide
+
+
+ROUTE = {"wide_c": "lx0", "wide_s": "lx0", "pick_c": "lx0", "pick_s": "lx0", "xr0": "xr0", "rn0": "rn0", "ret0_c": "ret0", "ret0_s": "ret0",
+         "xr1": "xr1", "land1_c": "land1", "land1_s": "land1", "rn1": "rn1", "ret1_c": "ret1", "ret1_s": "ret1"}
+
+
+def rank_program(g, core, T, topo):
+    rank = T.rank_of(core)
+    if rank is None:
+        return
+    cores = list(T.cores)
+    odd = rank % 2
+    plans = {c: _plan(topo, cores, c) for c in cores}
+    calls, picked, wide = plans[core]
+    want = {k: 0 for k in ARRIVE}
+    for c in cores:
+        if c != core:
+            for k, a in ROUTE.items():
+                want[a] += _bits(plans[c][0][k].get(core, 0))
+    ALU, X, CP = AluOpType, AxisListType.X, ActivationFunctionType.Copy
+    queues = {"g": g, "v": g.vector, "a": g.scalar, "p": g.tensor, "s": g.sync}
+    sems = {"g": "sg", "v": "sv", "a": "sa", "p": "sp"}
+    count = {k: 0 for k in sems}
+    known = {k: {} for k in queues}
+    snap = {}
+    wrote, readers = {}, {}
+
+    def waits(q, reads, writes):
+        need = [wrote[k] for k in reads]
+        for k in writes:
+            if k in wrote:
+                need.append(wrote[k])
+            for e, rq in readers.get(k, []):
+                if rq != q or e[0].startswith("d_"):
+                    need.append(e)
+        best = {}
+        for s, val in need:
+            if known[q].get(s, 0) < val:
+                best[s] = max(best.get(s, 0), val)
+        for s in sorted(best, key=lambda s: -len(snap.get((s, best[s]), {}))):
+            val = best[s]
+            if known[q].get(s, 0) >= val:
+                continue
+            queues[q].wait_ge(T.sem[s], val)
+            known[q][s] = val
+            for s2, v2 in snap.get((s, val), {}).items():
+                known[q][s2] = max(known[q].get(s2, 0), v2)
+
+    def note(q, ev, reads, writes):
+        snap[ev] = dict(known[q])
+        for k in reads:
+            readers.setdefault(k, []).append((ev, q))
+        for k in writes:
+            wrote[k] = ev
+            readers[k] = []
+
+    def op(q, fn, reads, writes):
+        waits(q, reads, writes)
+        count[q] += 1
+        fn(queues[q]).then_inc(T.sem[sems[q]], 1)
+        note(q, (sems[q], count[q]), reads, writes)
+
+    dcount = {}
+
+    def dma(q, name, out, in_, reads, writes):
+        s = "d_" + name
+        waits(q, reads, writes)
+        queues[q].dma_start(out, in_).then_inc(T.sem[s], 16)
+        dcount[s] = dcount.get(s, 0) + 16
+        note(q, (s, dcount[s]), reads, writes)
+
+    left = [0]
+
+    def send(call, src, dst, reads):
+        waits("g", reads, [])
+        tr = []
+        for c, m in calls[call].items():
+            rid, pid = topo.addr(c, core)
+            d = cores.index(c)
+            tr.append(RemoteDMATransfer(dst_ids=[DstId(rid=rid, pnc=pid)], dma_engine_mask=m, remote_sem=T.sem["a_" + ROUTE[call]], src=src(d), dst=dst(d)))
+            left[0] += _bits(m)
+        g.remote_dma_fused(tr, local_sem=T.sem.left)
+
+    for k in ARRIVE:
+        wrote["in_" + k] = ("a_" + k, want[k])
+
+    def codes(name, a, b):
+        return T[name + "c"][:, a:b].bitcast(dt.uint8)
+
+    def words(name, a, b):
+        return T[name + "c"][:, a:b].bitcast(dt.uint32)
+
+    def ts(out, in0, s1, op0, reads, writes, s2=None, op1=None):
+        if op1 is None:
+            op("v", lambda e: e.tensor_scalar(out, in0, s1, None, op0), reads, writes)
+        else:
+            op("v", lambda e: e.tensor_scalar(out, in0, s1, s2, op0, op1), reads, writes)
+
+    def tt(out, a, b, o, reads, writes):
+        op("v", lambda e: e.tensor_tensor(out, a, b, o), reads, writes)
+
+    def cp(out, a, reads, writes):
+        op("v", lambda e: e.tensor_copy(out, a), reads, writes)
+
+    def red(out, a, reads, writes, o=ALU.add):
+        op("v", lambda e: e.tensor_reduce(out, a, X, o), reads, writes)
+
+    def scan(out, a, b, init, o0, o1, reads, writes):
+        op("v", lambda e: e.tensor_tensor_scan(out, a, b, init, o0, o1), reads, writes)
+
+    def turn(out, a, reads, writes):
+        op("v", lambda e: e.transpose(out, a), reads, writes)
+
+    def fill(ap, value, writes):
+        op("v", lambda e: e.memset(ap, value), [], writes)
+
+    def quant(name, a, b, tile, reads, writes):
+        op("v", lambda e: e.quantize_mx(T[name + "c"][:, a:b], T[name + "s"][:, a:b], tile), reads, writes)
+
+    def iota(out, pattern, base, step, writes, flag=False):
+        if flag:
+            op("g", lambda e: e.iota(out, pattern, base, step, allow_small_or_imprecise_dtypes=True), [], writes)
+        else:
+            op("g", lambda e: e.iota(out, pattern, base, step), [], writes)
+
+    def mx(bank, n, l, la, r, ra, reads, start=True, stop=True):
+        op("p", lambda e: e.matmul_mx(T.bank[:, 512 * bank:512 * bank + n], T[l + "c"][:, la:la + 128], T[l + "s"][:, la:la + 128],
+                                      T[r + "c"][:, ra:ra + n], T[r + "s"][:, ra:ra + n], start, stop), reads, ["bank%d" % bank])
+
+    def bank(k, n):
+        return T.bank[:, 512 * k:512 * k + n]
+
+    def act(out, in_, reads, writes):
+        op("a", lambda e: e.activation(out, in_, CP), reads, writes)
+
+    def zero(out, in_, reads, writes):
+        op("a", lambda e: e.activation(out, in_, CP, scale=0.0), reads, writes)
+
+    def pick(out, oa, win, wb, off, n, reads, key):
+        cp(words(out, oa, oa + n), words(win, 0, wb).indirect(off), reads, [key + "_c"])
+        act(T[out + "s"][:, oa:oa + n], T[win + "s"][:, 0:wb].indirect(off), reads, [key + "_s"])
+
+    def place(r):
+        return r ^ odd
+
+    def seen(r):
+        return rank ^ (r % 2)
+
+    me = place(rank)
+    mine = CAPP * me
+    dma("s", "st", T.str1[0:1, 0:A], T.st[:], [], ["str1"])
+    dma("a", "x", T.xt[:, 0:4 * A], T.x[:], [], ["xt"])
+    dma("s", "ky", T.kt[:], T.ky[:], [], ["kt"])
+    fill(T.nxt[0:32, :], 0, ["nxt"])
+    iota(T.jmp[:], [[1, 128]], 0, -1, ["jmp"])
+    iota(T.iop[:], [[0, 8]], 0, 1, ["iop"])
+    iota(T.ioj[:], [[1, A]], 0, 0, ["ioj"])
+    iota(T.xa0[:], [[16384 + 64, A]], 0, 0, ["xa0"], True)
+    dma("a", "nx", T.nxt[0:16, 0:16], T.nx[:], ["nxt"], ["nxt"])
+    fill(T.xt[:, 4 * A:512], 0.0, ["xtz"])
+    fill(T.hb[:], 0.0, ["hb"])
+    dcol = []
+    for q in range(4):
+        for half in range(2):
+            dcol.append("dcol%d%d" % (q, half))
+            fill(T.dcol[64 * half:64 * half + 64, q:q + 1], float(place(4 * half + q)), dcol[-1:])
+    ts(T.hb[:, 3:515:4], T.jmp[:], 0.0, ALU.is_equal, ["jmp"], ["hb"], 0.5, ALU.mult)
+    ts(T.ia[:], T.iop[:], 15, ALU.bitwise_and, ["iop"], ["ia"])
+    fill(T.rst[:], 1.0, ["rst"])
+    fill(T.rst[:, 0:128:32], 0.0, ["rst"])
+    fill(T.rs2[:], 0.0, ["rs2"])
+    fill(T.rs2[:, 0:128:32], float(4 * BIG), ["rs2"])
+    ts(T.r1[:], T.ia[:, 0:1], 1.0, ALU.add, ["ia"], ["r1"])
+    ts(T.jmp[:], T.jmp[:], 15, ALU.bitwise_and, ["jmp"], ["jmp"])
+    ts(T.mm[:], T.jmp[:], 0.0, ALU.is_equal, ["jmp"], ["mm"])
+    zero(T.xb[:], T.hb[:, 0:512], ["hb"], ["xbz"])
+    zero(T.wb[:], T.hb[:, 0:512], ["hb"], ["wb"])
+    quant("qx", 0, 128, T.xt[:], ["xt", "xtz"], ["qx"])
+    op("g", lambda e: e.partition_broadcast(T.strb[:], T.str1[0:1, 0:A], 128), ["str1"], ["strb"])
+    send("wide_c", lambda d: codes("qx", 0, A), lambda d: codes("lx0", A * seen(d), A * seen(d) + A), ["qx"])
+    send("wide_s", lambda d: T.qxs[:, 0:A], lambda d: T.lx0s[:, A * seen(d):A * seen(d) + A], ["qx"])
+    dma("s", "own0", codes("lx0", A * me, A * me + A), codes("qx", 0, A), ["qx"], ["lx0own"])
+    dma("s", "own0", T.lx0s[:, A * me:A * me + A], T.qxs[:, 0:A], ["qx"], ["lx0own2"])
+
+    def tab(k):
+        return ["tab%s%d%d" % (k, a, b) for a in range(2) for b in range(2)]
+
+    def lists(t):
+        n = str(t)
+        ti, x, k = T["ti" + n], T["xr" + n], tab("l" + n)
+        quarters = [slice(A * q, A * q + A) for q in range(4)]
+        for q in range(4):
+            ts(T.eqb[:, quarters[q]], T.dr[:], T.dcol[:, q:q + 1], ALU.is_equal, ["dr"] + dcol, ["eqb%d" % q])
+        scan(T.cum[:], T.rst[:], T.eqb[:], 0.0, ALU.mult, ALU.add, ["rst"] + ["eqb%d" % q for q in range(4)], ["cum"])
+        tt(T.xx[:], T.xm[:], T["xa" + n][:], ALU.add, ["xm", "xa" + n], ["xx"])
+        ts(T.cum[:], T.cum[:], T.r1[:, 0:1], ALU.is_lt, ["cum", "r1"], ["cum"], float(BIG), ALU.mult)
+        for q in range(4):
+            tt(T.yy[:, quarters[q]], T.cum[:, quarters[q]], T.xx[:], ALU.add, ["cum", "xx"], ["yy%d" % q])
+        scan(T.mn[:], T.rs2[:], T.yy[:], 0.0, ALU.max, ALU.min, ["rs2"] + ["yy%d" % q for q in range(4)], ["mn"])
+        for a in range(2):
+            for b in range(2):
+                cp(ti[64 * b:64 * b + 64, 4 * a:4 * a + 4], T.mn[64 * a:64 * a + 64, 31:128:32], ["mn"], ["tabl%s%d%d" % (n, a, b)])
+        send("xr" + n, lambda d: ti[:, place(d):place(d) + 1], lambda d: x[:, 4 * seen(d):4 * seen(d) + 1], k)
+        ts(T.shx[:], ti[:], 6, ALU.logical_shift_right, k, ["shx"], 255, ALU.bitwise_and)
+
+    def inverse(t):
+        n = str(t)
+        ts(T.ia[:], T["ti" + n][:], 14, ALU.logical_shift_right, tab("l" + n), ["ia"])
+        cp(T.so[:, 0:A], T.ioj[:], ["ioj"], ["so"])
+        ts(T.fl[:], T.ia[:], 32.0, ALU.is_ge, ["ia"], ["fl"])
+        tt(T.fl[:], T.fl[:], T.slott[:], ALU.mult, ["fl", "slott"], ["fl"])
+        tt(T.fl[:], T.fl[:], T.ia[:], ALU.add, ["fl", "ia"], ["fl"])
+        cp(T.lu[:], T.fl[:], ["fl"], ["lu"])
+        cp(T.so[:, 0:160].indirect(T.lu[:, 0:8]), T.rowc[:], ["rowc", "lu"], ["so"])
+        tt(T.dn[:], T.so[:, 0:A], T.mm[:, 0:A], ALU.mult, ["so", "mm"], ["dn"])
+        for h in range(2):
+            red(T.n2[:, h:h + 1], T.dn[:, 16 * h:16 * h + 16], ["dn"], ["n2%d" % h])
+        cp(T["nu" + n][:], T.n2[:], ["n20", "n21"], ["nu" + n])
+
+    def received(t):
+        n = str(t)
+        xv = T["xr" + n][:, 0:4 * N:4]
+        src = ["in_xr" + n, "xrown" + n]
+        if t == 0:
+            ts(T.ia[:], xv, 6, ALU.logical_shift_right, src, ["ia"], 255, ALU.bitwise_and)
+        ts(T.vi[:], xv, 63, ALU.bitwise_and, src, ["vi"])
+        if t == 0:
+            tt(T.fl[:], T.ia[:], T.fs[:], ALU.mult, ["ia", "fs"], ["fl"])
+        tt(T.vm[:], T.vi[:], T.blk[:], ALU.mult, ["vi", "blk"], ["vm"])
+        if t == 0:
+            tt(T.fl[:], T.fl[:], T.cc[:], ALU.add, ["fl"] + ccs, ["fl"])
+        red(T.v[:], T.vm[:], ["vm"], ["v"])
+        if t == 0:
+            cp(T.lsu[:], T.fl[:], ["fl"], ["lsu"])
+            pick("land0", 0, "lx0", 256, T.lsu[:, 0:8], 128, ["in_lx0", "lx0own", "lx0own2", "lsu"], "land0")
+        ts(T.zlf[:], T.ibq[:], T.v[:, 0:1], ALU.add, ["ibq", "v"], ["zlf"], 4.0, ALU.mult)
+        ts(T.v4[:], T.vi[:], 4.0, ALU.mult, ["vi"], ["v4"])
+        cp(T.zl[:], T.zlf[:], ["zlf"], ["zl"])
+
+    def goes(d):
+        return slice(CAPP * place(d), CAPP * place(d) + CAPP)
+
+    def serve(t):
+        n = str(t)
+        land, nt, kp, xq, win = "land" + n, T["nt" + n], "kp" + n, "xq" + n, ("wina", "winb")[t]
+        lk = ["land0_c", "land0_s"] if t == 0 else ["in_land1", "land1own_c", "land1own_s"]
+        mx(0, 128, land, 0, "kq", 0, lk + ["kq"])
+        mx(5, 128, land, 0, "kq", 128, lk + ["kq"])
+        for i in range(4):
+            mx(1 + i, 128, "h", 128 * i, land, 0, lk + ["h%d" % i], True, False)
+        act(T.zs[:, 0:128], bank(0, 128), ["bank0"], ["zs0"])
+        cp(T.zs[:, 128:256], bank(5, 128), ["bank5"], ["zs1"])
+        tt(T.zg[:], T.zs[:, 0:P].indirect(T.zl[:, 0:4]), T.dm[:], ALU.add, ["zs0", "zs1", "zl", "dm"], ["zg"])
+        scan(T.rm[:], T.zg[:], T.zg[:], -2e29, ALU.max, ALU.max, ["zg"], ["rm"])
+        for k in range(3):
+            ts(T.xb[:, k:4 * N:4], T.bki[:], T.rm[:, 16 * k + 15:16 * k + 16], ALU.add, ["bki", "rm", "xbz"], ["xb%d" % k], T.rm[:, 63:64], ALU.is_lt)
+        quant(xq, 0, 128, T.xb[:], ["xbz", "xb0", "xb1", "xb2"], [xq])
+        mx(6, 128, "ws", 0, xq, 0, ["ws", xq])
+        tt(T.fl[:], bank(6, N), T.v4[:], ALU.add, ["bank6", "v4"], ["fl"])
+        cp(T.ct[:], T.fl[:], ["fl"], ["ct"])
+        pick(kp, 0, "kq", P, T.ct[:, 0:8], 128, ["kq", "ct"], kp)
+        for i in range(4):
+            mx(1 + i, 128, "h", 128 * i, kp, 0, [kp + "_c", kp + "_s", "h%d" % i], False, True)
+        nodt, rn = T["nodt" + n], T["rn" + n]
+        yk = ["yy0", "yy1", "yy2", "yy3"]
+        tt(T.yy[:], T.nxf[:, 0:P].indirect(T.ct[:, 0:8]), T.locrow[:], ALU.add, ["nxf", "ct", "locrow"], yk)
+        turn(nodt[:], T.yy[:], yk, ["nodt" + n])
+        send("rn" + n, lambda d: nodt[:, 32 * (d // 2):32 * (d // 2) + 1], lambda d: rn[:, 4 * rank:4 * rank + 1], ["nodt" + n])
+        for i in range(4):
+            if i % 2:
+                act(nt[:, i:512:4], bank(1 + i, 128), ["bank%d" % (1 + i)], ["nt%s%d" % (n, i)])
+            else:
+                cp(nt[:, i:512:4], bank(1 + i, 128), ["bank%d" % (1 + i)], ["nt%s%d" % (n, i)])
+        quant("new" + n, 0, 128, nt[:], ["nt%s%d" % (n, i) for i in range(4)], ["new" + n])
+
+        def back(d):
+            return A + CAPP * seen(d)
+
+        send("ret%s_c" % n, lambda d: codes("new" + n, CAPP * place(d), CAPP * place(d) + CAPP), lambda d: codes(win, back(d), back(d) + CAPP), ["new" + n])
+        send("ret%s_s" % n, lambda d: T["new%ss" % n][:, goes(d)], lambda d: T[win + "s"][:, back(d):back(d) + CAPP], ["new" + n])
+        cp(rn[:, 4 * rank:4 * rank + 1], nodt[:, 32 * (rank // 2):32 * (rank // 2) + 1], ["nodt" + n], ["rnown" + n])
+        pick(win, back(rank), "new" + n, 128, T.ol[:, 0:1], CAPP, ["new" + n, "ol"], win + "own")
+
+    def home(t):
+        n = str(t)
+        vv = T["vv" + n]
+        cp(T.vm[:], T["rn" + n][:, 0:4 * N:4], ["in_rn" + n, "rnown" + n], ["vm"])
+        cp(T.mn[:], T.vm[:, 0:N].indirect(T.elst[:, 0:8]), ["vm", "elst"], ["mn"])
+        turn(T.win[:, A:160], T.mn[:], ["mn"], ["winr"])
+        cp(vv[:], T.win[:, 0:160].indirect(T["nu" + n][:, 0:2]), ["winq", "winr", "nu" + n], ["vv" + n])
+        ts(T.dr[:], vv[:], 14, ALU.logical_shift_right, ["vv" + n], ["dr"])
+
+    def number(t):
+        n = str(t)
+        ts(T.dl[:], T["vv" + n][:], 63, ALU.bitwise_and, ["vv" + n], ["dl"])
+        ts(T.dn[:], T.dr[:], 64.0, ALU.mult, ["dr"], ["dn"])
+        tt(T["ndf" + n][:], T.dn[:], T.dl[:], ALU.add, ["dl", "dn"], ["ndf" + n])
+
+    for h in range(2):
+        ts(T.dr[:, 16 * h:16 * h + 16], T.strb[:, h:A:2], 6, ALU.arith_shift_right, ["strb"], ["dr"])
+    for h in range(2):
+        ts(T.xm[:, 16 * h:16 * h + 16], T.strb[:, h:A:2], 63, ALU.bitwise_and, ["strb"], ["xm"])
+    lists(0)
+    for i, c in enumerate(picked):
+        k = place(cores.index(c))
+        cp(T.pl[:, i:i + 1], T.shx[:, k:k + 1], ["shx"], ["pl%d" % i])
+    pick("send0", 0, "qx", 128, T.pl[:, 0:2], 32, ["qx", "pl0", "pl1"], "send0")
+    slot = {cores.index(c): i * CAPP for i, c in enumerate(picked)}
+    send("pick_c", lambda d: codes("send0", slot[d], slot[d] + CAPP), lambda d: codes("lx0", A * seen(d), A * seen(d) + CAPP), ["send0_c"])
+    send("pick_s", lambda d: T.send0s[:, slot[d]:slot[d] + CAPP], lambda d: T.lx0s[:, A * seen(d):A * seen(d) + CAPP], ["send0_s"])
+    cp(T.xr0[:, 4 * me:4 * me + 1], T.ti0[:, me:me + 1], tab("l0"), ["xrown0"])
+    ts(T.nxh[0:32, :], T.nxt[0:32, :], 6, ALU.arith_shift_right, ["nxt"], ["nxh"])
+    ts(T.nxp[0:32, :], T.nxh[0:32, :], float(16384 - 64), ALU.mult, ["nxh"], ["nxp"])
+    tt(T.nxp[0:32, :], T.nxp[0:32, :], T.nxt[0:32, :], ALU.add, ["nxp", "nxt"], ["nxp"])
+    turn(T.nxq[0:32, :], T.nxp[0:32, :], ["nxp"], ["nxq"])
+    dma("s", "nxr", T.nx1[0:1, :], T.nxq[0:16, 0:16], ["nxq"], ["nx1"])
+    for k in range(3):
+        act(T.wb[:, k:512:4], T.mm[:], ["mm", "wb"], ["wb%d" % k])
+    ts(T.pd[:], T.iop[:], 4, ALU.arith_shift_right, ["iop"], ["pd"])
+    fill(T.fs[:], 1.0, ["fs"])
+    ts(T.cc[:], T.ioj[:, 0:N], 32.0, ALU.mult, ["ioj"], ["cc"])
+    tt(T.blk[:], T.pd[:], T.ioj[:, 0:N], ALU.is_equal, ["pd", "ioj"], ["blk"])
+    ccs = ["cc"]
+    for s, c in enumerate(cores):
+        if c != core and core in plans[c][1]:
+            k = place(s)
+            fill(T.fs[:, k:k + 1], 0.0, ["fs"])
+            ts(T.cc[:, k:k + 1], T.r1[:], float(32 * k - 1), ALU.add, ["r1", "cc"], ["cc%d" % k])
+            ccs.append("cc%d" % k)
+    ts(T.ibq[:], T.ioj[:, 0:4], 0.25, ALU.mult, ["ioj"], ["ibq"])
+    quant("kq", 0, P, T.kt[:], ["kt"], ["kq"])
+    for i in range(4):
+        quant("h", 128 * i, 128 * i + 128, T.hb[:, 3 - i:515 - i], ["hb"], ["h%d" % i])
+    ts(T.bki[:], T.blk[:], -1.0, ALU.add, ["blk"], ["bki"], -1e29, ALU.mult)
+    ts(T.dm[:], T.mm[:, 0:64], -1.0, ALU.add, ["mm"], ["dm"], 1e29, ALU.mult)
+    quant("ws", 0, 128, T.wb[:], ["wb", "wb0", "wb1", "wb2"], ["ws"])
+    op("g", lambda e: e.partition_broadcast(T.nxf[:], T.nx1[0:1, :], 128), ["nx1"], ["nxf"])
+    iota(T.locrow[:], [[0, 4], [64, 32]], 64 * (A + 32 * (rank // 2)), 0, ["locrow"], True)
+    iota(T.el[:], [[2, 4], [0, 2]], 0, 0, ["el"])
+    iota(T.rowc[:], [[1, 128]], A, 0, ["rowc"], True)
+    iota(T.io16[:], [[16, 8]], -1, 0, ["io16"])
+    iota(T.xa1[:], [[16384, A]], 0, 0, ["xa1"], True)
+    received(0)
+    ts(T.ol[:, 0:1], T.r1[:], float(mine - 1), ALU.add, ["r1"], ["ol"])
+    serve(0)
+    dma("s", "w", T.wt[:], T.w[:], [], ["wt"])
+    dma("s", "ownw", codes("wina", 0, A), codes("qx", 0, A), ["qx"], ["winaq"])
+    dma("s", "ownw", T.winas[:, 0:A], T.qxs[:, 0:A], ["qx"], ["winaq2"])
+    ts(T.win[:, 0:A], T.dr[:], 16384.0, ALU.mult, ["dr"], ["winq"])
+    ts(T.slott[:], T.io16[:], T.r1[:, 0:1], ALU.add, ["io16", "r1"], ["slott"])
+    ts(T.ia[:], T.pd[:], 1, ALU.bitwise_and, ["pd"], ["ia"])
+    tt(T.win[:, 0:A], T.win[:, 0:A], T.xx[:], ALU.add, ["winq", "xx"], ["winq"])
+    ts(T.fl[:], T.ia[:], -1.0 if odd else 1.0, ALU.mult, ["ia"], ["fl"], float(odd), ALU.add)
+    tt(T.win[:, 0:A], T.win[:, 0:A], T.xa1[:], ALU.subtract, ["winq", "xa1"], ["winq"])
+    tt(T.fl[:], T.fl[:], T.el[:], ALU.add, ["fl", "el"], ["fl"])
+    cp(T.elst[:], T.fl[:], ["fl"], ["elst"])
+    inverse(0)
+    home(0)
+    ts(T.xm[:], T.vv0[:], 16383, ALU.bitwise_and, ["vv0"], ["xm"])
+    lists(1)
+    cp(T.sl[:], T.shx[:], ["shx"], ["sl"])
+    wina = ["winaq", "winaq2", "winaown_c", "winaown_s", "in_ret0"]
+    pick("send1", 0, "wina", 160, T.sl[:, 0:8], 128, wina + ["sl"], "send1")
+    send("land1_c", lambda d: codes("send1", CAPP * place(d), CAPP * place(d) + CAPP),
+         lambda d: codes("land1", CAPP * seen(d), CAPP * seen(d) + CAPP), ["send1_c"])
+    send("land1_s", lambda d: T.send1s[:, goes(d)], lambda d: T.land1s[:, CAPP * seen(d):CAPP * seen(d) + CAPP], ["send1_s"])
+    cp(T.xr1[:, 4 * me:4 * me + 1], T.ti1[:, me:me + 1], tab("l1"), ["xrown1"])
+    pick("land1", mine, "send1", 128, T.ol[:, 0:1], CAPP, ["send1_c", "send1_s", "ol"], "land1own")
+    for h in range(2):
+        cp(T.nd0f[:, 16 * h:16 * h + 16], T.strb[:, h:A:2], ["strb"], ["nd0f"])
+    number(0)
+    received(1)
+    serve(1)
+    dma("s", "nd0", T.nd[0:1, :], T.nd0f[0:1, :], ["nd0f"], [])
+    dma("s", "nd1", T.nd[1:2, :], T.ndf0[0:1, :], ["ndf0"], [])
+    cp(T.win[:, 0:A], T.vv0[:], ["vv0"], ["winq"])
+    inverse(1)
+    pick("winb", 0, "wina", 160, T.nu0[:, 0:2], A, wina + ["nu0"], "winbq")
+    quant("wq", 0, 128, T.wt[:], ["wt"], ["wq"])
+    quant("fin", 0, 128, T.xt[:], ["xt", "xtz"], ["fin_c", "fin_s"])
+    home(1)
+    number(1)
+    dma("s", "nd2", T.nd[2:3, :], T.ndf1[0:1, :], ["ndf1"], [])
+    pick("fin", 0, "winb", 160, T.nu1[:, 0:2], A, ["winbq_c", "winbq_s", "winbown_c", "winbown_s", "in_ret1", "nu1"], "fin")
+    mx(7, 128, "wq", 0, "fin", 0, ["wq", "fin_c", "fin_s"])
+    act(T.ys[:], bank(7, A), ["bank7"], ["ys"])
+    dma("a", "y", T.y[:], T.ys[:], ["ys"], [])
+    dma("s", "oc", T.oc[:], codes("fin", 0, A), ["fin_c"], [])
+    for k in range(4):
+        dma("s" if k % 2 else "a", "osc", T.osc[4 * k:4 * k + 4, :], T.fins[32 * k:32 * k + 4, 0:A], ["fin_s"], [])
+    g.wait_ge(T.sem.left, left[0])
+    for q, s in sems.items():
+        g.wait_ge(T.sem[s], count[q])
+    for s, v in dcount.items():
+        g.wait_ge(T.sem[s], v)

@@ -3,7 +3,9 @@ from concourse.mybir import dt, AluOpType, AxisListType, ActivationFunctionType
 
 N, P, A, CAPP = 8, 256, 32, 16
 F8, U8, F32, BF, I32, U16 = "float8_e4m3fn_x4", "uint8", "float32", "bfloat16", "int32", "uint16"
-BIG = 32 * 16384
+EMPTY = 256 * 16384
+S = A + 1
+OWN = N * A
 SCRATCH = {}
 
 
@@ -11,32 +13,34 @@ def _add(name, cols, dtype, where="sbuf"):
     SCRATCH[name] = (where, [128, cols], dtype)
 
 
-for _n, _c in (("qx", 128), ("lx0", 256), ("send0", 32), ("land0", 128), ("new0", 128), ("wina", 160), ("send1", 128),
+for _n, _c in (("qx", 128), ("lx0", OWN + 128), ("send0", 32), ("land0", 128), ("new0", 128), ("wina", 160), ("send1", 128),
                ("land1", 128), ("new1", 128), ("winb", 160), ("fin", 128), ("kq", 256), ("wq", 128), ("h", 512), ("ws", 128),
                ("kp0", 128), ("kp1", 128), ("xq0", 128), ("xq1", 128)):
     _add(_n + "c", _c, F8)
     _add(_n + "s", _c, U8)
+_add("hand0", A, U8)
+_add("hand1", 128, U8)
 for _n, _c, _d in (("xt", 512, BF), ("kt", 1024, BF), ("wt", 512, BF), ("hb", 516, BF), ("wb", 512, BF), ("xb", 512, BF),
                    ("iop", 8, I32), ("ioj", 32, I32), ("jmp", 128, I32), ("xa0", 32, F32), ("xa1", 32, F32),
                    ("el", 8, I32), ("elst", 8, U16), ("locrow", 128, F32), ("rowc", 128, F32), ("io16", 8, I32), ("slott", 8, F32),
                    ("pd", 8, I32), ("mm", 128, F32), ("dm", 64, F32), ("blk", 8, F32), ("bki", 8, F32),
-                   ("r1", 1, F32), ("ibq", 4, F32), ("dcol", 4, F32), ("rst", 128, BF), ("rs2", 128, F32),
-                   ("fs", 8, F32), ("cc", 8, F32), ("str1", 32, I32), ("strb", 32, I32), ("nd0f", 32, F32),
+                   ("r1", 1, F32), ("ibq", 4, F32), ("dcol", 4, F32), ("rst", 4 * S, BF),
+                   ("cc", 8, F32), ("str1", 32, I32), ("strb", 32, I32), ("nd0f", 32, F32),
                    ("nxt", 32, I32), ("nxh", 32, I32), ("nxp", 32, F32), ("nxq", 32, F32), ("nx1", 256, F32), ("nxf", 256, F32),
                    ("lsu", 8, U16), ("pl", 2, U16), ("sl", 8, U16), ("ol", 2, U16), ("ys", 32, F32),
-                   ("dr", 32, I32), ("xm", 32, I32), ("xx", 32, F32), ("shx", 8, I32), ("zl", 4, U16), ("ct", 8, U16),
+                   ("ib", 8, I32), ("f3", 8, F32),
+                   ("dr", 32, I32), ("xm", 32, I32), ("xx", S + 1, F32), ("shx", 8, I32), ("zl", 4, U16), ("ct", 8, U16),
                    ("win", 160, F32), ("lu", 8, U16), ("so", 160, F32), ("dn", 32, F32), ("dl", 32, I32),
-                   ("vi", 8, I32), ("vm", 8, F32), ("v", 1, F32), ("v4", 8, F32), ("zlf", 4, F32), ("zs", 256, F32), ("zg", 64, F32), ("rm", 64, F32),
-                   ("eqb", 128, BF), ("cum", 128, BF), ("yy", 128, F32), ("mn", 128, F32),
-                   ("ia", 8, I32), ("fl", 8, F32), ("n2", 2, F32)):
+                   ("vi", 8, I32), ("vm", 8, F32), ("v", 1, F32), ("v4", 8, F32), ("zs", 256, F32), ("zg", 64, F32), ("rm", 64, F32),
+                   ("eqb", 4 * S, BF), ("cum", 4 * S + 2, BF), ("ltb", 4 * S, BF), ("yy", 128, F32), ("mn", 4 * S, F32),
+                   ("ia", 8, I32), ("fl", 8, F32), ("f2", 8, F32), ("n2", 2, F32), ("nodt", 256, F32), ("ndf", 64, F32)):
     _add(_n, _c, _d)
 for _t in ("0", "1"):
-    for _n, _c, _d in (("ti", 8, I32), ("xr", 32, I32), ("nodt", 128, F32), ("nt", 512, BF), ("rn", 32, F32),
-                       ("vv", 32, I32), ("nu", 2, U16), ("ndf", 32, F32)):
+    for _n, _c, _d in (("ti", 8, I32), ("xr", 32, I32), ("nt", 512, BF), ("rn", 32, F32), ("vv", 32, I32), ("nu", 2, U16)):
         _add(_n + _t, _c, _d)
 _add("bank", 512 * 8, F32, "psum")
-ARRIVE = ["lx0", "xr0", "rn0", "ret0", "xr1", "land1", "rn1", "ret1"]
-DMAS = ["st", "x", "ky", "nx", "w", "nxr", "own0", "ownw", "nd0", "nd1", "nd2", "oc", "osc", "y"]
+ARRIVE = ["lx0", "xr0", "rn0", "ret0", "xr1", "land1", "rn1", "ret1", "hand0", "hand1"]
+DMAS = ["st", "x", "ky", "nx", "w", "nxr", "ownw", "nd0", "nd1", "nd2", "oc", "osc", "y"]
 SEMAPHORES = ["sg", "sv", "sa", "sp", "left"] + ["a_" + k for k in ARRIVE] + ["d_" + k for k in DMAS]
 
 
@@ -44,24 +48,33 @@ def _bits(m):
     return bin(m).count("1")
 
 
+def _helper(topo, cores, me):
+    return [c for c in topo.cores_of(me) if c not in cores and topo.die(c) == topo.die(me) and all(topo.may_write(c, d) for d in cores)][0]
+
+
 def _plan(topo, cores, me):
     others = [c for c in cores if c != me]
     near = [c for c in others if c in topo.cores_of(me)]
     far = [c for c in others if c not in near]
-    mate = [c for c in far if topo.mates(me, c) and topo.die(me) == topo.die(c)]
+    picked = [c for c in far if topo.mates(me, c)]
     port = topo.engines(me, far[0])
-    rest = [e for e in topo.engines(me, near[0]) if e not in port]
+    inner = [e for e in topo.engines(me, near[0]) if e not in port]
     load = {e: 0 for e in port}
     turn = [0]
 
-    def masks(dsts):
+    def masks(dsts, fresh=False):
         o = {}
+        if fresh:
+            for e in port:
+                load[e] = 0
         for c in dsts:
             if c in near:
-                o[c] = sum(1 << e for e in rest)
+                o[c] = sum(1 << e for e in inner[::2])
         f = [c for c in dsts if c in far]
-        if len(f) == 1:
-            o[f[0]] = sum(1 << e for e in port)
+        if len(port) % len(f) == 0:
+            share = len(port) // len(f)
+            for i, c in enumerate(f):
+                o[c] = sum(1 << e for e in port[share * i:share * i + share])
             return o
         k = turn[0] % len(f)
         turn[0] += 2
@@ -76,23 +89,48 @@ def _plan(topo, cores, me):
             free = free[take:]
         return o
 
-    picked = near + mate
-    wide = [c for c in far if c not in picked]
-    out = {"wide_c": masks(wide), "wide_s": masks(wide), "xr0": masks(others), "pick_c": masks(picked), "pick_s": masks(picked)}
-    for k in ("rn0", "ret0_c", "ret0_s", "xr1", "land1_c", "land1_s", "rn1", "ret1_c", "ret1_s"):
-        out[k] = masks(others)
+    wide = [c for c in others if c not in picked]
+    helper = _helper(topo, cores, me)
+    out = {"wide_c": masks(wide), "wide_s": masks(wide), "xr0": masks(others), "pick_c": masks(picked), "pick_s": masks(picked),
+           "ret0_s": masks(others, True), "hand0": {helper: sum(1 << e for e in inner[1::2])}, "hand1": {helper: sum(1 << e for e in inner)}}
+    for k in ("rn0", "ret0_c", "xr1", "land1_c", "land1_s", "rn1", "ret1_c", "ret1_s"):
+        out[k] = masks(others, k in ("rn0", "rn1"))
     return out, picked, wide
 
 
 ROUTE = {"wide_c": "lx0", "wide_s": "lx0", "pick_c": "lx0", "pick_s": "lx0", "xr0": "xr0", "rn0": "rn0", "ret0_c": "ret0", "ret0_s": "ret0",
-         "xr1": "xr1", "land1_c": "land1", "land1_s": "land1", "rn1": "rn1", "ret1_c": "ret1", "ret1_s": "ret1"}
+         "xr1": "xr1", "land1_c": "land1", "land1_s": "land1", "rn1": "rn1", "ret1_c": "ret1", "ret1_s": "ret1",
+         "hand0": "hand0", "hand1": "hand1"}
+
+
+def _hand_on(g, core, T, topo, cores, rank):
+    calls = _plan(topo, cores, cores[rank])[0]
+    odd, left = rank % 2, 0
+    for hand, call in (("hand0", "wide_s"), ("hand1", "ret0_s")):
+        g.wait_ge(T.sem["a_" + hand], _bits(calls[hand][core]))
+        tr = []
+        for c, m in calls[call].items():
+            rid, pid = topo.addr(c, core)
+            d = cores.index(c)
+            seen = rank ^ (d % 2)
+            if hand == "hand0":
+                src, dst = T.hand0[:, 0:A], T.lx0s[:, A * seen:A * seen + A]
+            else:
+                src, dst = T.hand1[:, CAPP * (d ^ odd):CAPP * (d ^ odd) + CAPP], T.winas[:, A + CAPP * seen:A + CAPP * seen + CAPP]
+            tr.append(RemoteDMATransfer(dst_ids=[DstId(rid=rid, pnc=pid)], dma_engine_mask=m, remote_sem=T.sem["a_" + ROUTE[call]], src=src, dst=dst))
+            left += _bits(m)
+        g.remote_dma_fused(tr, local_sem=T.sem.left)
+    g.wait_ge(T.sem.left, left)
 
 
 def rank_program(g, core, T, topo):
     rank = T.rank_of(core)
-    if rank is None:
-        return
     cores = list(T.cores)
+    if rank is None:
+        for r, c in enumerate(cores):
+            if core in topo.cores_of(c) and _helper(topo, cores, c) == core:
+                _hand_on(g, core, T, topo, cores, r)
+        return
     odd = rank % 2
     plans = {c: _plan(topo, cores, c) for c in cores}
     calls, picked, wide = plans[core]
@@ -160,7 +198,7 @@ def rank_program(g, core, T, topo):
         tr = []
         for c, m in calls[call].items():
             rid, pid = topo.addr(c, core)
-            d = cores.index(c)
+            d = cores.index(c) if c in cores else None
             tr.append(RemoteDMATransfer(dst_ids=[DstId(rid=rid, pnc=pid)], dma_engine_mask=m, remote_sem=T.sem["a_" + ROUTE[call]], src=src(d), dst=dst(d)))
             left[0] += _bits(m)
         g.remote_dma_fused(tr, local_sem=T.sem.left)
@@ -238,65 +276,66 @@ def rank_program(g, core, T, topo):
     fill(T.nxt[0:32, :], 0, ["nxt"])
     iota(T.jmp[:], [[1, 128]], 0, -1, ["jmp"])
     iota(T.iop[:], [[0, 8]], 0, 1, ["iop"])
-    iota(T.ioj[:], [[1, A]], 0, 0, ["ioj"])
+    iota(T.dcol[:], [[2, 2], [place(1) - place(0), 2]], place(0), 0, ["dcol"], True)
     iota(T.xa0[:], [[16384 + 64, A]], 0, 0, ["xa0"], True)
+    iota(T.ioj[:], [[1, A]], 0, 0, ["ioj"])
     dma("a", "nx", T.nxt[0:16, 0:16], T.nx[:], ["nxt"], ["nxt"])
     fill(T.xt[:, 4 * A:512], 0.0, ["xtz"])
     fill(T.hb[:], 0.0, ["hb"])
-    dcol = []
-    for q in range(4):
-        for half in range(2):
-            dcol.append("dcol%d%d" % (q, half))
-            fill(T.dcol[64 * half:64 * half + 64, q:q + 1], float(place(4 * half + q)), dcol[-1:])
+    fill(T.rst[:], 1.0, ["rst"])
+    fill(T.eqb[:, A:4 * S:S], 0.0, ["eqz"])
+    fill(T.cum[:, 0:1], 0.0, ["cumz"])
+    fill(T.xx[:, A:S], float(EMPTY), ["xxz"])
+    fill(T.rst[:, A:4 * S:S], 0.0, ["rst"])
     ts(T.hb[:, 3:515:4], T.jmp[:], 0.0, ALU.is_equal, ["jmp"], ["hb"], 0.5, ALU.mult)
     ts(T.ia[:], T.iop[:], 15, ALU.bitwise_and, ["iop"], ["ia"])
-    fill(T.rst[:], 1.0, ["rst"])
-    fill(T.rst[:, 0:128:32], 0.0, ["rst"])
-    fill(T.rs2[:], 0.0, ["rs2"])
-    fill(T.rs2[:, 0:128:32], float(4 * BIG), ["rs2"])
-    ts(T.r1[:], T.ia[:, 0:1], 1.0, ALU.add, ["ia"], ["r1"])
     ts(T.jmp[:], T.jmp[:], 15, ALU.bitwise_and, ["jmp"], ["jmp"])
+    ts(T.r1[:], T.ia[:, 0:1], 1.0, ALU.add, ["ia"], ["r1"])
+    ts(T.dcol[64:128, :], T.dcol[64:128, :], 4.0, ALU.add, ["dcol"], ["dcol"])
     ts(T.mm[:], T.jmp[:], 0.0, ALU.is_equal, ["jmp"], ["mm"])
+    zero(T.rn0[:], T.hb[:, 0:32], ["hb"], ["rnz0"])
+    zero(T.rn1[:], T.hb[:, 0:32], ["hb"], ["rnz1"])
     zero(T.xb[:], T.hb[:, 0:512], ["hb"], ["xbz"])
     zero(T.wb[:], T.hb[:, 0:512], ["hb"], ["wb"])
     quant("qx", 0, 128, T.xt[:], ["xt", "xtz"], ["qx"])
     op("g", lambda e: e.partition_broadcast(T.strb[:], T.str1[0:1, 0:A], 128), ["str1"], ["strb"])
     send("wide_c", lambda d: codes("qx", 0, A), lambda d: codes("lx0", A * seen(d), A * seen(d) + A), ["qx"])
-    send("wide_s", lambda d: T.qxs[:, 0:A], lambda d: T.lx0s[:, A * seen(d):A * seen(d) + A], ["qx"])
-    dma("s", "own0", codes("lx0", A * me, A * me + A), codes("qx", 0, A), ["qx"], ["lx0own"])
-    dma("s", "own0", T.lx0s[:, A * me:A * me + A], T.qxs[:, 0:A], ["qx"], ["lx0own2"])
+    send("hand0", lambda d: T.qxs[:, 0:A], lambda d: T.hand0[:, 0:A], ["qx"])
 
     def tab(k):
         return ["tab%s%d%d" % (k, a, b) for a in range(2) for b in range(2)]
 
-    def lists(t):
+    mns = ["mn%d" % q for q in range(4)]
+
+    def lists(t, masked):
         n = str(t)
         ti, x, k = T["ti" + n], T["xr" + n], tab("l" + n)
-        quarters = [slice(A * q, A * q + A) for q in range(4)]
         for q in range(4):
-            ts(T.eqb[:, quarters[q]], T.dr[:], T.dcol[:, q:q + 1], ALU.is_equal, ["dr"] + dcol, ["eqb%d" % q])
-        scan(T.cum[:], T.rst[:], T.eqb[:], 0.0, ALU.mult, ALU.add, ["rst"] + ["eqb%d" % q for q in range(4)], ["cum"])
-        tt(T.xx[:], T.xm[:], T["xa" + n][:], ALU.add, ["xm", "xa" + n], ["xx"])
-        ts(T.cum[:], T.cum[:], T.r1[:, 0:1], ALU.is_lt, ["cum", "r1"], ["cum"], float(BIG), ALU.mult)
+            ts(T.eqb[:, S * q:S * q + A], T.dr[:], T.dcol[:, q:q + 1], ALU.is_equal, ["dr", "dcol"], ["eqb%d" % q])
+        masked()
+        scan(T.cum[:, 1:4 * S + 1], T.rst[:], T.eqb[:], 0.0, ALU.mult, ALU.add, ["rst", "eqz"] + ["eqb%d" % q for q in range(4)], ["cum"])
+        tt(T.xx[:, 0:A], T.xm[:], T["xa" + n][:], ALU.add, ["xm", "xa" + n], ["xx"])
+        ts(T.ltb[:], T.cum[:, 0:4 * S], T.r1[:, 0:1], ALU.is_lt, ["cum", "cumz", "r1"], ["ltb"], float(2 * EMPTY), ALU.mult)
         for q in range(4):
-            tt(T.yy[:, quarters[q]], T.cum[:, quarters[q]], T.xx[:], ALU.add, ["cum", "xx"], ["yy%d" % q])
-        scan(T.mn[:], T.rs2[:], T.yy[:], 0.0, ALU.max, ALU.min, ["rs2"] + ["yy%d" % q for q in range(4)], ["mn"])
+            scan(T.mn[:, S * q:S * q + S], T.ltb[:, S * q:S * q + S], T.xx[:, 0:S], 0.0, ALU.max, ALU.min, ["ltb", "xx", "xxz"], [mns[q]])
         for a in range(2):
             for b in range(2):
-                cp(ti[64 * b:64 * b + 64, 4 * a:4 * a + 4], T.mn[64 * a:64 * a + 64, 31:128:32], ["mn"], ["tabl%s%d%d" % (n, a, b)])
-        send("xr" + n, lambda d: ti[:, place(d):place(d) + 1], lambda d: x[:, 4 * seen(d):4 * seen(d) + 1], k)
-        ts(T.shx[:], ti[:], 6, ALU.logical_shift_right, k, ["shx"], 255, ALU.bitwise_and)
+                cp(ti[64 * b:64 * b + 64, 4 * a:4 * a + 4], T.mn[64 * a:64 * a + 64, A:4 * S:S], mns, ["tabl%s%d%d" % (n, a, b)])
+        send("xr" + n, lambda d: ti[:, place(d):place(d) + 1], lambda d: x[:, 4 * seen(d):4 * seen(d) + 1], k + ["rnz0", "rnz1"])
 
-    def inverse(t):
+    def inverse_a(t):
         n = str(t)
         ts(T.ia[:], T["ti" + n][:], 14, ALU.logical_shift_right, tab("l" + n), ["ia"])
         cp(T.so[:, 0:A], T.ioj[:], ["ioj"], ["so"])
-        ts(T.fl[:], T.ia[:], 32.0, ALU.is_ge, ["ia"], ["fl"])
-        tt(T.fl[:], T.fl[:], T.slott[:], ALU.mult, ["fl", "slott"], ["fl"])
-        tt(T.fl[:], T.fl[:], T.ia[:], ALU.add, ["fl", "ia"], ["fl"])
-        cp(T.lu[:], T.fl[:], ["fl"], ["lu"])
+        tt(T.f2[:], T.ia[:], T.slott[:], ALU.min, ["ia", "slott"], ["f2"])
+        cp(T.lu[:], T.f2[:], ["f2"], ["lu"])
+
+    def inverse_b(t, beside):
+        n = str(t)
         cp(T.so[:, 0:160].indirect(T.lu[:, 0:8]), T.rowc[:], ["rowc", "lu"], ["so"])
+        beside[0]()
         tt(T.dn[:], T.so[:, 0:A], T.mm[:, 0:A], ALU.mult, ["so", "mm"], ["dn"])
+        beside[1]()
         for h in range(2):
             red(T.n2[:, h:h + 1], T.dn[:, 16 * h:16 * h + 16], ["dn"], ["n2%d" % h])
         cp(T["nu" + n][:], T.n2[:], ["n20", "n21"], ["nu" + n])
@@ -305,26 +344,24 @@ def rank_program(g, core, T, topo):
         n = str(t)
         xv = T["xr" + n][:, 0:4 * N:4]
         src = ["in_xr" + n, "xrown" + n]
-        if t == 0:
-            ts(T.ia[:], xv, 6, ALU.logical_shift_right, src, ["ia"], 255, ALU.bitwise_and)
         ts(T.vi[:], xv, 63, ALU.bitwise_and, src, ["vi"])
         if t == 0:
-            tt(T.fl[:], T.ia[:], T.fs[:], ALU.mult, ["ia", "fs"], ["fl"])
+            tt(T.fl[:], xv, T.cc[:], ALU.add, src + ["cc"], ["fl"])
         tt(T.vm[:], T.vi[:], T.blk[:], ALU.mult, ["vi", "blk"], ["vm"])
         if t == 0:
-            tt(T.fl[:], T.fl[:], T.cc[:], ALU.add, ["fl"] + ccs, ["fl"])
+            for a, b in runs:
+                lsk.append("lsu%d" % a)
+                ts(T.lsu[:, a:b], T.fl[:, a:b], 1.0 / 16384, ALU.mult, ["fl"], lsk[-1:], float(OWN + A - 1), ALU.min)
         red(T.v[:], T.vm[:], ["vm"], ["v"])
-        if t == 0:
-            cp(T.lsu[:], T.fl[:], ["fl"], ["lsu"])
-            pick("land0", 0, "lx0", 256, T.lsu[:, 0:8], 128, ["in_lx0", "lx0own", "lx0own2", "lsu"], "land0")
-        ts(T.zlf[:], T.ibq[:], T.v[:, 0:1], ALU.add, ["ibq", "v"], ["zlf"], 4.0, ALU.mult)
         ts(T.v4[:], T.vi[:], 4.0, ALU.mult, ["vi"], ["v4"])
-        cp(T.zl[:], T.zlf[:], ["zlf"], ["zl"])
+        ts(T.zl[:], T.ibq[:], T.v[:, 0:1], ALU.add, ["ibq", "v"], ["zl"], 4.0, ALU.mult)
+        if t == 0:
+            pick("land0", 0, "lx0", OWN + A, T.lsu[:, 0:8], 128, ["in_lx0", "lx0own"] + lsk, "land0")
 
     def goes(d):
         return slice(CAPP * place(d), CAPP * place(d) + CAPP)
 
-    def serve(t):
+    def serve(t, gaps):
         n = str(t)
         land, nt, kp, xq, win = "land" + n, T["nt" + n], "kp" + n, "xq" + n, ("wina", "winb")[t]
         lk = ["land0_c", "land0_s"] if t == 0 else ["in_land1", "land1own_c", "land1own_s"]
@@ -332,6 +369,7 @@ def rank_program(g, core, T, topo):
         mx(5, 128, land, 0, "kq", 128, lk + ["kq"])
         for i in range(4):
             mx(1 + i, 128, "h", 128 * i, land, 0, lk + ["h%d" % i], True, False)
+        gaps[0]()
         act(T.zs[:, 0:128], bank(0, 128), ["bank0"], ["zs0"])
         cp(T.zs[:, 128:256], bank(5, 128), ["bank5"], ["zs1"])
         tt(T.zg[:], T.zs[:, 0:P].indirect(T.zl[:, 0:4]), T.dm[:], ALU.add, ["zs0", "zs1", "zl", "dm"], ["zg"])
@@ -340,16 +378,16 @@ def rank_program(g, core, T, topo):
             ts(T.xb[:, k:4 * N:4], T.bki[:], T.rm[:, 16 * k + 15:16 * k + 16], ALU.add, ["bki", "rm", "xbz"], ["xb%d" % k], T.rm[:, 63:64], ALU.is_lt)
         quant(xq, 0, 128, T.xb[:], ["xbz", "xb0", "xb1", "xb2"], [xq])
         mx(6, 128, "ws", 0, xq, 0, ["ws", xq])
+        gaps[1]()
         tt(T.fl[:], bank(6, N), T.v4[:], ALU.add, ["bank6", "v4"], ["fl"])
         cp(T.ct[:], T.fl[:], ["fl"], ["ct"])
         pick(kp, 0, "kq", P, T.ct[:, 0:8], 128, ["kq", "ct"], kp)
         for i in range(4):
             mx(1 + i, 128, "h", 128 * i, kp, 0, [kp + "_c", kp + "_s", "h%d" % i], False, True)
-        nodt, rn = T["nodt" + n], T["rn" + n]
-        yk = ["yy0", "yy1", "yy2", "yy3"]
-        tt(T.yy[:], T.nxf[:, 0:P].indirect(T.ct[:, 0:8]), T.locrow[:], ALU.add, ["nxf", "ct", "locrow"], yk)
-        turn(nodt[:], T.yy[:], yk, ["nodt" + n])
-        send("rn" + n, lambda d: nodt[:, 32 * (d // 2):32 * (d // 2) + 1], lambda d: rn[:, 4 * rank:4 * rank + 1], ["nodt" + n])
+        rn, at = T["rn" + n], 128 * t
+        tt(T.yy[:], T.nxf[:, 0:P].indirect(T.ct[:, 0:8]), T.locrow[:], ALU.add, ["nxf", "ct", "locrow"], ["yy"])
+        turn(T.nodt[:, at:at + 128], T.yy[:], ["yy"], ["nodt" + n])
+        send("rn" + n, lambda d: T.nodt[:, at + 32 * (d // 2):at + 32 * (d // 2) + 1], lambda d: rn[:, 4 * rank:4 * rank + 1], ["nodt" + n])
         for i in range(4):
             if i % 2:
                 act(nt[:, i:512:4], bank(1 + i, 128), ["bank%d" % (1 + i)], ["nt%s%d" % (n, i)])
@@ -360,17 +398,19 @@ def rank_program(g, core, T, topo):
         def back(d):
             return A + CAPP * seen(d)
 
+        if t == 0:
+            send("hand1", lambda d: T.new0s[:, 0:128], lambda d: T.hand1[:, 0:128], ["new0"])
         send("ret%s_c" % n, lambda d: codes("new" + n, CAPP * place(d), CAPP * place(d) + CAPP), lambda d: codes(win, back(d), back(d) + CAPP), ["new" + n])
-        send("ret%s_s" % n, lambda d: T["new%ss" % n][:, goes(d)], lambda d: T[win + "s"][:, back(d):back(d) + CAPP], ["new" + n])
-        cp(rn[:, 4 * rank:4 * rank + 1], nodt[:, 32 * (rank // 2):32 * (rank // 2) + 1], ["nodt" + n], ["rnown" + n])
+        if t == 1:
+            send("ret1_s", lambda d: T.new1s[:, goes(d)], lambda d: T.winbs[:, back(d):back(d) + CAPP], ["new1"])
+        cp(rn[:, 4 * rank:4 * rank + 1], T.nodt[:, at + 32 * (rank // 2):at + 32 * (rank // 2) + 1], ["nodt" + n, "rnz" + n], ["rnown" + n])
         pick(win, back(rank), "new" + n, 128, T.ol[:, 0:1], CAPP, ["new" + n, "ol"], win + "own")
 
     def home(t):
         n = str(t)
         vv = T["vv" + n]
-        cp(T.vm[:], T["rn" + n][:, 0:4 * N:4], ["in_rn" + n, "rnown" + n], ["vm"])
-        cp(T.mn[:], T.vm[:, 0:N].indirect(T.elst[:, 0:8]), ["vm", "elst"], ["mn"])
-        turn(T.win[:, A:160], T.mn[:], ["mn"], ["winr"])
+        cp(T.mn[:, 0:128], T["rn" + n][:, 0:4 * N].indirect(T.elst[:, 0:8]), ["in_rn" + n, "rnown" + n, "rnz" + n, "elst"], mns)
+        turn(T.win[:, A:160], T.mn[:, 0:128], mns, ["winr"])
         cp(vv[:], T.win[:, 0:160].indirect(T["nu" + n][:, 0:2]), ["winq", "winr", "nu" + n], ["vv" + n])
         ts(T.dr[:], vv[:], 14, ALU.logical_shift_right, ["vv" + n], ["dr"])
 
@@ -378,100 +418,114 @@ def rank_program(g, core, T, topo):
         n = str(t)
         ts(T.dl[:], T["vv" + n][:], 63, ALU.bitwise_and, ["vv" + n], ["dl"])
         ts(T.dn[:], T.dr[:], 64.0, ALU.mult, ["dr"], ["dn"])
-        tt(T["ndf" + n][:], T.dn[:], T.dl[:], ALU.add, ["dl", "dn"], ["ndf" + n])
+        tt(T.ndf[:, A * t:A * t + A], T.dn[:], T.dl[:], ALU.add, ["dl", "dn"], ["ndf" + n])
+
+    def nothing():
+        pass
 
     for h in range(2):
-        ts(T.dr[:, 16 * h:16 * h + 16], T.strb[:, h:A:2], 6, ALU.arith_shift_right, ["strb"], ["dr"])
+        ts(T.dr[:, 16 * h:16 * h + 16], T.strb[:, h:A:2], 6, ALU.arith_shift_right, ["strb"], ["drh%d" % h])
     for h in range(2):
-        ts(T.xm[:, 16 * h:16 * h + 16], T.strb[:, h:A:2], 63, ALU.bitwise_and, ["strb"], ["xm"])
-    lists(0)
+        ts(T.xm[:, 16 * h:16 * h + 16], T.strb[:, h:A:2], 63, ALU.bitwise_and, ["strb"], ["xmh%d" % h])
+    wrote["dr"], wrote["xm"] = wrote["drh1"], wrote["xmh1"]
+    lists(0, nothing)
     for i, c in enumerate(picked):
         k = place(cores.index(c))
-        cp(T.pl[:, i:i + 1], T.shx[:, k:k + 1], ["shx"], ["pl%d" % i])
+        ts(T.pl[:, i:i + 1], T.ti0[:, k:k + 1], 1.0 / 16384, ALU.mult, tab("l0"), ["pl%d" % i], float(A - 1), ALU.min)
     pick("send0", 0, "qx", 128, T.pl[:, 0:2], 32, ["qx", "pl0", "pl1"], "send0")
     slot = {cores.index(c): i * CAPP for i, c in enumerate(picked)}
     send("pick_c", lambda d: codes("send0", slot[d], slot[d] + CAPP), lambda d: codes("lx0", A * seen(d), A * seen(d) + CAPP), ["send0_c"])
     send("pick_s", lambda d: T.send0s[:, slot[d]:slot[d] + CAPP], lambda d: T.lx0s[:, A * seen(d):A * seen(d) + CAPP], ["send0_s"])
     cp(T.xr0[:, 4 * me:4 * me + 1], T.ti0[:, me:me + 1], tab("l0"), ["xrown0"])
     ts(T.nxh[0:32, :], T.nxt[0:32, :], 6, ALU.arith_shift_right, ["nxt"], ["nxh"])
+    ts(T.pd[:], T.iop[:], 4, ALU.arith_shift_right, ["iop"], ["pd"])
     ts(T.nxp[0:32, :], T.nxh[0:32, :], float(16384 - 64), ALU.mult, ["nxh"], ["nxp"])
+    ts(T.cc[:], T.ioj[:, 0:N], float(A * 16384), ALU.mult, ["ioj"], ["cc"])
     tt(T.nxp[0:32, :], T.nxp[0:32, :], T.nxt[0:32, :], ALU.add, ["nxp", "nxt"], ["nxp"])
+    tt(T.blk[:], T.pd[:], T.ioj[:, 0:N], ALU.is_equal, ["pd", "ioj"], ["blk"])
     turn(T.nxq[0:32, :], T.nxp[0:32, :], ["nxp"], ["nxq"])
     dma("s", "nxr", T.nx1[0:1, :], T.nxq[0:16, 0:16], ["nxq"], ["nx1"])
     for k in range(3):
         act(T.wb[:, k:512:4], T.mm[:], ["mm", "wb"], ["wb%d" % k])
-    ts(T.pd[:], T.iop[:], 4, ALU.arith_shift_right, ["iop"], ["pd"])
-    fill(T.fs[:], 1.0, ["fs"])
-    ts(T.cc[:], T.ioj[:, 0:N], 32.0, ALU.mult, ["ioj"], ["cc"])
-    tt(T.blk[:], T.pd[:], T.ioj[:, 0:N], ALU.is_equal, ["pd", "ioj"], ["blk"])
-    ccs = ["cc"]
-    for s, c in enumerate(cores):
-        if c != core and core in plans[c][1]:
-            k = place(s)
-            fill(T.fs[:, k:k + 1], 0.0, ["fs"])
-            ts(T.cc[:, k:k + 1], T.r1[:], float(32 * k - 1), ALU.add, ["r1", "cc"], ["cc%d" % k])
-            ccs.append("cc%d" % k)
+    fill(T.cc[:, me:me + 1], float(OWN * 16384), ["cc"])
+    fixed = sorted(place(s) for s, c in enumerate(cores) if c != core and core in plans[c][1])
+    lsk, runs, begin = [], [], 0
+    for k in fixed + [N]:
+        if k > begin:
+            runs.append((begin, k))
+        begin = k + 1
+    for k in fixed:
+        lsk.append("lsu%d" % k)
+        ts(T.lsu[:, k:k + 1], T.r1[:], float(A * k - 1), ALU.add, ["r1"], lsk[-1:])
     ts(T.ibq[:], T.ioj[:, 0:4], 0.25, ALU.mult, ["ioj"], ["ibq"])
+    quant("lx0", OWN, OWN + 128, T.xt[:], ["xt", "xtz"], ["lx0own"])
     quant("kq", 0, P, T.kt[:], ["kt"], ["kq"])
     for i in range(4):
         quant("h", 128 * i, 128 * i + 128, T.hb[:, 3 - i:515 - i], ["hb"], ["h%d" % i])
     ts(T.bki[:], T.blk[:], -1.0, ALU.add, ["blk"], ["bki"], -1e29, ALU.mult)
     ts(T.dm[:], T.mm[:, 0:64], -1.0, ALU.add, ["mm"], ["dm"], 1e29, ALU.mult)
     quant("ws", 0, 128, T.wb[:], ["wb", "wb0", "wb1", "wb2"], ["ws"])
+    iota(T.io16[:], [[16, 8]], A - 1, 0, ["io16"])
+    iota(T.el[:], [[8, 4], [0, 2]], 0, 0, ["el"])
+    iota(T.xa1[:], [[16384, A]], 0, 0, ["xa1"], True)
     op("g", lambda e: e.partition_broadcast(T.nxf[:], T.nx1[0:1, :], 128), ["nx1"], ["nxf"])
     iota(T.locrow[:], [[0, 4], [64, 32]], 64 * (A + 32 * (rank // 2)), 0, ["locrow"], True)
-    iota(T.el[:], [[2, 4], [0, 2]], 0, 0, ["el"])
     iota(T.rowc[:], [[1, 128]], A, 0, ["rowc"], True)
-    iota(T.io16[:], [[16, 8]], -1, 0, ["io16"])
-    iota(T.xa1[:], [[16384, A]], 0, 0, ["xa1"], True)
-    received(0)
     ts(T.ol[:, 0:1], T.r1[:], float(mine - 1), ALU.add, ["r1"], ["ol"])
-    serve(0)
-    dma("s", "w", T.wt[:], T.w[:], [], ["wt"])
+    ts(T.slott[:], T.io16[:], T.r1[:, 0:1], ALU.add, ["io16", "r1"], ["slott"])
+    received(0)
+
+    def first_nodes():
+        ts(T.win[:, 0:A], T.dr[:], 16384.0, ALU.mult, ["dr"], ["winq"])
+        ts(T.ib[:], T.pd[:], 1, ALU.bitwise_and, ["pd"], ["ib"])
+        tt(T.win[:, 0:A], T.win[:, 0:A], T.xx[:, 0:A], ALU.add, ["winq", "xx"], ["winq"])
+        ts(T.f3[:], T.ib[:], -4.0 if odd else 4.0, ALU.mult, ["ib"], ["f3"], 4.0 * odd, ALU.add)
+
+    def more_nodes():
+        tt(T.win[:, 0:A], T.win[:, 0:A], T.xa1[:], ALU.subtract, ["winq", "xa1"], ["winq"])
+        tt(T.f3[:], T.f3[:], T.el[:], ALU.add, ["f3", "el"], ["f3"])
+
+    dma("s", "w", T.wt[:], T.w[:], ["land0_c"], ["wt"])
     dma("s", "ownw", codes("wina", 0, A), codes("qx", 0, A), ["qx"], ["winaq"])
     dma("s", "ownw", T.winas[:, 0:A], T.qxs[:, 0:A], ["qx"], ["winaq2"])
-    ts(T.win[:, 0:A], T.dr[:], 16384.0, ALU.mult, ["dr"], ["winq"])
-    ts(T.slott[:], T.io16[:], T.r1[:, 0:1], ALU.add, ["io16", "r1"], ["slott"])
-    ts(T.ia[:], T.pd[:], 1, ALU.bitwise_and, ["pd"], ["ia"])
-    tt(T.win[:, 0:A], T.win[:, 0:A], T.xx[:], ALU.add, ["winq", "xx"], ["winq"])
-    ts(T.fl[:], T.ia[:], -1.0 if odd else 1.0, ALU.mult, ["ia"], ["fl"], float(odd), ALU.add)
-    tt(T.win[:, 0:A], T.win[:, 0:A], T.xa1[:], ALU.subtract, ["winq", "xa1"], ["winq"])
-    tt(T.fl[:], T.fl[:], T.el[:], ALU.add, ["fl", "el"], ["fl"])
-    cp(T.elst[:], T.fl[:], ["fl"], ["elst"])
-    inverse(0)
+    serve(0, [lambda: inverse_a(0), first_nodes])
+    inverse_b(0, [more_nodes, lambda: cp(T.elst[:], T.f3[:], ["f3"], ["elst"])])
     home(0)
-    ts(T.xm[:], T.vv0[:], 16383, ALU.bitwise_and, ["vv0"], ["xm"])
-    lists(1)
+    lists(1, lambda: ts(T.xm[:], T.vv0[:], 16383, ALU.bitwise_and, ["vv0"], ["xm"]))
+    ts(T.shx[:], T.ti1[:], 6, ALU.logical_shift_right, tab("l1"), ["shx"], 255, ALU.bitwise_and)
+    cp(T.xr1[:, 4 * me:4 * me + 1], T.ti1[:, me:me + 1], tab("l1"), ["xrown1"])
     cp(T.sl[:], T.shx[:], ["shx"], ["sl"])
     wina = ["winaq", "winaq2", "winaown_c", "winaown_s", "in_ret0"]
     pick("send1", 0, "wina", 160, T.sl[:, 0:8], 128, wina + ["sl"], "send1")
     send("land1_c", lambda d: codes("send1", CAPP * place(d), CAPP * place(d) + CAPP),
          lambda d: codes("land1", CAPP * seen(d), CAPP * seen(d) + CAPP), ["send1_c"])
     send("land1_s", lambda d: T.send1s[:, goes(d)], lambda d: T.land1s[:, CAPP * seen(d):CAPP * seen(d) + CAPP], ["send1_s"])
-    cp(T.xr1[:, 4 * me:4 * me + 1], T.ti1[:, me:me + 1], tab("l1"), ["xrown1"])
     pick("land1", mine, "send1", 128, T.ol[:, 0:1], CAPP, ["send1_c", "send1_s", "ol"], "land1own")
-    for h in range(2):
-        cp(T.nd0f[:, 16 * h:16 * h + 16], T.strb[:, h:A:2], ["strb"], ["nd0f"])
-    number(0)
+    inverse_a(1)
+    inverse_b(1, [lambda: cp(T.win[:, 0:A], T.vv0[:], ["vv0"], ["winq"]),
+                  lambda: pick("winb", 0, "wina", 160, T.nu0[:, 0:2], A, wina + ["nu0"], "winbq")])
     received(1)
-    serve(1)
-    dma("s", "nd0", T.nd[0:1, :], T.nd0f[0:1, :], ["nd0f"], [])
-    dma("s", "nd1", T.nd[1:2, :], T.ndf0[0:1, :], ["ndf0"], [])
-    cp(T.win[:, 0:A], T.vv0[:], ["vv0"], ["winq"])
-    inverse(1)
-    pick("winb", 0, "wina", 160, T.nu0[:, 0:2], A, wina + ["nu0"], "winbq")
-    quant("wq", 0, 128, T.wt[:], ["wt"], ["wq"])
-    quant("fin", 0, 128, T.xt[:], ["xt", "xtz"], ["fin_c", "fin_s"])
+
+    def last_tiles():
+        quant("wq", 0, 128, T.wt[:], ["wt"], ["wq"])
+        quant("fin", 0, 128, T.xt[:], ["xt", "xtz"], ["fin_c", "fin_s"])
+
+    serve(1, [last_tiles, nothing])
+    for h in range(2):
+        cp(T.nd0f[:, 16 * h:16 * h + 16], T.strb[:, h:A:2], ["strb"], ["nd0f%d" % h])
+    number(0)
+    dma("s", "nd0", T.nd[0:1, :], T.nd0f[0:1, :], ["nd0f0", "nd0f1"], [])
+    dma("s", "nd1", T.nd[1:2, :], T.ndf[0:1, 0:A], ["ndf0"], [])
     home(1)
     number(1)
-    dma("s", "nd2", T.nd[2:3, :], T.ndf1[0:1, :], ["ndf1"], [])
+    dma("s", "nd2", T.nd[2:3, :], T.ndf[0:1, A:2 * A], ["ndf1"], [])
     pick("fin", 0, "winb", 160, T.nu1[:, 0:2], A, ["winbq_c", "winbq_s", "winbown_c", "winbown_s", "in_ret1", "nu1"], "fin")
     mx(7, 128, "wq", 0, "fin", 0, ["wq", "fin_c", "fin_s"])
-    act(T.ys[:], bank(7, A), ["bank7"], ["ys"])
-    dma("a", "y", T.y[:], T.ys[:], ["ys"], [])
+    cp(T.ys[:], bank(7, A), ["bank7"], ["ys"])
     dma("s", "oc", T.oc[:], codes("fin", 0, A), ["fin_c"], [])
     for k in range(4):
         dma("s" if k % 2 else "a", "osc", T.osc[4 * k:4 * k + 4, :], T.fins[32 * k:32 * k + 4, 0:A], ["fin_s"], [])
+    dma("a", "y", T.y[:], T.ys[:], ["ys"], [])
     g.wait_ge(T.sem.left, left[0])
     for q, s in sems.items():
         g.wait_ge(T.sem[s], count[q])

@@ -3,9 +3,25 @@ from concourse.mybir import dt, AluOpType, AxisListType, ActivationFunctionType
 
 N, P, A, CAPP = 8, 256, 32, 16
 F8, U8, F32, BF, I32, U16 = "float8_e4m3fn_x4", "uint8", "float32", "bfloat16", "int32", "uint16"
-EMPTY = 256 * 16384
+Q = 2048
+EMPTY = 256 * Q
 S = A + 1
 OWN = N * A
+KINDS = ["near", "plane", "diag", "mate"]
+
+MSG = {"wide_c": ("qxc", "lx0c", "lx0", A), "wide_s": ("qxs", "lx0s", "lx0", A), "pick_c": ("send0c", "lx0c", "lx0", CAPP),
+       "pick_s": ("send0s", "lx0s", "lx0", CAPP), "xr0": ("ti0", "xr0", "xr0", 1), "xr1": ("tx", "xr1", "xr1", 1),
+       "rn0": ("nodt0", "rn0", "rn0", 1), "rn1": ("nodt1", "rn1", "rn1", 1),
+       "ret0_c": ("new0c", "winac", "ret0", CAPP), "ret0_s": ("new0s", "winas", "ret0s", CAPP),
+       "land1_c": ("send1c", "land1c", "land1", CAPP), "land1_s": ("send1s", "land1s", "land1", CAPP),
+       "ret1_c": ("new1c", "winbc", "ret1", CAPP), "ret1_s": ("new1s", "winbs", "ret1", CAPP)}
+VIA = {"wide_s": {"diag": "F", "plane": "B"},
+       "ret0_s": {"diag": "F", "mate": "F", "plane": "B", "near": "B"},
+       "xr1": {"diag": "F", "mate": "F", "plane": "B", "near": "B"}}
+CALLS = {"wide": (["wide_c"], 4), "wide2": (["wide_s", "+wide_s"], 2), "xr0": (["xr0"], 4), "pick_c": (["pick_c"], 2), "pick_s": (["pick_s"], 4),
+         "rn0": (["rn0"], 4), "ret0": (["+ret0_s"], 4), "ret0_c": (["ret0_c"], 4),
+         "xr1": (["+xr1"], 4), "land1_c": (["land1_c"], 4), "land1_s": (["land1_s"], 4),
+         "rn1": (["rn1"], 4), "ret1_c": (["ret1_c"], 4), "ret1_s": (["ret1_s"], 4)}
 SCRATCH = {}
 
 
@@ -13,34 +29,34 @@ def _add(name, cols, dtype, where="sbuf"):
     SCRATCH[name] = (where, [128, cols], dtype)
 
 
-for _n, _c in (("qx", 128), ("lx0", OWN + 128), ("send0", 32), ("land0", 128), ("new0", 128), ("wina", 160), ("send1", 128),
+for _n, _c in (("qx", 128), ("lx0", OWN + 128), ("send0", 32), ("land0", 128), ("new0", 128), ("wina", 160), ("q1", 32), ("send1", 128),
                ("land1", 128), ("new1", 128), ("winb", 160), ("fin", 128), ("kq", 256), ("wq", 128), ("h", 512), ("ws", 128),
                ("kp0", 128), ("kp1", 128), ("xq0", 128), ("xq1", 128)):
     _add(_n + "c", _c, F8)
     _add(_n + "s", _c, U8)
-_add("hand0", A, U8)
-_add("hand1", 128, U8)
 for _n, _c, _d in (("xt", 512, BF), ("kt", 1024, BF), ("wt", 512, BF), ("hb", 516, BF), ("wb", 512, BF), ("xb", 512, BF),
-                   ("iop", 8, I32), ("ioj", 32, I32), ("jmp", 128, I32), ("xa0", 32, F32), ("xa1", 32, F32),
-                   ("el", 8, I32), ("elst", 8, U16), ("locrow", 128, F32), ("rowc", 128, F32), ("io16", 8, I32), ("slott", 8, F32),
-                   ("pd", 8, I32), ("mm", 128, F32), ("dm", 64, F32), ("blk", 8, F32), ("bki", 8, F32),
-                   ("r1", 1, F32), ("ibq", 4, F32), ("dcol", 4, F32), ("rst", 4 * S, BF),
-                   ("cc", 8, F32), ("str1", 32, I32), ("strb", 32, I32), ("nd0f", 32, F32),
-                   ("nxt", 32, I32), ("nxh", 32, I32), ("nxp", 32, F32), ("nxq", 32, F32), ("nx1", 256, F32), ("nxf", 256, F32),
-                   ("lsu", 8, U16), ("pl", 2, U16), ("sl", 8, U16), ("ol", 2, U16), ("ys", 32, F32),
-                   ("ib", 8, I32), ("f3", 8, F32),
-                   ("dr", 32, I32), ("xm", 32, I32), ("xx", S + 1, F32), ("shx", 8, I32), ("zl", 4, U16), ("ct", 8, U16),
-                   ("win", 160, F32), ("lu", 8, U16), ("so", 160, F32), ("dn", 32, F32), ("dl", 32, I32),
-                   ("vi", 8, I32), ("vm", 8, F32), ("v", 1, F32), ("v4", 8, F32), ("zs", 256, F32), ("zg", 64, F32), ("rm", 64, F32),
-                   ("eqb", 4 * S, BF), ("cum", 4 * S + 2, BF), ("ltb", 4 * S, BF), ("yy", 128, F32), ("mn", 4 * S, F32),
-                   ("ia", 8, I32), ("fl", 8, F32), ("f2", 8, F32), ("n2", 2, F32), ("nodt", 256, F32), ("ndf", 64, F32)):
+                   ("iop", 8, I32), ("ioj", 32, F32), ("jmp", 128, I32), ("jmq", 128, I32), ("xa", 32, F32),
+                   ("el", 16, I32), ("elst", 8, U16), ("rowc", 128, F32), ("io16", 8, I32), ("slott", 8, F32),
+                   ("pd", 8, I32), ("mm", 128, F32), ("dm", 64, F32), ("xl", 2, U16),
+                   ("r1", 4, F32), ("ec", 1, F32), ("dcol", 4, F32), ("rst", 4 * S, BF),
+                   ("cc", 8, F32), ("stc", 1, I32), ("stw", 32, F32), ("strb", 32, F32),
+                   ("nxt", 16, I32), ("gl", 2, U16), ("nxp", 16, F32), ("nl", 16, U16), ("nx1", 256, F32), ("nxf", 256, F32),
+                   ("lsu", 8, U16), ("sl", 8, U16), ("ol", 2, U16), ("ys", 32, F32), ("ib", 8, I32), ("f3", 8, F32),
+                   ("xr0", 4 * N, F32), ("tx", N, U16), ("xr1", 8 * N, U16),
+                   ("dr", 32, I32), ("xx", S + 1, F32), ("zl", 4, U16), ("ct", 8, U16),
+                   ("win", 160, F32), ("lu", 8, U16), ("so", 160, F32), ("dn", 32, F32),
+                   ("vi", 8, I32), ("v4", 8, I32), ("vm", 16, F32), ("v", 1, F32), ("zs", 256, F32), ("zg", 64, F32), ("rm", 72, F32),
+                   ("eqb", 4 * S, BF), ("cum", 4 * S + 2, BF), ("yy", 128, F32), ("mn", 4 * S, F32), ("sp", 128, F32),
+                   ("ia", 8, I32), ("fl", 8, F32), ("f2", 8, F32), ("n2", 2, F32)):
     _add(_n, _c, _d)
 for _t in ("0", "1"):
-    for _n, _c, _d in (("ti", 8, I32), ("xr", 32, I32), ("nt", 512, BF), ("rn", 32, F32), ("vv", 32, I32), ("nu", 2, U16)):
+    for _n, _c, _d in (("ti", 8, F32), ("nt", 512, BF), ("rn", 32, F32), ("nu", 2, U16), ("nodt", 128, F32)):
         _add(_n + _t, _c, _d)
+for _n in VIA:
+    _add("h" + _n, 4 * MSG[_n][3], SCRATCH[MSG[_n][0]][2])
 _add("bank", 512 * 8, F32, "psum")
-ARRIVE = ["lx0", "xr0", "rn0", "ret0", "xr1", "land1", "rn1", "ret1", "hand0", "hand1"]
-DMAS = ["st", "x", "ky", "nx", "w", "nxr", "ownw", "nd0", "nd1", "nd2", "oc", "osc", "y"]
+ARRIVE = ["lx0", "xr0", "rn0", "ret0", "ret0s", "xr1", "land1", "rn1", "ret1"] + ["h" + _n for _n in VIA]
+DMAS = ["st", "x", "ky", "nx", "w", "ownw", "nd0", "nd1", "nd2", "oc", "osc", "y"]
 SEMAPHORES = ["sg", "sv", "sa", "sp", "left"] + ["a_" + k for k in ARRIVE] + ["d_" + k for k in DMAS]
 
 
@@ -48,97 +64,128 @@ def _bits(m):
     return bin(m).count("1")
 
 
-def _helper(topo, cores, me):
-    return [c for c in topo.cores_of(me) if c not in cores and topo.die(c) == topo.die(me) and all(topo.may_write(c, d) for d in cores)][0]
+def _view(T, name, a, n):
+    v = T[name][:, a:a + n]
+    return v.bitcast(dt.uint8) if SCRATCH[name][2] == F8 else v
 
 
-def _plan(topo, cores, me):
-    others = [c for c in cores if c != me]
-    near = [c for c in others if c in topo.cores_of(me)]
-    far = [c for c in others if c not in near]
-    picked = [c for c in far if topo.mates(me, c)]
-    port = topo.engines(me, far[0])
-    inner = [e for e in topo.engines(me, near[0]) if e not in port]
-    load = {e: 0 for e in port}
+def _places(topo, cores, rank):
+    me = cores[rank]
+    kind = ["near" if c in topo.cores_of(me) else "plane" if topo.same_plane(me, c) else "mate" if topo.mates(me, c) else "diag" for c in cores]
+    return kind, [2 * KINDS.index(kind[r]) + (r + rank) % 2 for r in range(N)]
+
+
+def _plan(topo, T, cores, rank):
+    me = cores[rank]
+    kind, place = _places(topo, cores, rank)
+    others = [r for r in range(N) if r != rank]
+    spare = [c for c in topo.cores_of(me) if c not in cores and topo.die(c) == topo.die(me)]
+    full = [c for c in spare if all(topo.may_write(c, d) for d in cores)][0]
+    helper = {"F": full, "B": [c for c in spare if c != full][0]}
+    port = topo.engines(me, cores[kind.index("mate")])
+    inner = [e for e in topo.engines(me, full) if e not in port]
+
+    def ends(m, r):
+        k = place[r]
+        if m[:4] == "wide":
+            return 0, A * k
+        if m[:4] == "pick":
+            return CAPP * (k % 2), A * k
+        if m[:2] == "xr":
+            return k, SCRATCH[m][1][1] // N * k
+        if m[:2] == "rn":
+            return 32 * (k // 2), 4 * k
+        return CAPP * k, CAPP * k + (0 if m[:4] == "land" else A)
+
+    def dests(m):
+        return [r for r in others if (kind[r] == "mate") == (m[:4] == "pick") or m[:4] not in ("wide", "pick")]
+
+    load = {}
     turn = [0]
 
-    def masks(dsts, fresh=False):
-        o = {}
-        if fresh:
+    def deal(core, items, cap):
+        off = [i for i in items if i[0] not in topo.cores_of(core) or core != me]
+        on = [i for i in items if i[0] in topo.cores_of(core) and core == me]
+        if off and len(port) % len(off):
+            k = turn[0] % len(off)
+            turn[0] += 2
+            off = off[k:] + off[:k]
+        out = []
+        for group, pool in ((off, port), (on[::-1], inner)):
+            free = sorted(pool, key=lambda e: load.get((core, e), 0))
+            for i, (c, sem, src, dst) in enumerate(group):
+                rest = len(group) - i
+                most = min(cap, len(free) // rest if pool is port else len(free) - 2 * (rest - 1))
+                take = 1
+                while 2 * take <= most:
+                    take *= 2
+                for e in free[:take]:
+                    load[core, e] = load.get((core, e), 0) + 8 // take
+                out.append((c, sum(1 << e for e in free[:take]), sem, src, dst))
+                free = free[take:]
+        return out
+
+    plan = {}
+    for name, (parts, cap) in CALLS.items():
+        items = []
+        if name[:2] == "rn":
             for e in port:
-                load[e] = 0
-        for c in dsts:
-            if c in near:
-                o[c] = sum(1 << e for e in inner[::2])
-        f = [c for c in dsts if c in far]
-        if len(port) % len(f) == 0:
-            share = len(port) // len(f)
-            for i, c in enumerate(f):
-                o[c] = sum(1 << e for e in port[share * i:share * i + share])
-            return o
-        k = turn[0] % len(f)
-        turn[0] += 2
-        f = f[k:] + f[:k]
-        free = sorted(port, key=lambda e: load[e])
-        doubles = len(free) - len(f)
-        for i, c in enumerate(f):
-            take = 1 if i < len(f) - doubles else 2
-            o[c] = sum(1 << e for e in free[:take])
-            for e in free[:take]:
-                load[e] += 2 // take
-            free = free[take:]
-        return o
-
-    wide = [c for c in others if c not in picked]
-    helper = _helper(topo, cores, me)
-    out = {"wide_c": masks(wide), "wide_s": masks(wide), "xr0": masks(others), "pick_c": masks(picked), "pick_s": masks(picked),
-           "ret0_s": masks(others, True), "hand0": {helper: sum(1 << e for e in inner[1::2])}, "hand1": {helper: sum(1 << e for e in inner)}}
-    for k in ("rn0", "ret0_c", "xr1", "land1_c", "land1_s", "rn1", "ret1_c", "ret1_s"):
-        out[k] = masks(others, k in ("rn0", "rn1"))
-    return out, picked, wide
+                load[me, e] = 0
+        for m in parts:
+            if m[0] != "+":
+                src, dst, sem, n = MSG[m]
+                for r in dests(m):
+                    if kind[r] not in VIA.get(m, {}):
+                        a, b = ends(m, r)
+                        items.append((cores[r], sem, _view(T, src, a, n), _view(T, dst, b, n)))
+                continue
+            m = m[1:]
+            src, dst, sem, n = MSG[m]
+            w = A if m == "wide_s" else 4 * n
+            for h in sorted(set(VIA[m].values())):
+                mine = [r for r in dests(m) if VIA[m].get(kind[r]) == h]
+                lo = min(ends(m, r)[0] for r in mine) // w * w
+                items.append((helper[h], "h" + m, _view(T, src, lo, w), _view(T, "h" + m, 0, w)))
+                on = [(cores[r], sem, _view(T, "h" + m, ends(m, r)[0] - lo, n), _view(T, dst, ends(m, r)[1], n)) for r in mine]
+                plan[helper[h], m] = deal(helper[h], on, 4)
+        plan[me, name] = deal(me, items, cap)
+    return plan
 
 
-ROUTE = {"wide_c": "lx0", "wide_s": "lx0", "pick_c": "lx0", "pick_s": "lx0", "xr0": "xr0", "rn0": "rn0", "ret0_c": "ret0", "ret0_s": "ret0",
-         "xr1": "xr1", "land1_c": "land1", "land1_s": "land1", "rn1": "rn1", "ret1_c": "ret1", "ret1_s": "ret1",
-         "hand0": "hand0", "hand1": "hand1"}
-
-
-def _hand_on(g, core, T, topo, cores, rank):
-    calls = _plan(topo, cores, cores[rank])[0]
-    odd, left = rank % 2, 0
-    for hand, call in (("hand0", "wide_s"), ("hand1", "ret0_s")):
-        g.wait_ge(T.sem["a_" + hand], _bits(calls[hand][core]))
-        tr = []
-        for c, m in calls[call].items():
-            rid, pid = topo.addr(c, core)
-            d = cores.index(c)
-            seen = rank ^ (d % 2)
-            if hand == "hand0":
-                src, dst = T.hand0[:, 0:A], T.lx0s[:, A * seen:A * seen + A]
-            else:
-                src, dst = T.hand1[:, CAPP * (d ^ odd):CAPP * (d ^ odd) + CAPP], T.winas[:, A + CAPP * seen:A + CAPP * seen + CAPP]
-            tr.append(RemoteDMATransfer(dst_ids=[DstId(rid=rid, pnc=pid)], dma_engine_mask=m, remote_sem=T.sem["a_" + ROUTE[call]], src=src, dst=dst))
-            left += _bits(m)
-        g.remote_dma_fused(tr, local_sem=T.sem.left)
-    g.wait_ge(T.sem.left, left)
+def _fused(g, T, topo, core, call):
+    tr = []
+    for c, m, sem, src, dst in call:
+        rid, pid = topo.addr(c, core)
+        tr.append(RemoteDMATransfer(dst_ids=[DstId(rid=rid, pnc=pid)], dma_engine_mask=m, remote_sem=T.sem["a_" + sem], src=src, dst=dst))
+    g.remote_dma_fused(tr, local_sem=T.sem.left)
+    return sum(_bits(t[1]) for t in call)
 
 
 def rank_program(g, core, T, topo):
     rank = T.rank_of(core)
     cores = list(T.cores)
-    if rank is None:
-        for r, c in enumerate(cores):
-            if core in topo.cores_of(c) and _helper(topo, cores, c) == core:
-                _hand_on(g, core, T, topo, cores, r)
+    if not any(core in topo.cores_of(c) for c in cores):
         return
-    odd = rank % 2
-    plans = {c: _plan(topo, cores, c) for c in cores}
-    calls, picked, wide = plans[core]
+    plans = [_plan(topo, T, cores, r) for r in range(N)]
     want = {k: 0 for k in ARRIVE}
-    for c in cores:
-        if c != core:
-            for k, a in ROUTE.items():
-                want[a] += _bits(plans[c][0][k].get(core, 0))
+    for plan in plans:
+        for call in plan.values():
+            for c, m, sem, _s, _d in call:
+                if c == core:
+                    want[sem] += _bits(m)
+    if rank is None:
+        gone = 0
+        for plan in plans:
+            for (c, m), call in plan.items():
+                if c == core:
+                    g.wait_ge(T.sem["a_h" + m], want["h" + m])
+                    gone += _fused(g, T, topo, core, call)
+        if gone:
+            g.wait_ge(T.sem.left, gone)
+        return
+    calls = plans[rank]
+    kind, place = _places(topo, cores, rank)
+    at = [place.index(k) for k in range(N)]
     ALU, X, CP = AluOpType, AxisListType.X, ActivationFunctionType.Copy
     queues = {"g": g, "v": g.vector, "a": g.scalar, "p": g.tensor, "s": g.sync}
     sems = {"g": "sg", "v": "sv", "a": "sa", "p": "sp"}
@@ -193,15 +240,10 @@ def rank_program(g, core, T, topo):
 
     left = [0]
 
-    def send(call, src, dst, reads):
+    def send(names, reads):
         waits("g", reads, [])
-        tr = []
-        for c, m in calls[call].items():
-            rid, pid = topo.addr(c, core)
-            d = cores.index(c) if c in cores else None
-            tr.append(RemoteDMATransfer(dst_ids=[DstId(rid=rid, pnc=pid)], dma_engine_mask=m, remote_sem=T.sem["a_" + ROUTE[call]], src=src(d), dst=dst(d)))
-            left[0] += _bits(m)
-        g.remote_dma_fused(tr, local_sem=T.sem.left)
+        for name in names:
+            left[0] += _fused(g, T, topo, core, calls[core, name])
 
     for k in ARRIVE:
         wrote["in_" + k] = ("a_" + k, want[k])
@@ -258,110 +300,111 @@ def rank_program(g, core, T, topo):
     def zero(out, in_, reads, writes):
         op("a", lambda e: e.activation(out, in_, CP, scale=0.0), reads, writes)
 
-    def pick(out, oa, win, wb, off, n, reads, key):
-        cp(words(out, oa, oa + n), words(win, 0, wb).indirect(off), reads, [key + "_c"])
-        act(T[out + "s"][:, oa:oa + n], T[win + "s"][:, 0:wb].indirect(off), reads, [key + "_s"])
+    def scaled(out, in_, scale, bias, reads, writes):
+        op("a", lambda e: e.activation(out, in_, ActivationFunctionType.Identity, bias=bias, scale=scale), reads, writes)
 
-    def place(r):
-        return r ^ odd
+    def pick(out, oa, win, wb, off, n, reads, key, for_codes=(), for_scales=()):
+        cp(words(out, oa, oa + n), words(win, 0, wb).indirect(off), reads + list(for_codes), [key + "_c"])
+        act(T[out + "s"][:, oa:oa + n], T[win + "s"][:, 0:wb].indirect(off), reads + list(for_scales), [key + "_s"])
 
-    def seen(r):
-        return rank ^ (r % 2)
-
-    me = place(rank)
-    mine = CAPP * me
-    dma("s", "st", T.str1[0:1, 0:A], T.st[:], [], ["str1"])
     dma("a", "x", T.xt[:, 0:4 * A], T.x[:], [], ["xt"])
+    for b in range(4):
+        dma("s", "st", T.stc[32 * b:32 * b + 32, :], T.st[:], [], ["stc%d" % b])
     dma("s", "ky", T.kt[:], T.ky[:], [], ["kt"])
-    fill(T.nxt[0:32, :], 0, ["nxt"])
-    iota(T.jmp[:], [[1, 128]], 0, -1, ["jmp"])
+    for b in range(8):
+        dma("s", "nx", T.nxt[16 * b:16 * b + 16, :], T.nx[:], [], ["nxt%d" % b])
     iota(T.iop[:], [[0, 8]], 0, 1, ["iop"])
-    iota(T.dcol[:], [[2, 2], [place(1) - place(0), 2]], place(0), 0, ["dcol"], True)
-    iota(T.xa0[:], [[16384 + 64, A]], 0, 0, ["xa0"], True)
-    iota(T.ioj[:], [[1, A]], 0, 0, ["ioj"])
-    dma("a", "nx", T.nxt[0:16, 0:16], T.nx[:], ["nxt"], ["nxt"])
-    fill(T.xt[:, 4 * A:512], 0.0, ["xtz"])
+    iota(T.jmp[:], [[1, 128]], 0, -1, ["jmp"])
+    iota(T.dcol[:], [[at[2] - at[0], 2], [at[1] - at[0], 2]], at[0], 0, ["dcol"], True)
+    iota(T.xa[:], [[Q, A]], 0, 0, ["xa"], True)
+    iota(T.ioj[:], [[1, A]], 0, 0, ["ioj"], True)
+    iota(T.el[:], [[2, 8], [0, 2]], 0, 0, ["el"])
     fill(T.hb[:], 0.0, ["hb"])
+    zero(T.xt[:, 4 * A:512], T.hb[:, 4 * A:512], ["hb"], ["xtz"])
+    for j in (0, 2):
+        scaled(T.dcol[64:128, j:j + 2], T.dcol[64:128, j:j + 2], 1.0, float(at[4 + j] - at[j]), ["dcol"], ["dcol%d" % j])
     fill(T.rst[:], 1.0, ["rst"])
-    fill(T.eqb[:, A:4 * S:S], 0.0, ["eqz"])
-    fill(T.cum[:, 0:1], 0.0, ["cumz"])
+    fill(T.nu1[:], 0, ["nu1"])
     fill(T.xx[:, A:S], float(EMPTY), ["xxz"])
     fill(T.rst[:, A:4 * S:S], 0.0, ["rst"])
-    ts(T.hb[:, 3:515:4], T.jmp[:], 0.0, ALU.is_equal, ["jmp"], ["hb"], 0.5, ALU.mult)
     ts(T.ia[:], T.iop[:], 15, ALU.bitwise_and, ["iop"], ["ia"])
-    ts(T.jmp[:], T.jmp[:], 15, ALU.bitwise_and, ["jmp"], ["jmp"])
-    ts(T.r1[:], T.ia[:, 0:1], 1.0, ALU.add, ["ia"], ["r1"])
-    ts(T.dcol[64:128, :], T.dcol[64:128, :], 4.0, ALU.add, ["dcol"], ["dcol"])
-    ts(T.mm[:], T.jmp[:], 0.0, ALU.is_equal, ["jmp"], ["mm"])
-    zero(T.rn0[:], T.hb[:, 0:32], ["hb"], ["rnz0"])
-    zero(T.rn1[:], T.hb[:, 0:32], ["hb"], ["rnz1"])
-    zero(T.xb[:], T.hb[:, 0:512], ["hb"], ["xbz"])
-    zero(T.wb[:], T.hb[:, 0:512], ["hb"], ["wb"])
+    ts(T.pd[:], T.iop[:], 4, ALU.arith_shift_right, ["iop"], ["pd"])
+    ts(T.jmq[:], T.jmp[:], 15, ALU.bitwise_and, ["jmp"], ["jmq"])
+    ts(T.r1[:], T.ia[:, 0:4], 1.0, ALU.add, ["ia"], ["r1"])
+    scaled(T.cum[:, 0:1], T.r1[:, 0:1], float(2 * EMPTY), 0.0, ["r1"], ["cumz"])
+    scaled(T.eqb[:, A:4 * S:S], T.r1[:], float(2 * EMPTY), 0.0, ["r1"], ["eqz"])
+    ts(T.mm[:], T.jmq[:], 0.0, ALU.is_equal, ["jmq"], ["mm"])
+    ts(T.ib[:, 0:2], T.iop[:, 0:2], 2, ALU.arith_shift_right, ["iop"], ["ib"], 3, ALU.bitwise_and)
+    ts(T.vi[:, 0:1], T.iop[:, 0:1], 3, ALU.bitwise_and, ["iop"], ["vi"])
+    ts(T.v4[:, 0:1], T.iop[:, 0:1], 4, ALU.arith_shift_right, ["iop"], ["v4"], 1, ALU.bitwise_and)
+    ts(T.hb[:, 3:515:4], T.jmp[:], 0.0, ALU.is_equal, ["jmp"], ["hb"], 0.5, ALU.mult)
+    cp(T.ec[:], T.v4[:, 0:1], ["v4"], ["ec"])
+    ts(T.v[:], T.vi[:, 0:1], 16.0, ALU.mult, ["vi"], ["v"], 23.0, ALU.add)
+    zero(T.rn0[:], T.mm[:, 0:32], ["mm"], ["rnz0"])
+    zero(T.rn1[:], T.mm[:, 0:32], ["mm"], ["rnz1"])
+    zero(T.wb[:, 3:512:4], T.mm[:], ["mm"], ["wb"])
+    for k in range(3):
+        act(T.wb[:, k:512:4], T.mm[:], ["mm", "wb"], ["wb%d" % k])
     quant("qx", 0, 128, T.xt[:], ["xt", "xtz"], ["qx"])
-    op("g", lambda e: e.partition_broadcast(T.strb[:], T.str1[0:1, 0:A], 128), ["str1"], ["strb"])
-    send("wide_c", lambda d: codes("qx", 0, A), lambda d: codes("lx0", A * seen(d), A * seen(d) + A), ["qx"])
-    send("hand0", lambda d: T.qxs[:, 0:A], lambda d: T.hand0[:, 0:A], ["qx"])
+    send(["wide", "wide2"], ["qx"])
+    cp(T.stw[:], T.stc[:, 0:1].indirect(T.nu1[:, 0:2]), ["stc3", "nu1"], ["stw"])
+    turn(T.strb[:], T.stw[:], ["stw"], ["strb"])
 
     def tab(k):
         return ["tab%s%d%d" % (k, a, b) for a in range(2) for b in range(2)]
 
     mns = ["mn%d" % q for q in range(4)]
+    k0 = 2 * KINDS.index("mate")
 
-    def lists(t, masked):
-        n = str(t)
-        ti, x, k = T["ti" + n], T["xr" + n], tab("l" + n)
+    def lists(t):
         for q in range(4):
-            ts(T.eqb[:, S * q:S * q + A], T.dr[:], T.dcol[:, q:q + 1], ALU.is_equal, ["dr", "dcol"], ["eqb%d" % q])
-        masked()
-        scan(T.cum[:, 1:4 * S + 1], T.rst[:], T.eqb[:], 0.0, ALU.mult, ALU.add, ["rst", "eqz"] + ["eqb%d" % q for q in range(4)], ["cum"])
-        tt(T.xx[:, 0:A], T.xm[:], T["xa" + n][:], ALU.add, ["xm", "xa" + n], ["xx"])
-        ts(T.ltb[:], T.cum[:, 0:4 * S], T.r1[:, 0:1], ALU.is_lt, ["cum", "cumz", "r1"], ["ltb"], float(2 * EMPTY), ALU.mult)
+            ts(T.eqb[:, S * q:S * q + A], T.dr[:], T.dcol[:, q:q + 1], ALU.is_equal, ["dr", "dcol2"], ["eqb%d" % q], -2.0 * EMPTY, ALU.mult)
+        scan(T.cum[:, 1:4 * S + 1], T.rst[:], T.eqb[:], T.cum[:, 0:1], ALU.mult, ALU.add, ["rst", "eqz", "cumz"] + ["eqb%d" % q for q in range(4)], ["cum"])
         for q in range(4):
-            scan(T.mn[:, S * q:S * q + S], T.ltb[:, S * q:S * q + S], T.xx[:, 0:S], 0.0, ALU.max, ALU.min, ["ltb", "xx", "xxz"], [mns[q]])
+            scan(T.mn[:, S * q:S * q + S], T.cum[:, S * q:S * q + S], T.xx[:, 0:S], 0.0, ALU.max, ALU.min, ["cum", "cumz", "xx", "xxz"], [mns[q]])
         for a in range(2):
             for b in range(2):
-                cp(ti[64 * b:64 * b + 64, 4 * a:4 * a + 4], T.mn[64 * a:64 * a + 64, A:4 * S:S], mns, ["tabl%s%d%d" % (n, a, b)])
-        send("xr" + n, lambda d: ti[:, place(d):place(d) + 1], lambda d: x[:, 4 * seen(d):4 * seen(d) + 1], k + ["rnz0", "rnz1"])
+                if t:
+                    cp(T.tx[64 * b:64 * b + 64, 4 * a:4 * a + 4], T.mn[64 * a:64 * a + 64, A:4 * S:S], mns, ["tabx%d%d" % (a, b)])
+                elif a == k0 // 4:
+                    ts(T.sl[64 * b:64 * b + 64, k0:k0 + 2], T.mn[64 * a:64 * a + 64, S * (k0 % 4) + A:S * (k0 % 4 + 2):S], 1.0 / Q, ALU.mult, mns,
+                       ["sl%d" % b], float(A - 1), ALU.min)
+
+    def table(t):
+        for a in range(2):
+            for b in range(2):
+                act(T["ti%d" % t][64 * b:64 * b + 64, 4 * a:4 * a + 4], T.mn[64 * a:64 * a + 64, A:4 * S:S], mns, ["tabl%d%d%d" % (t, a, b)])
 
     def inverse_a(t):
         n = str(t)
-        ts(T.ia[:], T["ti" + n][:], 14, ALU.logical_shift_right, tab("l" + n), ["ia"])
-        cp(T.so[:, 0:A], T.ioj[:], ["ioj"], ["so"])
-        tt(T.f2[:], T.ia[:], T.slott[:], ALU.min, ["ia", "slott"], ["f2"])
-        cp(T.lu[:], T.f2[:], ["f2"], ["lu"])
+        tt(T.f2[:], T["ti" + n][:], T.slott[:], ALU.min, tab("l" + n) + ["slott"], ["f2"])
+        act(T.so[:, 0:A], T.ioj[:], ["ioj"], ["so"])
+        ts(T.lu[:], T.f2[:], 1.0 / Q, ALU.mult, ["f2"], ["lu"])
 
     def inverse_b(t, beside):
         n = str(t)
         cp(T.so[:, 0:160].indirect(T.lu[:, 0:8]), T.rowc[:], ["rowc", "lu"], ["so"])
-        beside[0]()
         tt(T.dn[:], T.so[:, 0:A], T.mm[:, 0:A], ALU.mult, ["so", "mm"], ["dn"])
-        beside[1]()
+        beside()
         for h in range(2):
             red(T.n2[:, h:h + 1], T.dn[:, 16 * h:16 * h + 16], ["dn"], ["n2%d" % h])
         cp(T["nu" + n][:], T.n2[:], ["n20", "n21"], ["nu" + n])
 
     def received(t):
         n = str(t)
-        xv = T["xr" + n][:, 0:4 * N:4]
         src = ["in_xr" + n, "xrown" + n]
-        ts(T.vi[:], xv, 63, ALU.bitwise_and, src, ["vi"])
         if t == 0:
-            tt(T.fl[:], xv, T.cc[:], ALU.add, src + ["cc"], ["fl"])
-        tt(T.vm[:], T.vi[:], T.blk[:], ALU.mult, ["vi", "blk"], ["vm"])
+            tt(T.fl[:, 0:k0], T.xr0[:, 0:4 * k0:4], T.cc[:, 0:k0], ALU.add, src + ["cc", "cc1"], ["fl"])
+        ts(T.vi[:], T.xr1[:, 0:8 * N:8] if t else T.xr0[:, 0:4 * N:4], 4.0, ALU.mult, src, ["vi"])
         if t == 0:
-            for a, b in runs:
-                lsk.append("lsu%d" % a)
-                ts(T.lsu[:, a:b], T.fl[:, a:b], 1.0 / 16384, ALU.mult, ["fl"], lsk[-1:], float(OWN + A - 1), ALU.min)
-        red(T.v[:], T.vm[:], ["vm"], ["v"])
-        ts(T.v4[:], T.vi[:], 4.0, ALU.mult, ["vi"], ["v4"])
-        ts(T.zl[:], T.ibq[:], T.v[:, 0:1], ALU.add, ["ibq", "v"], ["zl"], 4.0, ALU.mult)
+            ts(T.lsu[:, 0:k0], T.fl[:, 0:k0], 1.0 / Q, ALU.mult, ["fl"], ["lsu0"], float(OWN + A - 1), ALU.min)
+        ts(T.v4[:], T.vi[:], 255, ALU.bitwise_and, ["vi"], ["v4"])
         if t == 0:
-            pick("land0", 0, "lx0", OWN + A, T.lsu[:, 0:8], 128, ["in_lx0", "lx0own"] + lsk, "land0")
+            pick("land0", 0, "lx0", OWN + A, T.lsu[:, 0:8], 128, ["in_lx0", "lx0own", "lsu0", "lsu%d" % k0, "lsu%d" % (k0 + 1)], "land0")
+        cp(T.vm[:], T.v4[:, 0:8].indirect(T.gl[:, 0:1]), ["v4", "gl"], ["vm"])
+        ts(T.zl[:], T.ioj[:, 0:4], T.vm[:, 0:1], ALU.add, ["ioj", "vm"], ["zl"])
 
-    def goes(d):
-        return slice(CAPP * place(d), CAPP * place(d) + CAPP)
-
-    def serve(t, gaps):
+    def serve(t):
         n = str(t)
         land, nt, kp, xq, win = "land" + n, T["nt" + n], "kp" + n, "xq" + n, ("wina", "winb")[t]
         lk = ["land0_c", "land0_s"] if t == 0 else ["in_land1", "land1own_c", "land1own_s"]
@@ -369,156 +412,113 @@ def rank_program(g, core, T, topo):
         mx(5, 128, land, 0, "kq", 128, lk + ["kq"])
         for i in range(4):
             mx(1 + i, 128, "h", 128 * i, land, 0, lk + ["h%d" % i], True, False)
-        gaps[0]()
         act(T.zs[:, 0:128], bank(0, 128), ["bank0"], ["zs0"])
         cp(T.zs[:, 128:256], bank(5, 128), ["bank5"], ["zs1"])
         tt(T.zg[:], T.zs[:, 0:P].indirect(T.zl[:, 0:4]), T.dm[:], ALU.add, ["zs0", "zs1", "zl", "dm"], ["zg"])
-        scan(T.rm[:], T.zg[:], T.zg[:], -2e29, ALU.max, ALU.max, ["zg"], ["rm"])
-        for k in range(3):
-            ts(T.xb[:, k:4 * N:4], T.bki[:], T.rm[:, 16 * k + 15:16 * k + 16], ALU.add, ["bki", "rm", "xbz"], ["xb%d" % k], T.rm[:, 63:64], ALU.is_lt)
-        quant(xq, 0, 128, T.xb[:], ["xbz", "xb0", "xb1", "xb2"], [xq])
+        scan(T.rm[:, 8:72], T.zg[:], T.zg[:], -2e29, ALU.max, ALU.max, ["zg"], ["rm"])
+        ts(T.xb[:, 0:4 * N], T.rm[:, 0:64].indirect(T.xl[:, 0:2]), T.rm[:, 71:72], ALU.is_lt, ["xl", "rm", "rmz", "xbz"], ["xb"])
+        quant(xq, 0, 128, T.xb[:], ["xbz", "xb"], [xq])
         mx(6, 128, "ws", 0, xq, 0, ["ws", xq])
-        gaps[1]()
         tt(T.fl[:], bank(6, N), T.v4[:], ALU.add, ["bank6", "v4"], ["fl"])
         cp(T.ct[:], T.fl[:], ["fl"], ["ct"])
+        if t == 0:
+            act(T.yy[:], T.nxf[:, 0:P].indirect(T.ct[:, 0:8]), ["nxf", "ct"], ["yy"])
         pick(kp, 0, "kq", P, T.ct[:, 0:8], 128, ["kq", "ct"], kp)
         for i in range(4):
             mx(1 + i, 128, "h", 128 * i, kp, 0, [kp + "_c", kp + "_s", "h%d" % i], False, True)
-        rn, at = T["rn" + n], 128 * t
-        tt(T.yy[:], T.nxf[:, 0:P].indirect(T.ct[:, 0:8]), T.locrow[:], ALU.add, ["nxf", "ct", "locrow"], ["yy"])
-        turn(T.nodt[:, at:at + 128], T.yy[:], ["yy"], ["nodt" + n])
-        send("rn" + n, lambda d: T.nodt[:, at + 32 * (d // 2):at + 32 * (d // 2) + 1], lambda d: rn[:, 4 * rank:4 * rank + 1], ["nodt" + n])
+        rn, nodt = T["rn" + n], T["nodt" + n]
+        if t == 1:
+            cp(T.yy[:], T.nxf[:, 0:P].indirect(T.ct[:, 0:8]), ["nxf", "ct"], ["yy"])
+        turn(nodt[:], T.yy[:], ["yy"], ["nodt" + n])
+        send(["rn" + n], ["nodt" + n])
         for i in range(4):
-            if i % 2:
+            if (i != 2 if t else i % 2):
                 act(nt[:, i:512:4], bank(1 + i, 128), ["bank%d" % (1 + i)], ["nt%s%d" % (n, i)])
             else:
                 cp(nt[:, i:512:4], bank(1 + i, 128), ["bank%d" % (1 + i)], ["nt%s%d" % (n, i)])
         quant("new" + n, 0, 128, nt[:], ["nt%s%d" % (n, i) for i in range(4)], ["new" + n])
-
-        def back(d):
-            return A + CAPP * seen(d)
-
-        if t == 0:
-            send("hand1", lambda d: T.new0s[:, 0:128], lambda d: T.hand1[:, 0:128], ["new0"])
-        send("ret%s_c" % n, lambda d: codes("new" + n, CAPP * place(d), CAPP * place(d) + CAPP), lambda d: codes(win, back(d), back(d) + CAPP), ["new" + n])
-        if t == 1:
-            send("ret1_s", lambda d: T.new1s[:, goes(d)], lambda d: T.winbs[:, back(d):back(d) + CAPP], ["new1"])
-        cp(rn[:, 4 * rank:4 * rank + 1], T.nodt[:, at + 32 * (rank // 2):at + 32 * (rank // 2) + 1], ["nodt" + n, "rnz" + n], ["rnown" + n])
-        pick(win, back(rank), "new" + n, 128, T.ol[:, 0:1], CAPP, ["new" + n, "ol"], win + "own")
+        send(["ret1_c", "ret1_s"] if t else ["ret0", "ret0_c"], ["new" + n])
+        act(rn[:, 0:1], nodt[:, 0:1], ["nodt" + n, "rnz" + n], ["rnown" + n])
+        pick(win, A, "new" + n, 128, T.ol[:, 0:1], CAPP, ["new" + n, "ol"], win + "own")
 
     def home(t):
         n = str(t)
-        vv = T["vv" + n]
-        cp(T.mn[:, 0:128], T["rn" + n][:, 0:4 * N].indirect(T.elst[:, 0:8]), ["in_rn" + n, "rnown" + n, "rnz" + n, "elst"], mns)
-        turn(T.win[:, A:160], T.mn[:, 0:128], mns, ["winr"])
-        cp(vv[:], T.win[:, 0:160].indirect(T["nu" + n][:, 0:2]), ["winq", "winr", "nu" + n], ["vv" + n])
-        ts(T.dr[:], vv[:], 14, ALU.logical_shift_right, ["vv" + n], ["dr"])
-
-    def number(t):
-        n = str(t)
-        ts(T.dl[:], T["vv" + n][:], 63, ALU.bitwise_and, ["vv" + n], ["dl"])
-        ts(T.dn[:], T.dr[:], 64.0, ALU.mult, ["dr"], ["dn"])
-        tt(T.ndf[:, A * t:A * t + A], T.dn[:], T.dl[:], ALU.add, ["dl", "dn"], ["ndf" + n])
-
-    def nothing():
-        pass
+        src = ["in_rn" + n, "rnown" + n, "rnz" + n, "elst"]
+        cp(T.sp[:, 0:64], T["rn" + n][:, 0:4 * N].indirect(T.elst[:, 0:4]), src, ["sp0"])
+        act(T.sp[:, 64:128], T["rn" + n][:, 0:4 * N].indirect(T.elst[:, 4:8]), src, ["sp1"])
+        turn(T.win[:, A:160], T.sp[:], ["sp0", "sp1"], ["winr"])
 
     for h in range(2):
-        ts(T.dr[:, 16 * h:16 * h + 16], T.strb[:, h:A:2], 6, ALU.arith_shift_right, ["strb"], ["drh%d" % h])
+        ts(T.dr[:, 16 * h:16 * h + 16], T.strb[:, h:A:2], -31.5, ALU.add, ["strb"], ["drh%d" % h], 1.0 / 64, ALU.mult)
     for h in range(2):
-        ts(T.xm[:, 16 * h:16 * h + 16], T.strb[:, h:A:2], 63, ALU.bitwise_and, ["strb"], ["xmh%d" % h])
-    wrote["dr"], wrote["xm"] = wrote["drh1"], wrote["xmh1"]
-    lists(0, nothing)
-    for i, c in enumerate(picked):
-        k = place(cores.index(c))
-        ts(T.pl[:, i:i + 1], T.ti0[:, k:k + 1], 1.0 / 16384, ALU.mult, tab("l0"), ["pl%d" % i], float(A - 1), ALU.min)
-    pick("send0", 0, "qx", 128, T.pl[:, 0:2], 32, ["qx", "pl0", "pl1"], "send0")
-    slot = {cores.index(c): i * CAPP for i, c in enumerate(picked)}
-    send("pick_c", lambda d: codes("send0", slot[d], slot[d] + CAPP), lambda d: codes("lx0", A * seen(d), A * seen(d) + CAPP), ["send0_c"])
-    send("pick_s", lambda d: T.send0s[:, slot[d]:slot[d] + CAPP], lambda d: T.lx0s[:, A * seen(d):A * seen(d) + CAPP], ["send0_s"])
-    cp(T.xr0[:, 4 * me:4 * me + 1], T.ti0[:, me:me + 1], tab("l0"), ["xrown0"])
-    ts(T.nxh[0:32, :], T.nxt[0:32, :], 6, ALU.arith_shift_right, ["nxt"], ["nxh"])
-    ts(T.pd[:], T.iop[:], 4, ALU.arith_shift_right, ["iop"], ["pd"])
-    ts(T.nxp[0:32, :], T.nxh[0:32, :], float(16384 - 64), ALU.mult, ["nxh"], ["nxp"])
-    ts(T.cc[:], T.ioj[:, 0:N], float(A * 16384), ALU.mult, ["ioj"], ["cc"])
-    tt(T.nxp[0:32, :], T.nxp[0:32, :], T.nxt[0:32, :], ALU.add, ["nxp", "nxt"], ["nxp"])
-    tt(T.blk[:], T.pd[:], T.ioj[:, 0:N], ALU.is_equal, ["pd", "ioj"], ["blk"])
-    turn(T.nxq[0:32, :], T.nxp[0:32, :], ["nxp"], ["nxq"])
-    dma("s", "nxr", T.nx1[0:1, :], T.nxq[0:16, 0:16], ["nxq"], ["nx1"])
-    for k in range(3):
-        act(T.wb[:, k:512:4], T.mm[:], ["mm", "wb"], ["wb%d" % k])
-    fill(T.cc[:, me:me + 1], float(OWN * 16384), ["cc"])
-    fixed = sorted(place(s) for s, c in enumerate(cores) if c != core and core in plans[c][1])
-    lsk, runs, begin = [], [], 0
-    for k in fixed + [N]:
-        if k > begin:
-            runs.append((begin, k))
-        begin = k + 1
-    for k in fixed:
-        lsk.append("lsu%d" % k)
-        ts(T.lsu[:, k:k + 1], T.r1[:], float(A * k - 1), ALU.add, ["r1"], lsk[-1:])
-    ts(T.ibq[:], T.ioj[:, 0:4], 0.25, ALU.mult, ["ioj"], ["ibq"])
+        tt(T.xx[:, 16 * h:16 * h + 16], T.strb[:, h:A:2], T.xa[:, 16 * h:16 * h + 16], ALU.add, ["strb", "xa"], ["xxh%d" % h])
+    wrote["dr"], wrote["xx"] = wrote["drh1"], wrote["xxh1"]
+    lists(0)
+    table(0)
+    send(["xr0"], tab("l0") + ["rnz0", "rnz1"])
+    pick("send0", 0, "qx", 128, T.sl[:, k0:k0 + 2], 32, ["qx", "sl0", "sl1"], "send0")
+    send(["pick_c"], ["send0_c"])
+    send(["pick_s"], ["send0_s"])
+    act(T.xr0[:, 0:1], T.ti0[:, 0:1], tab("l0"), ["xrown0"])
+    cp(T.nxp[:], T.nxt[:], ["nxt7"], ["nxp"])
+    ts(T.nl[:], T.el[:], T.ec[:, 0:1], ALU.add, ["el", "ec"], ["nl"])
+    act(T.nx1[:], T.nxp[:, 0:16].indirect(T.nl[:, 0:16]), ["nxp", "nl"], ["nx1"])
+    scaled(T.cc[:, 1:N], T.ioj[:, 1:N], float(A * Q), 0.0, ["ioj"], ["cc1"])
+    scaled(T.cc[:, 0:1], T.ioj[:, 0:1], 0.0, float(OWN * Q), ["ioj"], ["cc"])
+    zero(T.xb[:, 4 * N:512], T.kt[:, 4 * N:512], ["kt"], ["xbz"])
+    scaled(T.rm[:, 0:8], T.mm[:, 0:8], 0.0, 5e29, ["mm"], ["rmz"])
+    scaled(T.dm[:], T.mm[:, 0:64], 1e29, -1e29, ["mm"], ["dm"])
+    for k in (k0, k0 + 1):
+        ts(T.lsu[:, k:k + 1], T.r1[:, 0:1], float(A * k - 1), ALU.add, ["r1"], ["lsu%d" % k])
     quant("lx0", OWN, OWN + 128, T.xt[:], ["xt", "xtz"], ["lx0own"])
     quant("kq", 0, P, T.kt[:], ["kt"], ["kq"])
     for i in range(4):
         quant("h", 128 * i, 128 * i + 128, T.hb[:, 3 - i:515 - i], ["hb"], ["h%d" % i])
-    ts(T.bki[:], T.blk[:], -1.0, ALU.add, ["blk"], ["bki"], -1e29, ALU.mult)
-    ts(T.dm[:], T.mm[:, 0:64], -1.0, ALU.add, ["mm"], ["dm"], 1e29, ALU.mult)
+    tt(T.f3[:, 0:2], T.pd[:, 0:2], T.ib[:, 0:2], ALU.subtract, ["pd", "ib"], ["f3"])
+    cp(T.gl[:, 0:1], T.pd[:, 0:1], ["pd"], ["gl"])
+    tt(T.f3[:, 0:2], T.f3[:, 0:2], T.ioj[:, 0:8:4], ALU.is_equal, ["f3", "ioj"], ["f3"])
     quant("ws", 0, 128, T.wb[:], ["wb", "wb0", "wb1", "wb2"], ["ws"])
+    ts(T.xl[:], T.f3[:, 0:2], T.v[:, 0:1], ALU.mult, ["f3", "v"], ["xl"], 63.0, ALU.min)
     iota(T.io16[:], [[16, 8]], A - 1, 0, ["io16"])
-    iota(T.el[:], [[8, 4], [0, 2]], 0, 0, ["el"])
-    iota(T.xa1[:], [[16384, A]], 0, 0, ["xa1"], True)
-    op("g", lambda e: e.partition_broadcast(T.nxf[:], T.nx1[0:1, :], 128), ["nx1"], ["nxf"])
-    iota(T.locrow[:], [[0, 4], [64, 32]], 64 * (A + 32 * (rank // 2)), 0, ["locrow"], True)
     iota(T.rowc[:], [[1, 128]], A, 0, ["rowc"], True)
-    ts(T.ol[:, 0:1], T.r1[:], float(mine - 1), ALU.add, ["r1"], ["ol"])
-    ts(T.slott[:], T.io16[:], T.r1[:, 0:1], ALU.add, ["io16", "r1"], ["slott"])
+    turn(T.nxf[:], T.nx1[:], ["nx1"], ["nxf"])
+    ts(T.slott[:], T.io16[:], T.r1[:, 0:1], ALU.add, ["io16", "r1"], ["slott"], float(Q), ALU.mult)
+    ts(T.elst[:], T.el[:, 0:8], T.ec[:, 0:1], ALU.add, ["el", "ec"], ["elst"], 4.0, ALU.mult)
+    tt(T.win[:, 0:A], T.xx[:, 0:A], T.xa[:], ALU.subtract, ["xx", "xa"], ["winq"])
+    inverse_a(0)
     received(0)
-
-    def first_nodes():
-        ts(T.win[:, 0:A], T.dr[:], 16384.0, ALU.mult, ["dr"], ["winq"])
-        ts(T.ib[:], T.pd[:], 1, ALU.bitwise_and, ["pd"], ["ib"])
-        tt(T.win[:, 0:A], T.win[:, 0:A], T.xx[:, 0:A], ALU.add, ["winq", "xx"], ["winq"])
-        ts(T.f3[:], T.ib[:], -4.0 if odd else 4.0, ALU.mult, ["ib"], ["f3"], 4.0 * odd, ALU.add)
-
-    def more_nodes():
-        tt(T.win[:, 0:A], T.win[:, 0:A], T.xa1[:], ALU.subtract, ["winq", "xa1"], ["winq"])
-        tt(T.f3[:], T.f3[:], T.el[:], ALU.add, ["f3", "el"], ["f3"])
-
+    cp(T.ol[:, 0:1], T.ia[:, 0:1], ["ia"], ["ol"])
     dma("s", "w", T.wt[:], T.w[:], ["land0_c"], ["wt"])
     dma("s", "ownw", codes("wina", 0, A), codes("qx", 0, A), ["qx"], ["winaq"])
     dma("s", "ownw", T.winas[:, 0:A], T.qxs[:, 0:A], ["qx"], ["winaq2"])
-    serve(0, [lambda: inverse_a(0), first_nodes])
-    inverse_b(0, [more_nodes, lambda: cp(T.elst[:], T.f3[:], ["f3"], ["elst"])])
+    dma("s", "nd0", T.nd[0:1, :], T.win[0:1, 0:A], ["winq"], [])
+    serve(0)
+    inverse_b(0, lambda: None)
     home(0)
-    lists(1, lambda: ts(T.xm[:], T.vv0[:], 16383, ALU.bitwise_and, ["vv0"], ["xm"]))
-    ts(T.shx[:], T.ti1[:], 6, ALU.logical_shift_right, tab("l1"), ["shx"], 255, ALU.bitwise_and)
-    cp(T.xr1[:, 4 * me:4 * me + 1], T.ti1[:, me:me + 1], tab("l1"), ["xrown1"])
-    cp(T.sl[:], T.shx[:], ["shx"], ["sl"])
-    wina = ["winaq", "winaq2", "winaown_c", "winaown_s", "in_ret0"]
-    pick("send1", 0, "wina", 160, T.sl[:, 0:8], 128, wina + ["sl"], "send1")
-    send("land1_c", lambda d: codes("send1", CAPP * place(d), CAPP * place(d) + CAPP),
-         lambda d: codes("land1", CAPP * seen(d), CAPP * seen(d) + CAPP), ["send1_c"])
-    send("land1_s", lambda d: T.send1s[:, goes(d)], lambda d: T.land1s[:, CAPP * seen(d):CAPP * seen(d) + CAPP], ["send1_s"])
-    pick("land1", mine, "send1", 128, T.ol[:, 0:1], CAPP, ["send1_c", "send1_s", "ol"], "land1own")
+    ts(T.dr[:], T.win[:, 0:160].indirect(T.nu0[:, 0:2]), -31.5, ALU.add, ["winq", "winr", "nu0"], ["dr"], 1.0 / 64, ALU.mult)
+    tt(T.xx[:, 0:A], T.win[:, 0:160].indirect(T.nu0[:, 0:2]), T.xa[:], ALU.add, ["winq", "winr", "nu0", "xa"], ["xx"])
+    lists(1)
+    send(["xr1"], tab("x"))
+    wina_c, wina_s = ["winaq2", "winaown_c", "in_ret0"], ["winaq2", "winaown_s", "in_ret0s"]
+    pick("q1", 0, "wina", 160, T.nu0[:, 0:2], A, ["nu0"], "q1", wina_c, wina_s)
+    ts(T.sl[:], T.tx[:], 1.0 / Q, ALU.mult, tab("x"), ["sl0", "sl1"], float(A - 1), ALU.min)
+    pick("send1", 0, "q1", A, T.sl[:, 0:8], 128, ["sl0"], "send1", ["q1_c"], ["q1_s"])
+    send(["land1_c"], ["send1_c"])
+    send(["land1_s"], ["send1_s"])
+    pick("land1", 0, "send1", 128, T.ol[:, 0:1], CAPP, ["ol"], "land1own", ["send1_c"], ["send1_s"])
+    table(1)
+    cp(T.xr1[:, 0:1], T.tx[:, 0:1], tab("x"), ["xrown1"])
+    tt(T.win[:, 0:A], T.xx[:, 0:A], T.xa[:], ALU.subtract, ["xx", "xa"], ["winq"])
+    dma("s", "nd1", T.nd[1:2, :], T.win[0:1, 0:A], ["winq"], [])
     inverse_a(1)
-    inverse_b(1, [lambda: cp(T.win[:, 0:A], T.vv0[:], ["vv0"], ["winq"]),
-                  lambda: pick("winb", 0, "wina", 160, T.nu0[:, 0:2], A, wina + ["nu0"], "winbq")])
+    inverse_b(1, lambda: pick("winb", 0, "wina", 160, T.nu0[:, 0:2], A, ["nu0"], "winbq", wina_c, wina_s))
     received(1)
-
-    def last_tiles():
-        quant("wq", 0, 128, T.wt[:], ["wt"], ["wq"])
-        quant("fin", 0, 128, T.xt[:], ["xt", "xtz"], ["fin_c", "fin_s"])
-
-    serve(1, [last_tiles, nothing])
-    for h in range(2):
-        cp(T.nd0f[:, 16 * h:16 * h + 16], T.strb[:, h:A:2], ["strb"], ["nd0f%d" % h])
-    number(0)
-    dma("s", "nd0", T.nd[0:1, :], T.nd0f[0:1, :], ["nd0f0", "nd0f1"], [])
-    dma("s", "nd1", T.nd[1:2, :], T.ndf[0:1, 0:A], ["ndf0"], [])
+    serve(1)
+    quant("wq", 0, 128, T.wt[:], ["wt"], ["wq"])
+    quant("fin", 0, 128, T.xt[:], ["xt", "xtz"], ["fin_c", "fin_s"])
     home(1)
-    number(1)
-    dma("s", "nd2", T.nd[2:3, :], T.ndf[0:1, A:2 * A], ["ndf1"], [])
+    cp(T.stw[:], T.win[:, 0:160].indirect(T.nu1[:, 0:2]), ["winq", "winr", "nu1"], ["stw"])
+    dma("s", "nd2", T.nd[2:3, :], T.stw[0:1, :], ["stw"], [])
     pick("fin", 0, "winb", 160, T.nu1[:, 0:2], A, ["winbq_c", "winbq_s", "winbown_c", "winbown_s", "in_ret1", "nu1"], "fin")
     mx(7, 128, "wq", 0, "fin", 0, ["wq", "fin_c", "fin_s"])
     cp(T.ys[:], bank(7, A), ["bank7"], ["ys"])

@@ -11,16 +11,15 @@ KINDS = ["near", "plane", "diag", "mate"]
 
 MSG = {"wide_c": ("qxc", "lx0c", "lx0", A), "wide_s": ("qxs", "lx0s", "lx0", A), "pick_c": ("send0c", "lx0c", "lx0", CAPP),
        "pick_s": ("send0s", "lx0s", "lx0", CAPP), "xr0": ("ti0", "xr0", "xr0", 1), "xr1": ("tx", "xr1", "xr1", 1),
-       "rn0": ("nodt0", "rn0", "rn0", 1), "rn1": ("nodt1", "rn1", "rn1", 1),
+       "rn0": ("rn0", "rn0", "rn0", 1), "rn1": ("rn1", "rn1", "rn1", 1),
        "ret0_c": ("new0c", "winac", "ret0", CAPP), "ret0_s": ("new0s", "winas", "ret0s", CAPP),
        "land1_c": ("send1c", "land1c", "land1", CAPP), "land1_s": ("send1s", "land1s", "land1", CAPP),
        "ret1_c": ("new1c", "winbc", "ret1", CAPP), "ret1_s": ("new1s", "winbs", "ret1", CAPP)}
-VIA = {"wide_s": {"diag": "F", "plane": "B"},
-       "ret0_s": {"diag": "F", "mate": "F", "plane": "B", "near": "B"},
-       "xr1": {"diag": "F", "mate": "F", "plane": "B", "near": "B"}}
-CALLS = {"wide": (["wide_c"], 4), "wide2": (["wide_s", "+wide_s"], 2), "xr0": (["xr0"], 4), "pick_c": (["pick_c"], 2), "pick_s": (["pick_s"], 4),
-         "rn0": (["rn0"], 4), "ret0": (["+ret0_s"], 4), "ret0_c": (["ret0_c"], 4),
-         "xr1": (["+xr1"], 4), "land1_c": (["land1_c"], 4), "land1_s": (["land1_s"], 4),
+SAME = ("wide_c", "wide_s", "rn0", "rn1")
+VIA = {"wide_s": ("diag",), "xr1": ("diag", "mate")}
+CALLS = {"wide": (["wide_c"], 4), "wide2": (["wide_s", "+wide_s"], 4), "xr0": (["xr0"], 4), "pick_c": (["pick_c"], 2), "pick_s": (["pick_s"], 4),
+         "rn0": (["rn0"], 4), "ret0_c": (["ret0_c"], 4), "ret0_s": (["ret0_s"], 4),
+         "xr1h": (["+xr1"], 8), "xr1": (["xr1"], 4), "land1_c": (["land1_c"], 4), "land1_s": (["land1_s"], 4),
          "rn1": (["rn1"], 4), "ret1_c": (["ret1_c"], 4), "ret1_s": (["ret1_s"], 4)}
 SCRATCH = {}
 
@@ -31,26 +30,28 @@ def _add(name, cols, dtype, where="sbuf"):
 
 for _n, _c in (("qx", 128), ("lx0", OWN + 128), ("send0", 32), ("land0", 128), ("new0", 128), ("wina", 160), ("q1", 32), ("send1", 128),
                ("land1", 128), ("new1", 128), ("winb", 160), ("fin", 128), ("kq", 256), ("wq", 128), ("h", 512), ("ws", 128),
-               ("kp0", 128), ("kp1", 128), ("xq0", 128), ("xq1", 128)):
+               ("xq0", 128), ("xq1", 128)):
     _add(_n + "c", _c, F8)
     _add(_n + "s", _c, U8)
 for _n, _c, _d in (("xt", 512, BF), ("kt", 1024, BF), ("wt", 512, BF), ("hb", 516, BF), ("wb", 512, BF), ("xb", 512, BF),
                    ("iop", 8, I32), ("ioj", 32, F32), ("jmp", 128, I32), ("jmq", 128, I32), ("xa", 32, F32),
-                   ("el", 16, I32), ("elst", 8, U16), ("rowc", 128, F32), ("io16", 8, I32), ("slott", 8, F32),
-                   ("pd", 8, I32), ("mm", 128, F32), ("dm", 64, F32), ("xl", 2, U16),
+                   ("el", 16, I32), ("rowc", 128, F32), ("io16", 8, F32), ("slott", 8, F32),
+                   ("ia", 8, I32), ("cu", 8, U16), ("pm", 2, U16), ("rq1", 1, F32),
+                   ("mm", 128, F32), ("dm", 64, F32), ("xl", 2, U16), ("rq", 64, F32),
                    ("r1", 4, F32), ("ec", 1, F32), ("dcol", 4, F32), ("rst", 4 * S, BF),
                    ("cc", 8, F32), ("stc", 1, I32), ("stw", 32, F32), ("strb", 32, F32),
-                   ("nxt", 16, I32), ("gl", 2, U16), ("nxp", 16, F32), ("nl", 16, U16), ("nx1", 256, F32), ("nxf", 256, F32),
-                   ("lsu", 8, U16), ("sl", 8, U16), ("ol", 2, U16), ("ys", 32, F32), ("ib", 8, I32), ("f3", 8, F32),
-                   ("xr0", 4 * N, F32), ("tx", N, U16), ("xr1", 8 * N, U16),
+                   ("nxt", 16, I32), ("nxp", 16, F32), ("nl", 16, U16), ("nx1", 256, F32), ("nxf", 256, F32),
+                   ("lsu", 8, U16), ("sl", 8, U16), ("ys", 32, F32), ("ib", 8, I32), ("f3", 8, F32),
+                   ("ti0", N, F32), ("xr0", 4 * N, F32), ("ti1", N, F32), ("tx", 4, U16), ("xr1", 8 * N, U16), ("dk", 4 * P, F32),
                    ("dr", 32, I32), ("xx", S + 1, F32), ("zl", 4, U16), ("ct", 8, U16),
                    ("win", 160, F32), ("lu", 8, U16), ("so", 160, F32), ("dn", 32, F32),
                    ("vi", 8, I32), ("v4", 8, I32), ("vm", 16, F32), ("v", 1, F32), ("zs", 256, F32), ("zg", 64, F32), ("rm", 72, F32),
-                   ("eqb", 4 * S, BF), ("cum", 4 * S + 2, BF), ("yy", 128, F32), ("mn", 4 * S, F32), ("sp", 128, F32),
-                   ("ia", 8, I32), ("fl", 8, F32), ("f2", 8, F32), ("n2", 2, F32)):
+                   ("ng", 64, F32), ("nq", 88, F32), ("nd4", 4, F32), ("bb", 4, F32), ("sp", 64, F32), ("sq", 64, F32),
+                   ("dq", 256, F32), ("dg", 256, F32), ("eqb", 4 * S, BF), ("cum", 4 * S + 2, BF), ("mn", 4 * S, F32),
+                   ("fl", 8, F32), ("f2", 8, F32), ("n2", 2, F32)):
     _add(_n, _c, _d)
 for _t in ("0", "1"):
-    for _n, _c, _d in (("ti", 8, F32), ("nt", 512, BF), ("rn", 32, F32), ("nu", 2, U16), ("nodt", 128, F32)):
+    for _n, _c, _d in (("nt", 512, BF), ("rn", 40, F32), ("nu", 2, U16)):
         _add(_n + _t, _c, _d)
 for _n in VIA:
     _add("h" + _n, 4 * MSG[_n][3], SCRATCH[MSG[_n][0]][2])
@@ -79,11 +80,9 @@ def _plan(topo, T, cores, rank):
     me = cores[rank]
     kind, place = _places(topo, cores, rank)
     others = [r for r in range(N) if r != rank]
-    spare = [c for c in topo.cores_of(me) if c not in cores and topo.die(c) == topo.die(me)]
-    full = [c for c in spare if all(topo.may_write(c, d) for d in cores)][0]
-    helper = {"F": full, "B": [c for c in spare if c != full][0]}
+    helper = [c for c in topo.cores_of(me) if c not in cores and topo.die(c) == topo.die(me) and all(topo.may_write(c, d) for d in cores)][0]
     port = topo.engines(me, cores[kind.index("mate")])
-    inner = [e for e in topo.engines(me, full) if e not in port]
+    inner = [e for e in topo.engines(me, helper) if e not in port]
 
     def ends(m, r):
         k = place[r]
@@ -92,9 +91,9 @@ def _plan(topo, T, cores, rank):
         if m[:4] == "pick":
             return CAPP * (k % 2), A * k
         if m[:2] == "xr":
-            return k, SCRATCH[m][1][1] // N * k
+            return k % SCRATCH[MSG[m][0]][1][1], SCRATCH[m][1][1] // N * k
         if m[:2] == "rn":
-            return 32 * (k // 2), 4 * k
+            return 8, 4 * k + 8
         return CAPP * k, CAPP * k + (0 if m[:4] == "land" else A)
 
     def dests(m):
@@ -103,19 +102,22 @@ def _plan(topo, T, cores, rank):
     load = {}
     turn = [0]
 
-    def deal(core, items, cap):
-        off = [i for i in items if i[0] not in topo.cores_of(core) or core != me]
-        on = [i for i in items if i[0] in topo.cores_of(core) and core == me]
+    def deal(core, items, cap, same):
+        off = [i for i in items if i[0] not in topo.cores_of(core)]
+        on = [i for i in items if i[0] in topo.cores_of(core)]
         if off and len(port) % len(off):
             k = turn[0] % len(off)
             turn[0] += 2
             off = off[k:] + off[:k]
         out = []
         for group, pool in ((off, port), (on[::-1], inner)):
+            if same and pool is port:
+                out += [(c, sum(1 << e for e in port), sem, src, dst) for c, sem, src, dst in group]
+                continue
             free = sorted(pool, key=lambda e: load.get((core, e), 0))
             for i, (c, sem, src, dst) in enumerate(group):
                 rest = len(group) - i
-                most = min(cap, len(free) // rest if pool is port else len(free) - 2 * (rest - 1))
+                most = min(cap, len(free) // rest)
                 take = 1
                 while 2 * take <= most:
                     take *= 2
@@ -128,37 +130,36 @@ def _plan(topo, T, cores, rank):
     plan = {}
     for name, (parts, cap) in CALLS.items():
         items = []
-        if name[:2] == "rn":
+        if name == "rn0":
             for e in port:
                 load[me, e] = 0
         for m in parts:
             if m[0] != "+":
                 src, dst, sem, n = MSG[m]
                 for r in dests(m):
-                    if kind[r] not in VIA.get(m, {}):
+                    if kind[r] not in VIA.get(m, ()):
                         a, b = ends(m, r)
                         items.append((cores[r], sem, _view(T, src, a, n), _view(T, dst, b, n)))
                 continue
             m = m[1:]
             src, dst, sem, n = MSG[m]
-            w = A if m == "wide_s" else 4 * n
-            for h in sorted(set(VIA[m].values())):
-                mine = [r for r in dests(m) if VIA[m].get(kind[r]) == h]
-                lo = min(ends(m, r)[0] for r in mine) // w * w
-                items.append((helper[h], "h" + m, _view(T, src, lo, w), _view(T, "h" + m, 0, w)))
-                on = [(cores[r], sem, _view(T, "h" + m, ends(m, r)[0] - lo, n), _view(T, dst, ends(m, r)[1], n)) for r in mine]
-                plan[helper[h], m] = deal(helper[h], on, 4)
-        plan[me, name] = deal(me, items, cap)
+            w = n if m in SAME else 4 * n
+            items.append((helper, "h" + m, _view(T, src, 0, w), _view(T, "h" + m, 0, w)))
+            on = [(cores[r], sem, _view(T, "h" + m, ends(m, r)[0], n), _view(T, dst, ends(m, r)[1], n)) for r in dests(m) if kind[r] in VIA[m]]
+            plan[helper, m] = deal(helper, on, 4, m in SAME)
+        plan[me, name] = deal(me, items, cap, parts[0] in SAME)
     return plan
 
 
 def _fused(g, T, topo, core, call):
     tr = []
-    for c, m, sem, src, dst in call:
-        rid, pid = topo.addr(c, core)
-        tr.append(RemoteDMATransfer(dst_ids=[DstId(rid=rid, pnc=pid)], dma_engine_mask=m, remote_sem=T.sem["a_" + sem], src=src, dst=dst))
+    masks = sorted(set(t[1] for t in call))
+    for m in masks:
+        same = [t for t in call if t[1] == m]
+        ids = [DstId(rid=topo.addr(t[0], core)[0], pnc=topo.addr(t[0], core)[1]) for t in same]
+        tr.append(RemoteDMATransfer(dst_ids=ids, dma_engine_mask=m, remote_sem=T.sem["a_" + same[0][2]], srcs=[same[0][3]], dsts=[t[4] for t in same]))
     g.remote_dma_fused(tr, local_sem=T.sem.left)
-    return sum(_bits(t[1]) for t in call)
+    return sum(_bits(m) for m in masks)
 
 
 def rank_program(g, core, T, topo):
@@ -287,9 +288,9 @@ def rank_program(g, core, T, topo):
         else:
             op("g", lambda e: e.iota(out, pattern, base, step), [], writes)
 
-    def mx(bank, n, l, la, r, ra, reads, start=True, stop=True):
+    def mx(bank, n, l, la, r, ra, reads):
         op("p", lambda e: e.matmul_mx(T.bank[:, 512 * bank:512 * bank + n], T[l + "c"][:, la:la + 128], T[l + "s"][:, la:la + 128],
-                                      T[r + "c"][:, ra:ra + n], T[r + "s"][:, ra:ra + n], start, stop), reads, ["bank%d" % bank])
+                                      T[r + "c"][:, ra:ra + n], T[r + "s"][:, ra:ra + n], True, True), reads, ["bank%d" % bank])
 
     def bank(k, n):
         return T.bank[:, 512 * k:512 * k + n]
@@ -316,9 +317,10 @@ def rank_program(g, core, T, topo):
     iota(T.iop[:], [[0, 8]], 0, 1, ["iop"])
     iota(T.jmp[:], [[1, 128]], 0, -1, ["jmp"])
     iota(T.dcol[:], [[at[2] - at[0], 2], [at[1] - at[0], 2]], at[0], 0, ["dcol"], True)
-    iota(T.xa[:], [[Q, A]], 0, 0, ["xa"], True)
     iota(T.ioj[:], [[1, A]], 0, 0, ["ioj"], True)
+    iota(T.xa[:], [[Q, A]], 0, 0, ["xa"], True)
     iota(T.el[:], [[2, 8], [0, 2]], 0, 0, ["el"])
+    iota(T.io16[:], [[16, 8]], A - 1, 0, ["io16"], True)
     fill(T.hb[:], 0.0, ["hb"])
     zero(T.xt[:, 4 * A:512], T.hb[:, 4 * A:512], ["hb"], ["xtz"])
     for j in (0, 2):
@@ -327,21 +329,24 @@ def rank_program(g, core, T, topo):
     fill(T.nu1[:], 0, ["nu1"])
     fill(T.xx[:, A:S], float(EMPTY), ["xxz"])
     fill(T.rst[:, A:4 * S:S], 0.0, ["rst"])
-    ts(T.ia[:], T.iop[:], 15, ALU.bitwise_and, ["iop"], ["ia"])
-    ts(T.pd[:], T.iop[:], 4, ALU.arith_shift_right, ["iop"], ["pd"])
+    ts(T.ia[:, 0:4], T.iop[:, 0:4], 15, ALU.bitwise_and, ["iop"], ["ia"])
+    ts(T.ia[:, 4:6], T.iop[:, 0:2], 4, ALU.arith_shift_right, ["iop"], ["pd"])
+    ts(T.ia[:, 6:8], T.iop[:, 0:2], 2, ALU.arith_shift_right, ["iop"], ["pe"], 28, ALU.bitwise_and)
     ts(T.jmq[:], T.jmp[:], 15, ALU.bitwise_and, ["jmp"], ["jmq"])
     ts(T.r1[:], T.ia[:, 0:4], 1.0, ALU.add, ["ia"], ["r1"])
     scaled(T.cum[:, 0:1], T.r1[:, 0:1], float(2 * EMPTY), 0.0, ["r1"], ["cumz"])
     scaled(T.eqb[:, A:4 * S:S], T.r1[:], float(2 * EMPTY), 0.0, ["r1"], ["eqz"])
+    scaled(T.n2[:, 0:1], T.r1[:, 0:1], 2.0, -2.0, ["r1"], ["n20"])
     ts(T.mm[:], T.jmq[:], 0.0, ALU.is_equal, ["jmq"], ["mm"])
     ts(T.ib[:, 0:2], T.iop[:, 0:2], 2, ALU.arith_shift_right, ["iop"], ["ib"], 3, ALU.bitwise_and)
     ts(T.vi[:, 0:1], T.iop[:, 0:1], 3, ALU.bitwise_and, ["iop"], ["vi"])
     ts(T.v4[:, 0:1], T.iop[:, 0:1], 4, ALU.arith_shift_right, ["iop"], ["v4"], 1, ALU.bitwise_and)
     ts(T.hb[:, 3:515:4], T.jmp[:], 0.0, ALU.is_equal, ["jmp"], ["hb"], 0.5, ALU.mult)
     cp(T.ec[:], T.v4[:, 0:1], ["v4"], ["ec"])
+    ts(T.pm[:], T.ioj[:, 0:2], T.n2[:, 0:1], ALU.add, ["ioj", "n20"], ["pm"])
     ts(T.v[:], T.vi[:, 0:1], 16.0, ALU.mult, ["vi"], ["v"], 23.0, ALU.add)
-    zero(T.rn0[:], T.mm[:, 0:32], ["mm"], ["rnz0"])
-    zero(T.rn1[:], T.mm[:, 0:32], ["mm"], ["rnz1"])
+    zero(T.rn0[:], T.mm[:, 0:40], ["mm"], ["rnz0"])
+    zero(T.rn1[:], T.mm[:, 0:40], ["mm"], ["rnz1"])
     zero(T.wb[:, 3:512:4], T.mm[:], ["mm"], ["wb"])
     for k in range(3):
         act(T.wb[:, k:512:4], T.mm[:], ["mm", "wb"], ["wb%d" % k])
@@ -356,39 +361,41 @@ def rank_program(g, core, T, topo):
     mns = ["mn%d" % q for q in range(4)]
     k0 = 2 * KINDS.index("mate")
 
-    def lists(t):
+    def lists():
         for q in range(4):
             ts(T.eqb[:, S * q:S * q + A], T.dr[:], T.dcol[:, q:q + 1], ALU.is_equal, ["dr", "dcol2"], ["eqb%d" % q], -2.0 * EMPTY, ALU.mult)
         scan(T.cum[:, 1:4 * S + 1], T.rst[:], T.eqb[:], T.cum[:, 0:1], ALU.mult, ALU.add, ["rst", "eqz", "cumz"] + ["eqb%d" % q for q in range(4)], ["cum"])
         for q in range(4):
             scan(T.mn[:, S * q:S * q + S], T.cum[:, S * q:S * q + S], T.xx[:, 0:S], 0.0, ALU.max, ALU.min, ["cum", "cumz", "xx", "xxz"], [mns[q]])
-        for a in range(2):
-            for b in range(2):
-                if t:
-                    cp(T.tx[64 * b:64 * b + 64, 4 * a:4 * a + 4], T.mn[64 * a:64 * a + 64, A:4 * S:S], mns, ["tabx%d%d" % (a, b)])
-                elif a == k0 // 4:
-                    ts(T.sl[64 * b:64 * b + 64, k0:k0 + 2], T.mn[64 * a:64 * a + 64, S * (k0 % 4) + A:S * (k0 % 4 + 2):S], 1.0 / Q, ALU.mult, mns,
-                       ["sl%d" % b], float(A - 1), ALU.min)
 
     def table(t):
         for a in range(2):
             for b in range(2):
                 act(T["ti%d" % t][64 * b:64 * b + 64, 4 * a:4 * a + 4], T.mn[64 * a:64 * a + 64, A:4 * S:S], mns, ["tabl%d%d%d" % (t, a, b)])
 
-    def inverse_a(t):
-        n = str(t)
-        tt(T.f2[:], T["ti" + n][:], T.slott[:], ALU.min, tab("l" + n) + ["slott"], ["f2"])
-        act(T.so[:, 0:A], T.ioj[:], ["ioj"], ["so"])
-        ts(T.lu[:], T.f2[:], 1.0 / Q, ALU.mult, ["f2"], ["lu"])
+    def queries(lo, hi):
+        a = lo // 4
+        for b in range(2):
+            ts(T.sl[64 * b:64 * b + 64, lo:hi], T.mn[64 * a:64 * a + 64, S * (lo % 4) + A:S * (hi - 4 * a):S], 1.0 / Q, ALU.mult, mns,
+               ["sl%d%d" % (a, b)], float(A - 1), ALU.min)
 
-    def inverse_b(t, beside):
-        n = str(t)
+    def inverse(t, first, second):
+        tt(T.f2[:], T["ti%d" % t][:], T.slott[:], ALU.min, tab("l%d" % t) + ["slott"], ["f2"])
+        act(T.so[:, 0:A], T.ioj[:], ["ioj"], ["so"])
+        first()
+        ts(T.lu[:], T.f2[:], 1.0 / Q, ALU.mult, ["f2"], ["lu"])
+        second()
         cp(T.so[:, 0:160].indirect(T.lu[:, 0:8]), T.rowc[:], ["rowc", "lu"], ["so"])
+
+    def listed_a():
         tt(T.dn[:], T.so[:, 0:A], T.mm[:, 0:A], ALU.mult, ["so", "mm"], ["dn"])
-        beside()
+
+    def listed_b():
         for h in range(2):
             red(T.n2[:, h:h + 1], T.dn[:, 16 * h:16 * h + 16], ["dn"], ["n2%d" % h])
-        cp(T["nu" + n][:], T.n2[:], ["n20", "n21"], ["nu" + n])
+
+    def listed_c(t):
+        cp(T["nu%d" % t][:], T.n2[:], ["n20", "n21"], ["nu%d" % t])
 
     def received(t):
         n = str(t)
@@ -400,124 +407,163 @@ def rank_program(g, core, T, topo):
             ts(T.lsu[:, 0:k0], T.fl[:, 0:k0], 1.0 / Q, ALU.mult, ["fl"], ["lsu0"], float(OWN + A - 1), ALU.min)
         ts(T.v4[:], T.vi[:], 255, ALU.bitwise_and, ["vi"], ["v4"])
         if t == 0:
-            pick("land0", 0, "lx0", OWN + A, T.lsu[:, 0:8], 128, ["in_lx0", "lx0own", "lsu0", "lsu%d" % k0, "lsu%d" % (k0 + 1)], "land0")
-        cp(T.vm[:], T.v4[:, 0:8].indirect(T.gl[:, 0:1]), ["v4", "gl"], ["vm"])
+            pick("land0", 0, "lx0", OWN + A, T.lsu[:, 0:8], 128, ["in_lx0", "lx0own", "lsu0", "lsu1"], "land0")
+        cp(T.vm[:], T.v4[:, 0:8].indirect(T.cu[:, 4:5]), ["v4", "cu"], ["vm"])
         ts(T.zl[:], T.ioj[:, 0:4], T.vm[:, 0:1], ALU.add, ["ioj", "vm"], ["zl"])
+
+    def keys(i):
+        act(T.dk[:, P * i:P * i + P], bank(6 + i % 2, P), ["bank%d" % (6 + i % 2)], ["dk%d" % i])
 
     def serve(t):
         n = str(t)
-        land, nt, kp, xq, win = "land" + n, T["nt" + n], "kp" + n, "xq" + n, ("wina", "winb")[t]
+        land, nt, xq, win = "land" + n, T["nt" + n], "xq" + n, ("wina", "winb")[t]
         lk = ["land0_c", "land0_s"] if t == 0 else ["in_land1", "land1own_c", "land1own_s"]
         mx(0, 128, land, 0, "kq", 0, lk + ["kq"])
         mx(5, 128, land, 0, "kq", 128, lk + ["kq"])
         for i in range(4):
-            mx(1 + i, 128, "h", 128 * i, land, 0, lk + ["h%d" % i], True, False)
+            mx(1 + i, 128, "h", 128 * i, land, 0, lk + ["h%d" % i])
         act(T.zs[:, 0:128], bank(0, 128), ["bank0"], ["zs0"])
-        cp(T.zs[:, 128:256], bank(5, 128), ["bank5"], ["zs1"])
+        (act if t else cp)(T.zs[:, 128:256], bank(5, 128), ["bank5"], ["zs1"])
+        if t == 0:
+            keys(2)
+            keys(3)
+        for i in range(2):
+            act(T.dq[:, 128 * i:128 * i + 128], bank(1 + i, 128), ["bank%d" % (1 + i)], ["dq%d" % i])
+        tt(T.ng[:], T.nxf[:, 0:P].indirect(T.zl[:, 0:4]), T.dm[:], ALU.add, ["nxf", "zl", "dm"], ["ng"])
         tt(T.zg[:], T.zs[:, 0:P].indirect(T.zl[:, 0:4]), T.dm[:], ALU.add, ["zs0", "zs1", "zl", "dm"], ["zg"])
+        scan(T.nq[:, 8:72], T.rq[:], T.ng[:], 0.0, ALU.add, ALU.max, ["rq", "ng"], ["nq"])
         scan(T.rm[:, 8:72], T.zg[:], T.zg[:], -2e29, ALU.max, ALU.max, ["zg"], ["rm"])
+        tt(T.nd4[:], T.nq[:, 23:72:16], T.nq[:, 39:88:16], ALU.subtract, ["nq", "nqz"], ["nd4"])
+
+        def reached():
+            ts(T.bb[:], T.rm[:, 7:56:16], T.rm[:, 71:72], ALU.is_ge, ["rm", "rmz"], ["bb"])
+
+        def node():
+            scan(T["rn" + n][:, 5:9], T.bb[:], T.nd4[:], 0.0, ALU.mult, ALU.add, ["bb", "nd4", "rnz" + n], ["rnown" + n])
+            send(["rn" + n], ["rnown" + n])
+
+        if t == 0:
+            reached()
         ts(T.xb[:, 0:4 * N], T.rm[:, 0:64].indirect(T.xl[:, 0:2]), T.rm[:, 71:72], ALU.is_lt, ["xl", "rm", "rmz", "xbz"], ["xb"])
+        (reached if t else node)()
         quant(xq, 0, 128, T.xb[:], ["xbz", "xb"], [xq])
         mx(6, 128, "ws", 0, xq, 0, ["ws", xq])
+        if t:
+            node()
+            for h in range(2):
+                cp(T.v4[64 - 64 * h:128 - 64 * h, 4 * h:4 * h + 4], T.v4[64 * h:64 * h + 64, 4 * h:4 * h + 4], ["v4", "vm"], ["v4%d" % h])
+            wrote["v4"] = wrote["v41"]
+        else:
+            listed_b()
         tt(T.fl[:], bank(6, N), T.v4[:], ALU.add, ["bank6", "v4"], ["fl"])
-        cp(T.ct[:], T.fl[:], ["fl"], ["ct"])
         if t == 0:
-            act(T.yy[:], T.nxf[:, 0:P].indirect(T.ct[:, 0:8]), ["nxf", "ct"], ["yy"])
-        pick(kp, 0, "kq", P, T.ct[:, 0:8], 128, ["kq", "ct"], kp)
-        for i in range(4):
-            mx(1 + i, 128, "h", 128 * i, kp, 0, [kp + "_c", kp + "_s", "h%d" % i], False, True)
-        rn, nodt = T["rn" + n], T["nodt" + n]
-        if t == 1:
-            cp(T.yy[:], T.nxf[:, 0:P].indirect(T.ct[:, 0:8]), ["nxf", "ct"], ["yy"])
-        turn(nodt[:], T.yy[:], ["yy"], ["nodt" + n])
-        send(["rn" + n], ["nodt" + n])
-        for i in range(4):
-            if (i != 2 if t else i % 2):
-                act(nt[:, i:512:4], bank(1 + i, 128), ["bank%d" % (1 + i)], ["nt%s%d" % (n, i)])
-            else:
-                cp(nt[:, i:512:4], bank(1 + i, 128), ["bank%d" % (1 + i)], ["nt%s%d" % (n, i)])
+            listed_c(0)
+        cp(T.ct[:], T.fl[:], ["fl"], ["ct"])
+        for i in range(2):
+            act(T.dg[:, 128 * i:128 * i + 128], T.dk[:, P * (2 + i):P * (3 + i)].indirect(T.ct[:, 0:8]), ["dk%d" % (2 + i), "ct"], ["dg%d" % i])
+        for i in range(2):
+            tt(nt[:, i:512:4], T.dk[:, P * i:P * i + P].indirect(T.ct[:, 0:8]), T.dq[:, 128 * i:128 * i + 128], ALU.add,
+               ["dk%d" % i, "dq%d" % i, "ct"], ["nt%s%d" % (n, i)])
+        for i in range(2):
+            tt(nt[:, 2 + i:512:4], bank(3 + i, 128), T.dg[:, 128 * i:128 * i + 128], ALU.add, ["bank%d" % (3 + i), "dg%d" % i], ["nt%s%d" % (n, 2 + i)])
         quant("new" + n, 0, 128, nt[:], ["nt%s%d" % (n, i) for i in range(4)], ["new" + n])
-        send(["ret1_c", "ret1_s"] if t else ["ret0", "ret0_c"], ["new" + n])
-        act(rn[:, 0:1], nodt[:, 0:1], ["nodt" + n, "rnz" + n], ["rnown" + n])
-        pick(win, A, "new" + n, 128, T.ol[:, 0:1], CAPP, ["new" + n, "ol"], win + "own")
+        send(["ret%s_c" % n, "ret%s_s" % n], ["new" + n])
+        pick(win, A, "new" + n, 128, T.cu[:, 0:1], CAPP, ["new" + n, "cu"], win + "own")
 
     def home(t):
         n = str(t)
-        src = ["in_rn" + n, "rnown" + n, "rnz" + n, "elst"]
-        cp(T.sp[:, 0:64], T["rn" + n][:, 0:4 * N].indirect(T.elst[:, 0:4]), src, ["sp0"])
-        act(T.sp[:, 64:128], T["rn" + n][:, 0:4 * N].indirect(T.elst[:, 4:8]), src, ["sp1"])
-        turn(T.win[:, A:160], T.sp[:], ["sp0", "sp1"], ["winr"])
+        src = ["in_rn" + n, "rnown" + n, "rnz" + n, "cu"]
+        cp(T.sp[:, 0:32], T["rn" + n][:, 8:40].indirect(T.cu[:, 6:8]), src, ["sp0"])
+        if t:
+            turn(T.sq[:, 0:32], T.sp[:, 0:32], ["sp0"], ["sq"])
+            for b in range(4):
+                (act if b % 2 else cp)(T.win[0:32, A + 32 * b:A + 32 * b + 32], T.sq[32 * b:32 * b + 32, 0:32], ["sq"], ["winr%d%d" % (b // 2, b % 2)])
+            return
+        act(T.sp[:, 32:64], T["rn" + n][:, 8:40].indirect(T.cu[:, 6:8]), src, ["sp1"])
+        turn(T.sq[:], T.sp[:], ["sp0", "sp1"], ["sq"])
+        for b in range(4):
+            c, o = 32 * (b % 2), 32 * (b ^ 1)
+            (cp if b < 2 else act)(T.sq[o:o + 32, c:c + 32], T.sq[32 * b:32 * b + 32, c:c + 32], ["sq"], ["sq%d" % b])
+        for x in range(2):
+            for h in range(2):
+                (act if h else cp)(T.win[64 * x:64 * x + 64, A + 64 * h:A + 64 * h + 64], T.sq[64 * h:64 * h + 64, :],
+                                   ["sq%d" % (2 * h), "sq%d" % (2 * h + 1)], ["winr%d%d" % (x, h)])
 
-    for h in range(2):
-        ts(T.dr[:, 16 * h:16 * h + 16], T.strb[:, h:A:2], -31.5, ALU.add, ["strb"], ["drh%d" % h], 1.0 / 64, ALU.mult)
-    for h in range(2):
-        tt(T.xx[:, 16 * h:16 * h + 16], T.strb[:, h:A:2], T.xa[:, 16 * h:16 * h + 16], ALU.add, ["strb", "xa"], ["xxh%d" % h])
-    wrote["dr"], wrote["xx"] = wrote["drh1"], wrote["xxh1"]
-    lists(0)
+    ts(T.dr[:], T.strb[:, 0:A].indirect(T.pm[:, 0:2]), -31.5, ALU.add, ["strb", "pm"], ["dr"], 1.0 / 64, ALU.mult)
+    tt(T.xx[:, 0:A], T.strb[:, 0:A].indirect(T.pm[:, 0:2]), T.xa[:], ALU.add, ["strb", "pm", "xa"], ["xx"])
+    scaled(T.cc[:, 1:N], T.ioj[:, 1:N], float(A * Q), 0.0, ["ioj"], ["cc1"])
+    scaled(T.cc[:, 0:1], T.ioj[:, 0:1], 0.0, float(OWN * Q), ["ioj"], ["cc"])
+    zero(T.rq[:], T.mm[:, 0:64], ["mm"], ["rq"])
+    scaled(T.rq1[:], T.r1[:, 0:1], float(Q), 0.0, ["r1"], ["rq1"])
+    scaled(T.rm[:, 0:8], T.mm[:, 0:8], 0.0, 5e29, ["mm"], ["rmz"])
+    zero(T.nq[:, 80:88], T.mm[:, 0:8], ["mm"], ["nqz"])
+    scaled(T.rq[:, 0:64:16], T.mm[:, 0:4], 0.0, -5e29, ["mm", "rq"], ["rq"])
+    scaled(T.dm[:], T.mm[:, 0:64], 1e29, -1e29, ["mm"], ["dm"])
+    scaled(T.slott[:], T.io16[:], float(Q), T.rq1[:, 0:1], ["io16", "rq1"], ["slott"])
+    act(T.win[:, 0:A], T.strb[:, 0:A].indirect(T.pm[:, 0:2]), ["strb", "pm"], ["winq"])
+    zero(T.xb[:, 4 * N:512], T.xt[:, 4 * N:512], ["xt", "xtz"], ["xbz"])
+    lists()
+    queries(k0, k0 + 2)
     table(0)
     send(["xr0"], tab("l0") + ["rnz0", "rnz1"])
-    pick("send0", 0, "qx", 128, T.sl[:, k0:k0 + 2], 32, ["qx", "sl0", "sl1"], "send0")
+    pick("send0", 0, "qx", 128, T.sl[:, k0:k0 + 2], 32, ["qx", "sl%d1" % (k0 // 4)], "send0")
     send(["pick_c"], ["send0_c"])
     send(["pick_s"], ["send0_s"])
     act(T.xr0[:, 0:1], T.ti0[:, 0:1], tab("l0"), ["xrown0"])
     cp(T.nxp[:], T.nxt[:], ["nxt7"], ["nxp"])
     ts(T.nl[:], T.el[:], T.ec[:, 0:1], ALU.add, ["el", "ec"], ["nl"])
     act(T.nx1[:], T.nxp[:, 0:16].indirect(T.nl[:, 0:16]), ["nxp", "nl"], ["nx1"])
-    scaled(T.cc[:, 1:N], T.ioj[:, 1:N], float(A * Q), 0.0, ["ioj"], ["cc1"])
-    scaled(T.cc[:, 0:1], T.ioj[:, 0:1], 0.0, float(OWN * Q), ["ioj"], ["cc"])
-    zero(T.xb[:, 4 * N:512], T.kt[:, 4 * N:512], ["kt"], ["xbz"])
-    scaled(T.rm[:, 0:8], T.mm[:, 0:8], 0.0, 5e29, ["mm"], ["rmz"])
-    scaled(T.dm[:], T.mm[:, 0:64], 1e29, -1e29, ["mm"], ["dm"])
-    for k in (k0, k0 + 1):
-        ts(T.lsu[:, k:k + 1], T.r1[:, 0:1], float(A * k - 1), ALU.add, ["r1"], ["lsu%d" % k])
-    quant("lx0", OWN, OWN + 128, T.xt[:], ["xt", "xtz"], ["lx0own"])
+    ts(T.lsu[:, k0:k0 + 2], T.io16[:, 0:4:2], T.r1[:, 0:1], ALU.add, ["io16", "r1"], ["lsu1"], float(A * k0 - A), ALU.add)
     quant("kq", 0, P, T.kt[:], ["kt"], ["kq"])
     for i in range(4):
         quant("h", 128 * i, 128 * i + 128, T.hb[:, 3 - i:515 - i], ["hb"], ["h%d" % i])
-    tt(T.f3[:, 0:2], T.pd[:, 0:2], T.ib[:, 0:2], ALU.subtract, ["pd", "ib"], ["f3"])
-    cp(T.gl[:, 0:1], T.pd[:, 0:1], ["pd"], ["gl"])
+    for i in range(4):
+        mx(6 + i % 2, P, "h", 128 * i, "kq", 0, ["h%d" % i, "kq"])
+        if i < 2:
+            keys(i)
+    tt(T.f3[:, 0:2], T.ia[:, 4:6], T.ib[:, 0:2], ALU.subtract, ["pd", "ib"], ["f3"])
+    cp(T.cu[:], T.ia[:], ["ia", "pd", "pe"], ["cu"])
     tt(T.f3[:, 0:2], T.f3[:, 0:2], T.ioj[:, 0:8:4], ALU.is_equal, ["f3", "ioj"], ["f3"])
     quant("ws", 0, 128, T.wb[:], ["wb", "wb0", "wb1", "wb2"], ["ws"])
     ts(T.xl[:], T.f3[:, 0:2], T.v[:, 0:1], ALU.mult, ["f3", "v"], ["xl"], 63.0, ALU.min)
-    iota(T.io16[:], [[16, 8]], A - 1, 0, ["io16"])
     iota(T.rowc[:], [[1, 128]], A, 0, ["rowc"], True)
-    turn(T.nxf[:], T.nx1[:], ["nx1"], ["nxf"])
-    ts(T.slott[:], T.io16[:], T.r1[:, 0:1], ALU.add, ["io16", "r1"], ["slott"], float(Q), ALU.mult)
-    ts(T.elst[:], T.el[:, 0:8], T.ec[:, 0:1], ALU.add, ["el", "ec"], ["elst"], 4.0, ALU.mult)
-    tt(T.win[:, 0:A], T.xx[:, 0:A], T.xa[:], ALU.subtract, ["xx", "xa"], ["winq"])
-    inverse_a(0)
+    inverse(0, lambda: turn(T.nxf[:], T.nx1[:], ["nx1"], ["nxf"]), lambda: quant("lx0", OWN, OWN + 128, T.xt[:], ["xt", "xtz"], ["lx0own"]))
     received(0)
-    cp(T.ol[:, 0:1], T.ia[:, 0:1], ["ia"], ["ol"])
+    listed_a()
     dma("s", "w", T.wt[:], T.w[:], ["land0_c"], ["wt"])
     dma("s", "ownw", codes("wina", 0, A), codes("qx", 0, A), ["qx"], ["winaq"])
     dma("s", "ownw", T.winas[:, 0:A], T.qxs[:, 0:A], ["qx"], ["winaq2"])
     dma("s", "nd0", T.nd[0:1, :], T.win[0:1, 0:A], ["winq"], [])
     serve(0)
-    inverse_b(0, lambda: None)
     home(0)
-    ts(T.dr[:], T.win[:, 0:160].indirect(T.nu0[:, 0:2]), -31.5, ALU.add, ["winq", "winr", "nu0"], ["dr"], 1.0 / 64, ALU.mult)
-    tt(T.xx[:, 0:A], T.win[:, 0:160].indirect(T.nu0[:, 0:2]), T.xa[:], ALU.add, ["winq", "winr", "nu0", "xa"], ["xx"])
-    lists(1)
-    send(["xr1"], tab("x"))
+    row = ["winq", "winr10", "winr11"]
+    ts(T.dr[:], T.win[:, 0:160].indirect(T.nu0[:, 0:2]), -31.5, ALU.add, row + ["nu0"], ["dr"], 1.0 / 64, ALU.mult)
+    tt(T.xx[:, 0:A], T.win[:, 0:160].indirect(T.nu0[:, 0:2]), T.xa[:], ALU.add, row + ["nu0", "xa"], ["xx"])
+    lists()
+    cp(T.tx[:], T.mn[:, A:4 * S:S], mns, ["tx"])
+    send(["xr1h", "xr1"], ["tx"])
+    queries(0, 4)
+    queries(4, N)
     wina_c, wina_s = ["winaq2", "winaown_c", "in_ret0"], ["winaq2", "winaown_s", "in_ret0s"]
     pick("q1", 0, "wina", 160, T.nu0[:, 0:2], A, ["nu0"], "q1", wina_c, wina_s)
-    ts(T.sl[:], T.tx[:], 1.0 / Q, ALU.mult, tab("x"), ["sl0", "sl1"], float(A - 1), ALU.min)
-    pick("send1", 0, "q1", A, T.sl[:, 0:8], 128, ["sl0"], "send1", ["q1_c"], ["q1_s"])
+    pick("send1", 0, "q1", A, T.sl[:, 0:8], 128, ["sl11"], "send1", ["q1_c"], ["q1_s"])
     send(["land1_c"], ["send1_c"])
     send(["land1_s"], ["send1_s"])
-    pick("land1", 0, "send1", 128, T.ol[:, 0:1], CAPP, ["ol"], "land1own", ["send1_c"], ["send1_s"])
+    pick("land1", 0, "send1", 128, T.cu[:, 0:1], CAPP, ["cu"], "land1own", ["send1_c"], ["send1_s"])
     table(1)
-    cp(T.xr1[:, 0:1], T.tx[:, 0:1], tab("x"), ["xrown1"])
+    cp(T.xr1[:, 0:1], T.tx[:, 0:1], ["tx"], ["xrown1"])
     tt(T.win[:, 0:A], T.xx[:, 0:A], T.xa[:], ALU.subtract, ["xx", "xa"], ["winq"])
     dma("s", "nd1", T.nd[1:2, :], T.win[0:1, 0:A], ["winq"], [])
-    inverse_a(1)
-    inverse_b(1, lambda: pick("winb", 0, "wina", 160, T.nu0[:, 0:2], A, ["nu0"], "winbq", wina_c, wina_s))
+    inverse(1, lambda: pick("winb", 0, "wina", 160, T.nu0[:, 0:2], A, ["nu0"], "winbq", wina_c, wina_s), lambda: None)
+    listed_a()
+    listed_b()
+    listed_c(1)
     received(1)
     serve(1)
     quant("wq", 0, 128, T.wt[:], ["wt"], ["wq"])
     quant("fin", 0, 128, T.xt[:], ["xt", "xtz"], ["fin_c", "fin_s"])
     home(1)
-    cp(T.stw[:], T.win[:, 0:160].indirect(T.nu1[:, 0:2]), ["winq", "winr", "nu1"], ["stw"])
+    cp(T.stw[:], T.win[:, 0:160].indirect(T.nu1[:, 0:2]), row + ["nu1"], ["stw"])
     dma("s", "nd2", T.nd[2:3, :], T.stw[0:1, :], ["stw"], [])
     pick("fin", 0, "winb", 160, T.nu1[:, 0:2], A, ["winbq_c", "winbq_s", "winbown_c", "winbown_s", "in_ret1", "nu1"], "fin")
     mx(7, 128, "wq", 0, "fin", 0, ["wq", "fin_c", "fin_s"])

from concourse.bass import DstId, RemoteDMATransfer
from concourse.mybir import dt, AluOpType, AxisListType, ActivationFunctionType

N, P, A, CAPP = 8, 256, 32, 16
F8, U8, F32, BF, I32, U16 = "float8_e4m3fn_x4", "uint8", "float32", "bfloat16", "int32", "uint16"
Q = 2048
EMPTY = 256 * Q
S = A + 1
OWN = N * A
KINDS = ["near", "plane", "diag", "mate"]

MSG = {"wide_c": ("qxc", "lx0c", "lx0", A), "wide_s": ("qxs", "lx0s", "lx0", A), "pick_c": ("send0c", "lx0c", "lx0", CAPP),
       "pick_s": ("send0s", "lx0s", "lx0", CAPP), "xr0": ("ti0", "xr0", "xr0", 1), "xr1": ("tx", "xr1", "xr1", 1),
       "rn0": ("rn0", "rn0", "rn0", 1), "rn1": ("rn1", "rn1", "rn1", 1),
       "ret0_c": ("new0c", "winac", "ret0", CAPP), "ret0_s": ("new0s", "winas", "ret0s", CAPP),
       "land1_c": ("send1c", "land1c", "land1", CAPP), "land1_s": ("send1s", "land1s", "land1", CAPP),
       "ret1_c": ("new1c", "winbc", "ret1", CAPP), "ret1_s": ("new1s", "winbs", "ret1", CAPP)}
SAME = ("wide_c", "wide_s", "rn0", "rn1")
VIA = {"wide_s": ("diag",), "xr1": ("diag", "mate")}
CALLS = {"wide": (["wide_c"], 4), "wide2": (["wide_s", "+wide_s"], 4), "xr0": (["xr0"], 4), "pick_c": (["pick_c"], 2), "pick_s": (["pick_s"], 4),
         "rn0": (["rn0"], 4), "ret0_c": (["ret0_c"], 4), "ret0_s": (["ret0_s"], 4),
         "xr1h": (["+xr1"], 8), "xr1": (["xr1"], 4), "land1_c": (["land1_c"], 4), "land1_s": (["land1_s"], 4),
         "rn1": (["rn1"], 4), "ret1_c": (["ret1_c"], 4), "ret1_s": (["ret1_s"], 4)}
SCRATCH = {}


def _add(name, cols, dtype, where="sbuf"):
    SCRATCH[name] = (where, [128, cols], dtype)


for _n, _c in (("qx", 128), ("lx0", OWN + 128), ("send0", 32), ("land0", 128), ("new0", 128), ("wina", 160), ("q1", 32), ("send1", 128),
               ("land1", 128), ("new1", 128), ("winb", 160), ("fin", 128), ("kq", 256), ("wq", 128), ("h", 512), ("ws", 128),
               ("xq0", 128), ("xq1", 128)):
    _add(_n + "c", _c, F8)
    _add(_n + "s", _c, U8)
for _n, _c, _d in (("xt", 512, BF), ("kt", 1024, BF), ("wt", 512, BF), ("hb", 516, BF), ("wb", 512, BF), ("xb", 512, BF),
                   ("iop", 8, I32), ("ioj", 32, F32), ("jmp", 128, I32), ("jmq", 128, I32), ("xa", 32, F32),
                   ("el", 16, I32), ("rowc", 128, F32), ("io16", 8, F32), ("slott", 8, F32),
                   ("ia", 8, I32), ("cu", 8, U16), ("pm", 2, U16), ("rq1", 1, F32),
                   ("mm", 128, F32), ("dm", 64, F32), ("xl", 2, U16), ("rq", 64, F32),
                   ("r1", 4, F32), ("ec", 1, F32), ("dcol", 4, F32), ("rst", 4 * S, BF),
                   ("cc", 8, F32), ("stc", 1, I32), ("stw", 32, F32), ("strb", 32, F32),
                   ("nxt", 16, I32), ("nxp", 16, F32), ("nl", 16, U16), ("nx1", 256, F32), ("nxf", 256, F32),
                   ("lsu", 8, U16), ("sl", 8, U16), ("ys", 32, F32), ("ib", 8, I32), ("f3", 8, F32),
                   ("ti0", N, F32), ("xr0", 4 * N, F32), ("ti1", N, F32), ("tx", 4, U16), ("xr1", 8 * N, U16), ("dk", 4 * P, F32),
                   ("dr", 32, I32), ("xx", S + 1, F32), ("zl", 4, U16), ("ct", 8, U16),
                   ("win", 160, F32), ("lu", 8, U16), ("so", 160, F32), ("dn", 32, F32),
                   ("vi", 8, I32), ("v4", 8, I32), ("vm", 16, F32), ("v", 1, F32), ("zs", 256, F32), ("zg", 64, F32), ("rm", 72, F32),
                   ("ng", 64, F32), ("nq", 88, F32), ("nd4", 4, F32), ("bb", 4, F32), ("sp", 64, F32), ("sq", 64, F32),
                   ("dq", 256, F32), ("dg", 256, F32), ("eqb", 4 * S, BF), ("cum", 4 * S + 2, BF), ("mn", 4 * S, F32),
                   ("fl", 8, F32), ("f2", 8, F32), ("n2", 2, F32)):
    _add(_n, _c, _d)
for _t in ("0", "1"):
    for _n, _c, _d in (("nt", 512, BF), ("rn", 40, F32), ("nu", 2, U16)):
        _add(_n + _t, _c, _d)
for _n in VIA:
    _add("h" + _n, 4 * MSG[_n][3], SCRATCH[MSG[_n][0]][2])
_add("bank", 512 * 8, F32, "psum")
ARRIVE = ["lx0", "xr0", "rn0", "ret0", "ret0s", "xr1", "land1", "rn1", "ret1"] + ["h" + _n for _n in VIA]
DMAS = ["st", "x", "ky", "nx", "w", "ownw", "nd0", "nd1", "nd2", "oc", "osc", "y"]
SEMAPHORES = ["sg", "sv", "sa", "sp", "left"] + ["a_" + k for k in ARRIVE] + ["d_" + k for k in DMAS]


def _bits(m):
    return bin(m).count("1")


def _view(T, name, a, n):
    v = T[name][:, a:a + n]
    return v.bitcast(dt.uint8) if SCRATCH[name][2] == F8 else v


def _places(topo, cores, rank):
    me = cores[rank]
    kind = ["near" if c in topo.cores_of(me) else "plane" if topo.same_plane(me, c) else "mate" if topo.mates(me, c) else "diag" for c in cores]
    return kind, [2 * KINDS.index(kind[r]) + (r + rank) % 2 for r in range(N)]


def _plan(topo, T, cores, rank):
    me = cores[rank]
    kind, place = _places(topo, cores, rank)
    others = [r for r in range(N) if r != rank]
    helper = [c for c in topo.cores_of(me) if c not in cores and topo.die(c) == topo.die(me) and all(topo.may_write(c, d) for d in cores)][0]
    port = topo.engines(me, cores[kind.index("mate")])
    inner = [e for e in topo.engines(me, helper) if e not in port]

    def ends(m, r):
        k = place[r]
        if m[:4] == "wide":
            return 0, A * k
        if m[:4] == "pick":
            return CAPP * (k % 2), A * k
        if m[:2] == "xr":
            return k % SCRATCH[MSG[m][0]][1][1], SCRATCH[m][1][1] // N * k
        if m[:2] == "rn":
            return 8, 4 * k + 8
        return CAPP * k, CAPP * k + (0 if m[:4] == "land" else A)

    def dests(m):
        return [r for r in others if (kind[r] == "mate") == (m[:4] == "pick") or m[:4] not in ("wide", "pick")]

    load = {}
    turn = [0]

    def deal(core, items, cap, same):
        off = [i for i in items if i[0] not in topo.cores_of(core)]
        on = [i for i in items if i[0] in topo.cores_of(core)]
        if off and len(port) % len(off):
            k = turn[0] % len(off)
            turn[0] += 2
            off = off[k:] + off[:k]
        out = []
        for group, pool in ((off, port), (on[::-1], inner)):
            if same and pool is port:
                out += [(c, sum(1 << e for e in port), sem, src, dst) for c, sem, src, dst in group]
                continue
            free = sorted(pool, key=lambda e: load.get((core, e), 0))
            for i, (c, sem, src, dst) in enumerate(group):
                rest = len(group) - i
                most = min(cap, len(free) // rest)
                take = 1
                while 2 * take <= most:
                    take *= 2
                for e in free[:take]:
                    load[core, e] = load.get((core, e), 0) + 8 // take
                out.append((c, sum(1 << e for e in free[:take]), sem, src, dst))
                free = free[take:]
        return out

    plan = {}
    for name, (parts, cap) in CALLS.items():
        items = []
        if name == "rn0":
            for e in port:
                load[me, e] = 0
        for m in parts:
            if m[0] != "+":
                src, dst, sem, n = MSG[m]
                for r in dests(m):
                    if kind[r] not in VIA.get(m, ()):
                        a, b = ends(m, r)
                        items.append((cores[r], sem, _view(T, src, a, n), _view(T, dst, b, n)))
                continue
            m = m[1:]
            src, dst, sem, n = MSG[m]
            w = n if m in SAME else 4 * n
            items.append((helper, "h" + m, _view(T, src, 0, w), _view(T, "h" + m, 0, w)))
            on = [(cores[r], sem, _view(T, "h" + m, ends(m, r)[0], n), _view(T, dst, ends(m, r)[1], n)) for r in dests(m) if kind[r] in VIA[m]]
            plan[helper, m] = deal(helper, on, 4, m in SAME)
        plan[me, name] = deal(me, items, cap, parts[0] in SAME)
    return plan


def _fused(g, T, topo, core, call):
    tr = []
    masks = sorted(set(t[1] for t in call))
    for m in masks:
        same = [t for t in call if t[1] == m]
        ids = [DstId(rid=topo.addr(t[0], core)[0], pnc=topo.addr(t[0], core)[1]) for t in same]
        tr.append(RemoteDMATransfer(dst_ids=ids, dma_engine_mask=m, remote_sem=T.sem["a_" + same[0][2]], srcs=[same[0][3]], dsts=[t[4] for t in same]))
    g.remote_dma_fused(tr, local_sem=T.sem.left)
    return sum(_bits(m) for m in masks)


def rank_program(g, core, T, topo):
    rank = T.rank_of(core)
    cores = list(T.cores)
    if not any(core in topo.cores_of(c) for c in cores):
        return
    plans = [_plan(topo, T, cores, r) for r in range(N)]
    want = {k: 0 for k in ARRIVE}
    for plan in plans:
        for call in plan.values():
            for c, m, sem, _s, _d in call:
                if c == core:
                    want[sem] += _bits(m)
    if rank is None:
        gone = 0
        for plan in plans:
            for (c, m), call in plan.items():
                if c == core:
                    g.wait_ge(T.sem["a_h" + m], want["h" + m])
                    gone += _fused(g, T, topo, core, call)
        if gone:
            g.wait_ge(T.sem.left, gone)
        return
    calls = plans[rank]
    kind, place = _places(topo, cores, rank)
    at = [place.index(k) for k in range(N)]
    ALU, X, CP = AluOpType, AxisListType.X, ActivationFunctionType.Copy
    queues = {"g": g, "v": g.vector, "a": g.scalar, "p": g.tensor, "s": g.sync}
    sems = {"g": "sg", "v": "sv", "a": "sa", "p": "sp"}
    count = {k: 0 for k in sems}
    known = {k: {} for k in queues}
    snap = {}
    wrote, readers = {}, {}

    def waits(q, reads, writes):
        need = [wrote[k] for k in reads]
        for k in writes:
            if k in wrote:
                need.append(wrote[k])
            for e, rq in readers.get(k, []):
                if rq != q or e[0].startswith("d_"):
                    need.append(e)
        best = {}
        for s, val in need:
            if known[q].get(s, 0) < val:
                best[s] = max(best.get(s, 0), val)
        for s in sorted(best, key=lambda s: -len(snap.get((s, best[s]), {}))):
            val = best[s]
            if known[q].get(s, 0) >= val:
                continue
            queues[q].wait_ge(T.sem[s], val)
            known[q][s] = val
            for s2, v2 in snap.get((s, val), {}).items():
                known[q][s2] = max(known[q].get(s2, 0), v2)

    def note(q, ev, reads, writes):
        snap[ev] = dict(known[q])
        for k in reads:
            readers.setdefault(k, []).append((ev, q))
        for k in writes:
            wrote[k] = ev
            readers[k] = []

    def op(q, fn, reads, writes):
        waits(q, reads, writes)
        count[q] += 1
        fn(queues[q]).then_inc(T.sem[sems[q]], 1)
        note(q, (sems[q], count[q]), reads, writes)

    dcount = {}

    def dma(q, name, out, in_, reads, writes):
        s = "d_" + name
        waits(q, reads, writes)
        queues[q].dma_start(out, in_).then_inc(T.sem[s], 16)
        dcount[s] = dcount.get(s, 0) + 16
        note(q, (s, dcount[s]), reads, writes)

    left = [0]

    def send(names, reads):
        waits("g", reads, [])
        for name in names:
            left[0] += _fused(g, T, topo, core, calls[core, name])

    for k in ARRIVE:
        wrote["in_" + k] = ("a_" + k, want[k])

    def codes(name, a, b):
        return T[name + "c"][:, a:b].bitcast(dt.uint8)

    def words(name, a, b):
        return T[name + "c"][:, a:b].bitcast(dt.uint32)

    def ts(out, in0, s1, op0, reads, writes, s2=None, op1=None):
        if op1 is None:
            op("v", lambda e: e.tensor_scalar(out, in0, s1, None, op0), reads, writes)
        else:
            op("v", lambda e: e.tensor_scalar(out, in0, s1, s2, op0, op1), reads, writes)

    def tt(out, a, b, o, reads, writes):
        op("v", lambda e: e.tensor_tensor(out, a, b, o), reads, writes)

    def cp(out, a, reads, writes):
        op("v", lambda e: e.tensor_copy(out, a), reads, writes)

    def red(out, a, reads, writes, o=ALU.add):
        op("v", lambda e: e.tensor_reduce(out, a, X, o), reads, writes)

    def scan(out, a, b, init, o0, o1, reads, writes):
        op("v", lambda e: e.tensor_tensor_scan(out, a, b, init, o0, o1), reads, writes)

    def turn(out, a, reads, writes):
        op("v", lambda e: e.transpose(out, a), reads, writes)

    def fill(ap, value, writes):
        op("v", lambda e: e.memset(ap, value), [], writes)

    def quant(name, a, b, tile, reads, writes):
        op("v", lambda e: e.quantize_mx(T[name + "c"][:, a:b], T[name + "s"][:, a:b], tile), reads, writes)

    def iota(out, pattern, base, step, writes, flag=False):
        if flag:
            op("g", lambda e: e.iota(out, pattern, base, step, allow_small_or_imprecise_dtypes=True), [], writes)
        else:
            op("g", lambda e: e.iota(out, pattern, base, step), [], writes)

    def mx(bank, n, l, la, r, ra, reads):
        op("p", lambda e: e.matmul_mx(T.bank[:, 512 * bank:512 * bank + n], T[l + "c"][:, la:la + 128], T[l + "s"][:, la:la + 128],
                                      T[r + "c"][:, ra:ra + n], T[r + "s"][:, ra:ra + n], True, True), reads, ["bank%d" % bank])

    def bank(k, n):
        return T.bank[:, 512 * k:512 * k + n]

    def act(out, in_, reads, writes):
        op("a", lambda e: e.activation(out, in_, CP), reads, writes)

    def zero(out, in_, reads, writes):
        op("a", lambda e: e.activation(out, in_, CP, scale=0.0), reads, writes)

    def scaled(out, in_, scale, bias, reads, writes):
        op("a", lambda e: e.activation(out, in_, ActivationFunctionType.Identity, bias=bias, scale=scale), reads, writes)

    def pick(out, oa, win, wb, off, n, reads, key, for_codes=(), for_scales=()):
        cp(words(out, oa, oa + n), words(win, 0, wb).indirect(off), reads + list(for_codes), [key + "_c"])
        act(T[out + "s"][:, oa:oa + n], T[win + "s"][:, 0:wb].indirect(off), reads + list(for_scales), [key + "_s"])

    dma("a", "x", T.xt[:, 0:4 * A], T.x[:], [], ["xt"])
    for b in range(4):
        dma("s", "st", T.stc[32 * b:32 * b + 32, :], T.st[:], [], ["stc%d" % b])
    dma("s", "ky", T.kt[:], T.ky[:], [], ["kt"])
    for b in range(8):
        dma("s", "nx", T.nxt[16 * b:16 * b + 16, :], T.nx[:], [], ["nxt%d" % b])
    iota(T.iop[:], [[0, 8]], 0, 1, ["iop"])
    iota(T.jmp[:], [[1, 128]], 0, -1, ["jmp"])
    iota(T.dcol[:], [[at[2] - at[0], 2], [at[1] - at[0], 2]], at[0], 0, ["dcol"], True)
    iota(T.ioj[:], [[1, A]], 0, 0, ["ioj"], True)
    iota(T.xa[:], [[Q, A]], 0, 0, ["xa"], True)
    iota(T.el[:], [[2, 8], [0, 2]], 0, 0, ["el"])
    iota(T.io16[:], [[16, 8]], A - 1, 0, ["io16"], True)
    fill(T.hb[:], 0.0, ["hb"])
    zero(T.xt[:, 4 * A:512], T.hb[:, 4 * A:512], ["hb"], ["xtz"])
    for j in (0, 2):
        scaled(T.dcol[64:128, j:j + 2], T.dcol[64:128, j:j + 2], 1.0, float(at[4 + j] - at[j]), ["dcol"], ["dcol%d" % j])
    fill(T.rst[:], 1.0, ["rst"])
    fill(T.nu1[:], 0, ["nu1"])
    fill(T.xx[:, A:S], float(EMPTY), ["xxz"])
    fill(T.rst[:, A:4 * S:S], 0.0, ["rst"])
    ts(T.ia[:, 0:4], T.iop[:, 0:4], 15, ALU.bitwise_and, ["iop"], ["ia"])
    ts(T.ia[:, 4:6], T.iop[:, 0:2], 4, ALU.arith_shift_right, ["iop"], ["pd"])
    ts(T.ia[:, 6:8], T.iop[:, 0:2], 2, ALU.arith_shift_right, ["iop"], ["pe"], 28, ALU.bitwise_and)
    ts(T.jmq[:], T.jmp[:], 15, ALU.bitwise_and, ["jmp"], ["jmq"])
    ts(T.r1[:], T.ia[:, 0:4], 1.0, ALU.add, ["ia"], ["r1"])
    scaled(T.cum[:, 0:1], T.r1[:, 0:1], float(2 * EMPTY), 0.0, ["r1"], ["cumz"])
    scaled(T.eqb[:, A:4 * S:S], T.r1[:], float(2 * EMPTY), 0.0, ["r1"], ["eqz"])
    scaled(T.n2[:, 0:1], T.r1[:, 0:1], 2.0, -2.0, ["r1"], ["n20"])
    ts(T.mm[:], T.jmq[:], 0.0, ALU.is_equal, ["jmq"], ["mm"])
    ts(T.ib[:, 0:2], T.iop[:, 0:2], 2, ALU.arith_shift_right, ["iop"], ["ib"], 3, ALU.bitwise_and)
    ts(T.vi[:, 0:1], T.iop[:, 0:1], 3, ALU.bitwise_and, ["iop"], ["vi"])
    ts(T.v4[:, 0:1], T.iop[:, 0:1], 4, ALU.arith_shift_right, ["iop"], ["v4"], 1, ALU.bitwise_and)
    ts(T.hb[:, 3:515:4], T.jmp[:], 0.0, ALU.is_equal, ["jmp"], ["hb"], 0.5, ALU.mult)
    cp(T.ec[:], T.v4[:, 0:1], ["v4"], ["ec"])
    ts(T.pm[:], T.ioj[:, 0:2], T.n2[:, 0:1], ALU.add, ["ioj", "n20"], ["pm"])
    ts(T.v[:], T.vi[:, 0:1], 16.0, ALU.mult, ["vi"], ["v"], 23.0, ALU.add)
    zero(T.rn0[:], T.mm[:, 0:40], ["mm"], ["rnz0"])
    zero(T.rn1[:], T.mm[:, 0:40], ["mm"], ["rnz1"])
    zero(T.wb[:, 3:512:4], T.mm[:], ["mm"], ["wb"])
    for k in range(3):
        act(T.wb[:, k:512:4], T.mm[:], ["mm", "wb"], ["wb%d" % k])
    quant("qx", 0, 128, T.xt[:], ["xt", "xtz"], ["qx"])
    send(["wide", "wide2"], ["qx"])
    cp(T.stw[:], T.stc[:, 0:1].indirect(T.nu1[:, 0:2]), ["stc3", "nu1"], ["stw"])
    turn(T.strb[:], T.stw[:], ["stw"], ["strb"])

    def tab(k):
        return ["tab%s%d%d" % (k, a, b) for a in range(2) for b in range(2)]

    mns = ["mn%d" % q for q in range(4)]
    k0 = 2 * KINDS.index("mate")

    def lists():
        for q in range(4):
            ts(T.eqb[:, S * q:S * q + A], T.dr[:], T.dcol[:, q:q + 1], ALU.is_equal, ["dr", "dcol2"], ["eqb%d" % q], -2.0 * EMPTY, ALU.mult)
        scan(T.cum[:, 1:4 * S + 1], T.rst[:], T.eqb[:], T.cum[:, 0:1], ALU.mult, ALU.add, ["rst", "eqz", "cumz"] + ["eqb%d" % q for q in range(4)], ["cum"])
        for q in range(4):
            scan(T.mn[:, S * q:S * q + S], T.cum[:, S * q:S * q + S], T.xx[:, 0:S], 0.0, ALU.max, ALU.min, ["cum", "cumz", "xx", "xxz"], [mns[q]])

    def table(t):
        for a in range(2):
            for b in range(2):
                act(T["ti%d" % t][64 * b:64 * b + 64, 4 * a:4 * a + 4], T.mn[64 * a:64 * a + 64, A:4 * S:S], mns, ["tabl%d%d%d" % (t, a, b)])

    def queries(lo, hi):
        a = lo // 4
        for b in range(2):
            ts(T.sl[64 * b:64 * b + 64, lo:hi], T.mn[64 * a:64 * a + 64, S * (lo % 4) + A:S * (hi - 4 * a):S], 1.0 / Q, ALU.mult, mns,
               ["sl%d%d" % (a, b)], float(A - 1), ALU.min)

    def inverse(t, first, second):
        tt(T.f2[:], T["ti%d" % t][:], T.slott[:], ALU.min, tab("l%d" % t) + ["slott"], ["f2"])
        act(T.so[:, 0:A], T.ioj[:], ["ioj"], ["so"])
        first()
        ts(T.lu[:], T.f2[:], 1.0 / Q, ALU.mult, ["f2"], ["lu"])
        second()
        cp(T.so[:, 0:160].indirect(T.lu[:, 0:8]), T.rowc[:], ["rowc", "lu"], ["so"])

    def listed_a():
        tt(T.dn[:], T.so[:, 0:A], T.mm[:, 0:A], ALU.mult, ["so", "mm"], ["dn"])

    def listed_b():
        for h in range(2):
            red(T.n2[:, h:h + 1], T.dn[:, 16 * h:16 * h + 16], ["dn"], ["n2%d" % h])

    def listed_c(t):
        cp(T["nu%d" % t][:], T.n2[:], ["n20", "n21"], ["nu%d" % t])

    def received(t):
        n = str(t)
        src = ["in_xr" + n, "xrown" + n]
        if t == 0:
            tt(T.fl[:, 0:k0], T.xr0[:, 0:4 * k0:4], T.cc[:, 0:k0], ALU.add, src + ["cc", "cc1"], ["fl"])
        ts(T.vi[:], T.xr1[:, 0:8 * N:8] if t else T.xr0[:, 0:4 * N:4], 4.0, ALU.mult, src, ["vi"])
        if t == 0:
            ts(T.lsu[:, 0:k0], T.fl[:, 0:k0], 1.0 / Q, ALU.mult, ["fl"], ["lsu0"], float(OWN + A - 1), ALU.min)
        ts(T.v4[:], T.vi[:], 255, ALU.bitwise_and, ["vi"], ["v4"])
        if t == 0:
            pick("land0", 0, "lx0", OWN + A, T.lsu[:, 0:8], 128, ["in_lx0", "lx0own", "lsu0", "lsu1"], "land0")
        cp(T.vm[:], T.v4[:, 0:8].indirect(T.cu[:, 4:5]), ["v4", "cu"], ["vm"])
        ts(T.zl[:], T.ioj[:, 0:4], T.vm[:, 0:1], ALU.add, ["ioj", "vm"], ["zl"])

    def keys(i):
        act(T.dk[:, P * i:P * i + P], bank(6 + i % 2, P), ["bank%d" % (6 + i % 2)], ["dk%d" % i])

    def serve(t):
        n = str(t)
        land, nt, xq, win = "land" + n, T["nt" + n], "xq" + n, ("wina", "winb")[t]
        lk = ["land0_c", "land0_s"] if t == 0 else ["in_land1", "land1own_c", "land1own_s"]
        mx(0, 128, land, 0, "kq", 0, lk + ["kq"])
        mx(5, 128, land, 0, "kq", 128, lk + ["kq"])
        for i in range(4):
            mx(1 + i, 128, "h", 128 * i, land, 0, lk + ["h%d" % i])
        act(T.zs[:, 0:128], bank(0, 128), ["bank0"], ["zs0"])
        (act if t else cp)(T.zs[:, 128:256], bank(5, 128), ["bank5"], ["zs1"])
        if t == 0:
            keys(2)
            keys(3)
        for i in range(2):
            act(T.dq[:, 128 * i:128 * i + 128], bank(1 + i, 128), ["bank%d" % (1 + i)], ["dq%d" % i])
        tt(T.ng[:], T.nxf[:, 0:P].indirect(T.zl[:, 0:4]), T.dm[:], ALU.add, ["nxf", "zl", "dm"], ["ng"])
        tt(T.zg[:], T.zs[:, 0:P].indirect(T.zl[:, 0:4]), T.dm[:], ALU.add, ["zs0", "zs1", "zl", "dm"], ["zg"])
        scan(T.nq[:, 8:72], T.rq[:], T.ng[:], 0.0, ALU.add, ALU.max, ["rq", "ng"], ["nq"])
        scan(T.rm[:, 8:72], T.zg[:], T.zg[:], -2e29, ALU.max, ALU.max, ["zg"], ["rm"])
        tt(T.nd4[:], T.nq[:, 23:72:16], T.nq[:, 39:88:16], ALU.subtract, ["nq", "nqz"], ["nd4"])

        def reached():
            ts(T.bb[:], T.rm[:, 7:56:16], T.rm[:, 71:72], ALU.is_ge, ["rm", "rmz"], ["bb"])

        def node():
            scan(T["rn" + n][:, 5:9], T.bb[:], T.nd4[:], 0.0, ALU.mult, ALU.add, ["bb", "nd4", "rnz" + n], ["rnown" + n])
            send(["rn" + n], ["rnown" + n])

        if t == 0:
            reached()
        ts(T.xb[:, 0:4 * N], T.rm[:, 0:64].indirect(T.xl[:, 0:2]), T.rm[:, 71:72], ALU.is_lt, ["xl", "rm", "rmz", "xbz"], ["xb"])
        (reached if t else node)()
        quant(xq, 0, 128, T.xb[:], ["xbz", "xb"], [xq])
        mx(6, 128, "ws", 0, xq, 0, ["ws", xq])
        if t:
            node()
            for h in range(2):
                cp(T.v4[64 - 64 * h:128 - 64 * h, 4 * h:4 * h + 4], T.v4[64 * h:64 * h + 64, 4 * h:4 * h + 4], ["v4", "vm"], ["v4%d" % h])
            wrote["v4"] = wrote["v41"]
        else:
            listed_b()
        tt(T.fl[:], bank(6, N), T.v4[:], ALU.add, ["bank6", "v4"], ["fl"])
        if t == 0:
            listed_c(0)
        cp(T.ct[:], T.fl[:], ["fl"], ["ct"])
        for i in range(2):
            act(T.dg[:, 128 * i:128 * i + 128], T.dk[:, P * (2 + i):P * (3 + i)].indirect(T.ct[:, 0:8]), ["dk%d" % (2 + i), "ct"], ["dg%d" % i])
        for i in range(2):
            tt(nt[:, i:512:4], T.dk[:, P * i:P * i + P].indirect(T.ct[:, 0:8]), T.dq[:, 128 * i:128 * i + 128], ALU.add,
               ["dk%d" % i, "dq%d" % i, "ct"], ["nt%s%d" % (n, i)])
        for i in range(2):
            tt(nt[:, 2 + i:512:4], bank(3 + i, 128), T.dg[:, 128 * i:128 * i + 128], ALU.add, ["bank%d" % (3 + i), "dg%d" % i], ["nt%s%d" % (n, 2 + i)])
        quant("new" + n, 0, 128, nt[:], ["nt%s%d" % (n, i) for i in range(4)], ["new" + n])
        send(["ret%s_c" % n, "ret%s_s" % n], ["new" + n])
        pick(win, A, "new" + n, 128, T.cu[:, 0:1], CAPP, ["new" + n, "cu"], win + "own")

    def home(t):
        n = str(t)
        src = ["in_rn" + n, "rnown" + n, "rnz" + n, "cu"]
        cp(T.sp[:, 0:32], T["rn" + n][:, 8:40].indirect(T.cu[:, 6:8]), src, ["sp0"])
        if t:
            turn(T.sq[:, 0:32], T.sp[:, 0:32], ["sp0"], ["sq"])
            for b in range(4):
                (act if b % 2 else cp)(T.win[0:32, A + 32 * b:A + 32 * b + 32], T.sq[32 * b:32 * b + 32, 0:32], ["sq"], ["winr%d%d" % (b // 2, b % 2)])
            return
        act(T.sp[:, 32:64], T["rn" + n][:, 8:40].indirect(T.cu[:, 6:8]), src, ["sp1"])
        turn(T.sq[:], T.sp[:], ["sp0", "sp1"], ["sq"])
        for b in range(4):
            c, o = 32 * (b % 2), 32 * (b ^ 1)
            (cp if b < 2 else act)(T.sq[o:o + 32, c:c + 32], T.sq[32 * b:32 * b + 32, c:c + 32], ["sq"], ["sq%d" % b])
        for x in range(2):
            for h in range(2):
                (act if h else cp)(T.win[64 * x:64 * x + 64, A + 64 * h:A + 64 * h + 64], T.sq[64 * h:64 * h + 64, :],
                                   ["sq%d" % (2 * h), "sq%d" % (2 * h + 1)], ["winr%d%d" % (x, h)])

    ts(T.dr[:], T.strb[:, 0:A].indirect(T.pm[:, 0:2]), -31.5, ALU.add, ["strb", "pm"], ["dr"], 1.0 / 64, ALU.mult)
    tt(T.xx[:, 0:A], T.strb[:, 0:A].indirect(T.pm[:, 0:2]), T.xa[:], ALU.add, ["strb", "pm", "xa"], ["xx"])
    scaled(T.cc[:, 1:N], T.ioj[:, 1:N], float(A * Q), 0.0, ["ioj"], ["cc1"])
    scaled(T.cc[:, 0:1], T.ioj[:, 0:1], 0.0, float(OWN * Q), ["ioj"], ["cc"])
    zero(T.rq[:], T.mm[:, 0:64], ["mm"], ["rq"])
    scaled(T.rq1[:], T.r1[:, 0:1], float(Q), 0.0, ["r1"], ["rq1"])
    scaled(T.rm[:, 0:8], T.mm[:, 0:8], 0.0, 5e29, ["mm"], ["rmz"])
    zero(T.nq[:, 80:88], T.mm[:, 0:8], ["mm"], ["nqz"])
    scaled(T.rq[:, 0:64:16], T.mm[:, 0:4], 0.0, -5e29, ["mm", "rq"], ["rq"])
    scaled(T.dm[:], T.mm[:, 0:64], 1e29, -1e29, ["mm"], ["dm"])
    scaled(T.slott[:], T.io16[:], float(Q), T.rq1[:, 0:1], ["io16", "rq1"], ["slott"])
    act(T.win[:, 0:A], T.strb[:, 0:A].indirect(T.pm[:, 0:2]), ["strb", "pm"], ["winq"])
    zero(T.xb[:, 4 * N:512], T.xt[:, 4 * N:512], ["xt", "xtz"], ["xbz"])
    lists()
    queries(k0, k0 + 2)
    table(0)
    send(["xr0"], tab("l0") + ["rnz0", "rnz1"])
    pick("send0", 0, "qx", 128, T.sl[:, k0:k0 + 2], 32, ["qx", "sl%d1" % (k0 // 4)], "send0")
    send(["pick_c"], ["send0_c"])
    send(["pick_s"], ["send0_s"])
    act(T.xr0[:, 0:1], T.ti0[:, 0:1], tab("l0"), ["xrown0"])
    cp(T.nxp[:], T.nxt[:], ["nxt7"], ["nxp"])
    ts(T.nl[:], T.el[:], T.ec[:, 0:1], ALU.add, ["el", "ec"], ["nl"])
    act(T.nx1[:], T.nxp[:, 0:16].indirect(T.nl[:, 0:16]), ["nxp", "nl"], ["nx1"])
    ts(T.lsu[:, k0:k0 + 2], T.io16[:, 0:4:2], T.r1[:, 0:1], ALU.add, ["io16", "r1"], ["lsu1"], float(A * k0 - A), ALU.add)
    quant("kq", 0, P, T.kt[:], ["kt"], ["kq"])
    for i in range(4):
        quant("h", 128 * i, 128 * i + 128, T.hb[:, 3 - i:515 - i], ["hb"], ["h%d" % i])
    for i in range(4):
        mx(6 + i % 2, P, "h", 128 * i, "kq", 0, ["h%d" % i, "kq"])
        if i < 2:
            keys(i)
    tt(T.f3[:, 0:2], T.ia[:, 4:6], T.ib[:, 0:2], ALU.subtract, ["pd", "ib"], ["f3"])
    cp(T.cu[:], T.ia[:], ["ia", "pd", "pe"], ["cu"])
    tt(T.f3[:, 0:2], T.f3[:, 0:2], T.ioj[:, 0:8:4], ALU.is_equal, ["f3", "ioj"], ["f3"])
    quant("ws", 0, 128, T.wb[:], ["wb", "wb0", "wb1", "wb2"], ["ws"])
    ts(T.xl[:], T.f3[:, 0:2], T.v[:, 0:1], ALU.mult, ["f3", "v"], ["xl"], 63.0, ALU.min)
    iota(T.rowc[:], [[1, 128]], A, 0, ["rowc"], True)
    inverse(0, lambda: turn(T.nxf[:], T.nx1[:], ["nx1"], ["nxf"]), lambda: quant("lx0", OWN, OWN + 128, T.xt[:], ["xt", "xtz"], ["lx0own"]))
    received(0)
    listed_a()
    dma("s", "w", T.wt[:], T.w[:], ["land0_c"], ["wt"])
    dma("s", "ownw", codes("wina", 0, A), codes("qx", 0, A), ["qx"], ["winaq"])
    dma("s", "ownw", T.winas[:, 0:A], T.qxs[:, 0:A], ["qx"], ["winaq2"])
    dma("s", "nd0", T.nd[0:1, :], T.win[0:1, 0:A], ["winq"], [])
    serve(0)
    home(0)
    row = ["winq", "winr10", "winr11"]
    ts(T.dr[:], T.win[:, 0:160].indirect(T.nu0[:, 0:2]), -31.5, ALU.add, row + ["nu0"], ["dr"], 1.0 / 64, ALU.mult)
    tt(T.xx[:, 0:A], T.win[:, 0:160].indirect(T.nu0[:, 0:2]), T.xa[:], ALU.add, row + ["nu0", "xa"], ["xx"])
    lists()
    cp(T.tx[:], T.mn[:, A:4 * S:S], mns, ["tx"])
    send(["xr1h", "xr1"], ["tx"])
    queries(0, 4)
    queries(4, N)
    wina_c, wina_s = ["winaq2", "winaown_c", "in_ret0"], ["winaq2", "winaown_s", "in_ret0s"]
    pick("q1", 0, "wina", 160, T.nu0[:, 0:2], A, ["nu0"], "q1", wina_c, wina_s)
    pick("send1", 0, "q1", A, T.sl[:, 0:8], 128, ["sl11"], "send1", ["q1_c"], ["q1_s"])
    send(["land1_c"], ["send1_c"])
    send(["land1_s"], ["send1_s"])
    pick("land1", 0, "send1", 128, T.cu[:, 0:1], CAPP, ["cu"], "land1own", ["send1_c"], ["send1_s"])
    table(1)
    cp(T.xr1[:, 0:1], T.tx[:, 0:1], ["tx"], ["xrown1"])
    tt(T.win[:, 0:A], T.xx[:, 0:A], T.xa[:], ALU.subtract, ["xx", "xa"], ["winq"])
    dma("s", "nd1", T.nd[1:2, :], T.win[0:1, 0:A], ["winq"], [])
    inverse(1, lambda: pick("winb", 0, "wina", 160, T.nu0[:, 0:2], A, ["nu0"], "winbq", wina_c, wina_s), lambda: None)
    listed_a()
    listed_b()
    listed_c(1)
    received(1)
    serve(1)
    quant("wq", 0, 128, T.wt[:], ["wt"], ["wq"])
    quant("fin", 0, 128, T.xt[:], ["xt", "xtz"], ["fin_c", "fin_s"])
    home(1)
    cp(T.stw[:], T.win[:, 0:160].indirect(T.nu1[:, 0:2]), row + ["nu1"], ["stw"])
    dma("s", "nd2", T.nd[2:3, :], T.stw[0:1, :], ["stw"], [])
    pick("fin", 0, "winb", 160, T.nu1[:, 0:2], A, ["winbq_c", "winbq_s", "winbown_c", "winbown_s", "in_ret1", "nu1"], "fin")
    mx(7, 128, "wq", 0, "fin", 0, ["wq", "fin_c", "fin_s"])
    cp(T.ys[:], bank(7, A), ["bank7"], ["ys"])
    dma("s", "oc", T.oc[:], codes("fin", 0, A), ["fin_c"], [])
    for k in range(4):
        dma("s" if k % 2 else "a", "osc", T.osc[4 * k:4 * k + 4, :], T.fins[32 * k:32 * k + 4, 0:A], ["fin_s"], [])
    dma("a", "y", T.y[:], T.ys[:], ["ys"], [])
    g.wait_ge(T.sem.left, left[0])
    for q, s in sems.items():
        g.wait_ge(T.sem[s], count[q])
    for s, v in dcount.items():
        g.wait_ge(T.sem[s], v)
